import numpy as np
import ml_dtypes


def mxq(x, axis, fmt="e4m3"):
    dtype, down = {"e4m3": (ml_dtypes.float8_e4m3fn, 7), "e5m2": (ml_dtypes.float8_e5m2, 14)}[fmt]
    v = np.moveaxis(np.asarray(x, np.float32).astype(ml_dtypes.bfloat16).astype(np.float64), axis, -1)
    blocks = v.reshape(v.shape[:-1] + (-1, 32))
    amax = np.abs(blocks).max(-1, keepdims=True)
    byte = np.maximum(np.where(amax > 0, np.frexp(amax)[1] - 1 + 127, 0) - down, 1)
    scale = np.exp2(byte - 127.0)
    codes = (blocks / scale).astype(np.float32).astype(dtype).astype(np.float64)
    return np.moveaxis((codes * scale).reshape(v.shape), -1, axis)


WIDE = False


def mx_kscale(k):
    if not WIDE:
        return np.ones(k)
    levels = np.array([10, -10, 5, -5, 0])
    if k % 512:
        return np.exp2(np.random.permutation(np.resize(levels, k // 32))).repeat(32)
    a = np.empty((k // 512, 16))
    for p in range(k // 512):
        a[p, :8] = np.random.permutation(np.resize(levels, 8))
        for g in range(8):
            far = levels[np.abs(levels - a[p, g]) >= 10]
            a[p, g + 8] = far[np.random.randint(len(far))]
    return np.exp2(a.ravel()).repeat(32)


def f64(x):
    return np.asarray(x).astype(np.float64)


def striped(idx):
    return np.tile(idx.reshape(-1, 16).T, (8, 1)).astype(np.uint16)


def unstriped(offs):
    return offs[:16].T.reshape(-1).astype(np.int64)


E2M1 = np.array([0.0, 0.5, 1.0, 1.5, 2.0, 3.0, 4.0, 6.0, -0.0, -0.5, -1.0, -1.5, -2.0, -3.0, -4.0, -6.0])


def pack_weight(w, fmt):
    k, n = w.shape
    w = f64(np.asarray(w, np.float32).astype(ml_dtypes.bfloat16)).reshape(k // 32, 32, n)
    amax = np.abs(w).max(1)
    if fmt == "e4m3":
        byte = np.frexp(amax)[1] - 1 + 127 - 7
    else:
        mant, ex = np.frexp(amax / 6.0)
        byte = np.where(mant > 0.5, ex, ex - 1) + 127
    byte = np.clip(np.where(amax > 0, byte, 1), 1, 254)
    scaled = (w * np.exp2(127.0 - byte)[:, None, :]).reshape(k, n).astype(np.float32)
    by_word = np.ascontiguousarray(scaled.reshape(k // 512, 128, 4, n).transpose(0, 1, 3, 2))
    if fmt == "e4m3":
        words = by_word.astype(ml_dtypes.float8_e4m3fn).view(np.uint8)
    else:
        c = by_word.astype(ml_dtypes.float4_e2m1fn).view(np.uint8) & 0xF
        words = (c[..., 0::2] | (c[..., 1::2] << 4)).reshape(k // 512, 128, 2 * n)
    return np.ascontiguousarray(words), np.ascontiguousarray(byte.astype(np.uint8).reshape(k // 512, 16, n))


def unpack_weight(words, scales, fmt):
    g, _, n = scales.shape
    words = np.ascontiguousarray(words).reshape(g, 128, n, -1)
    if fmt == "e4m3":
        vals = words.view(ml_dtypes.float8_e4m3fn).astype(np.float64)
    else:
        nib = np.empty((g, 128, n, 4), np.uint8)
        nib[..., 0::2] = words & 0xF
        nib[..., 1::2] = words >> 4
        vals = E2M1[nib]
    vals = vals * np.repeat(np.exp2(scales.astype(np.float64) - 127.0), 8, axis=1)[..., None]
    return vals.transpose(0, 1, 3, 2).reshape(g * 512, n)


def gelu(v):
    return 0.5 * v * (1.0 + np.tanh(np.sqrt(2.0 / np.pi) * (v + 0.044715 * v**3)))


K, H, N, T, S, P, P2 = 1024, 1024, 512, 2048, 1024, 512, 256

def setup_inputs():
    n = np.random.standard_normal
    s = mx_kscale(K)[:, None]
    u = mx_kscale(H)[:, None]
    tab_words, tab_scales = pack_weight(n((K, T)) * s, "e4m3")
    w4_words, w4_scales = pack_weight(n((K, H)) / np.sqrt(K) / s, "e2m1")
    return {
        "tab_words": tab_words, "tab_scales": tab_scales,
        "offs": striped(np.random.permutation(T)[:S]),
        "w4_words": w4_words, "w4_scales": w4_scales,
        "pos1": striped(np.random.permutation(S)[:P]),
        "pos2": striped(np.random.permutation(S)[:P]),
        "gain": (np.exp(0.3 * n(H)) * u[:, 0]).astype(np.float32),
        "w2": (2.0 * n((H, N)) / np.sqrt(H) / u).astype(np.float32),
        "pos3": striped(np.random.permutation(P)[:P2]),
        "pos4": striped(np.random.permutation(P)[:P2]),
        "bias": (0.5 * n(N)).astype(np.float32),
    }

def reference(tab_words, tab_scales, offs, w4_words, w4_scales, pos1, pos2,
              gain, w2, pos3, pos4, bias):
    v = unpack_weight(tab_words, tab_scales, "e4m3")[:, unstriped(offs)]
    w4 = unpack_weight(w4_words, w4_scales, "e2m1")
    h = w4.T @ v
    mastery = 1.0 / (1.0 + np.exp(-h[:, unstriped(pos1)]))
    z = mastery * h[:, unstriped(pos2)] * f64(gain)[:, None]
    y = mxq(f64(w2), 0, "e4m3").T @ mxq(z, 0, "e4m3")
    unit = y[:, unstriped(pos3)] + y[:, unstriped(pos4)] + f64(bias)[:, None]
    return unit / (1.0 + np.exp(-unit))

@@ -1,0 +1,260 @@
+from contextlib import ExitStack
+
+import concourse.mybir as mybir
+
+K, H, N, T, S, PC, PU = 1024, 1024, 512, 2048, 1024, 512, 256
+FLOPS = 2 * K * H * S + 2 * H * N * PC
+
+F32 = mybir.dt.float32
+BF16 = mybir.dt.bfloat16
+I32 = mybir.dt.int32
+U32 = mybir.dt.uint32
+U16 = mybir.dt.uint16
+U8 = mybir.dt.uint8
+FP8X4 = mybir.dt.float8_e4m3fn_x4
+FP4X4 = mybir.dt.float4_e2m1fn_x4
+ACT = mybir.ActivationFunctionType
+ALU = mybir.AluOpType
+
+P = 128
+BANK = 512
+LAST_CHUNKS = ((0, 256), (256, 256))
+
+
+def tile_list_prerequisite_mastery_kernel(
+    tc, tab_words, tab_scales, offs, w4_words, w4_scales, pos1, pos2, gain, w2, pos3, pos4, bias, out
+):
+    nc = tc.nc
+    with ExitStack() as ctx:
+        lists = ctx.enter_context(tc.tile_pool(name="lists", bufs=1))
+        keep = ctx.enter_context(tc.tile_pool(name="keep", bufs=1))
+        shared = ctx.enter_context(tc.tile_pool(name="shared", bufs=1))
+        ring = ctx.enter_context(tc.tile_pool(name="ring", bufs=3))
+        psum = ctx.enter_context(tc.psum_pool(name="psum", bufs=8))
+
+        def load_list(name, dram):
+            tile = lists.tile([P, dram.shape[1]], U16, name=name)
+            nc.sync.dma_start(tile[:], dram)
+            return tile
+
+        def kept(name, shape, dtype):
+            return keep.tile(shape, dtype, name=name, align_bytes=64)
+
+        offs_sb = load_list("offs_sb", offs)
+        pos1_sb = load_list("pos1_sb", pos1)
+        pos2_sb = load_list("pos2_sb", pos2)
+        pos3_sb = load_list("pos3_sb", pos3)
+        pos4_sb = load_list("pos4_sb", pos4)
+
+        w4s_raw = kept("w4s_raw", [P, 2, H], U8)
+        nc.vector.memset(w4s_raw[:].bitcast(I32), 0)
+        for quad in range(4):
+            nc.gpsimd.dma_start(
+                w4s_raw[32 * quad : 32 * quad + 4, :, :].bitcast(I32),
+                w4_scales[:, 4 * quad : 4 * quad + 4, :].rearrange("a r c -> r a c").bitcast(I32),
+            )
+        scale_window = kept("scale_window", [P, T], U8)
+        nc.vector.memset(scale_window[64:128, :].bitcast(I32), 0)
+        nc.vector.memset(scale_window[32:64, :].bitcast(I32), 0)
+        nc.scalar.dma_start(
+            scale_window[0:32, :].bitcast(I32), tab_scales.rearrange("a q t -> (a q) t").bitcast(I32)
+        )
+        v_planes = kept("v_planes", [P, 2, S], U8)
+        nc.vector.memset(v_planes[:].bitcast(I32), 0)
+
+        def load_table(a, words):
+            nc.scalar.dma_start(words[:].bitcast(I32), tab_words[a].rearrange("p t i -> p (t i)").bitcast(I32))
+            return words
+
+        def load_w4(b, raw, queue):
+            queue.dma_start(
+                raw[:].bitcast(I32),
+                w4_words[:, :, 1024 * b : 1024 * b + 1024].rearrange("a p c -> p a c").bitcast(I32),
+            )
+            return raw
+
+        table = [load_table(0, shared.tile([P, T], U32, name="table0", offset=6144))]
+        w4_raw = [load_w4(0, kept("w4_raw0", [P, 2, H], U8), nc.scalar)]
+        table.append(load_table(1, kept("table1", [P, T], U32)))
+
+        v_rows = kept("v_rows", [P, S], U8)
+        nc.vector.tensor_copy(v_rows[:], scale_window[:].indirect(offs_sb[:]))
+        for a in range(2):
+            for quad in range(4):
+                first_row = 16 * a + 4 * quad
+                nc.sync.dma_start(
+                    v_planes[32 * quad : 32 * quad + 4, a, :].bitcast(I32),
+                    v_rows[first_row : first_row + 4, :].bitcast(I32),
+                )
+
+        v_words = {}
+
+        def gather_words(a, half):
+            picked = kept("v_words%d%d" % (a, half), [P, BANK], U32)
+            nc.vector.tensor_copy(picked[:], table[a][:].indirect(offs_sb[:, 32 * half : 32 * half + 32]))
+            v_words[a, half] = picked
+
+        w4_codes = {}
+        w4_planes = {}
+
+        def order_w4(b):
+            codes = kept("w4_codes%d" % b, [P, 2, 4, 2 * P], U8)
+            nc.vector.tensor_copy(
+                codes[:].bitcast(I32).rearrange("p a t (q w) -> p a t q w", w=2),
+                w4_raw[b][:].bitcast(I32).rearrange("p a (q t w) -> p a t q w", t=4, w=2),
+            )
+            planes = kept("w4_planes%d" % b, [P, 2, 4, P], U8)
+            nc.vector.tensor_copy(
+                planes[:].bitcast(I32),
+                w4s_raw[:, :, 512 * b : 512 * b + 512].bitcast(I32).rearrange("p a (q t) -> p a t q", t=4),
+            )
+            w4_codes[b] = codes
+            w4_planes[b] = planes
+
+        gather_words(0, 0)
+        gather_words(0, 1)
+
+        w4_raw.append(load_w4(1, shared.tile([P, 2, H], U8, name="w4_raw1", offset=8192), nc.sync))
+        gain_sb = shared.tile([P, 2, 16], F32, name="gain_sb", offset=10240)
+        gain_view = gain.rearrange("(b q c) -> q b c", b=2, c=16)
+        for e in range(4):
+            nc.sync.dma_start(gain_sb[e:P:4, :, 0:13], gain_view[:, :, e : e + 13])
+        w2_raw = []
+        w2_view = w2.rearrange("(b q t e) n -> b e q t n", b=2, t=4, e=4)
+        for b in range(2):
+            raw = shared.tile([P, 4, N], F32, name="w2_raw%d" % b, offset=12288 * b)
+            for e in range(4):
+                nc.sync.dma_start(raw[e:P:4, :, :], w2_view[b][e])
+            w2_raw.append(raw)
+        bias_sb = shared.tile([P, 4], F32, name="bias_sb", offset=10368)
+        with nc.allow_non_contiguous_dma(reason="one value a partition"):
+            nc.sync.dma_start(bias_sb[:], bias.rearrange("(j p) -> p j", p=P))
+
+        gather_words(1, 0)
+        order_w4(0)
+        gather_words(1, 1)
+        zero = kept("zero", [P, 1], F32)
+        nc.gpsimd.memset(zero[:], 0.0)
+        warm = kept("warm", [P, 1], F32)
+        nc.scalar.activation(warm[:], zero[:], ACT.Sigmoid)
+
+        h = {}
+
+        def first_product(j):
+            b, t = divmod(j, 4)
+            rows = kept("h%d" % j, [P, S], F32)
+            for half in range(2):
+                cols = slice(BANK * half, BANK * half + BANK)
+                acc = psum.tile([P, BANK], F32, name="acc")
+                for a in range(2):
+                    nc.tensor.matmul_mx(
+                        out=acc[:],
+                        lhsT=w4_codes[b][:, a, t, :].bitcast(FP4X4),
+                        lhsT_scale=w4_planes[b][:, a, t, :],
+                        rhs=v_words[a, half][:].bitcast(FP8X4),
+                        rhs_scale=v_planes[:, a, cols],
+                        start=(a == 0),
+                        stop=(a == 1),
+                    )
+                nc.scalar.copy(rows[:, cols], acc[:])
+            h[j] = rows
+
+        def weave(engine_copy, woven, rows):
+            engine_copy(
+                woven.rearrange("p (c i) t -> p c t i", i=4),
+                rows.rearrange("p t (c i) -> p c t i", i=4),
+            )
+
+        def quantise(name, woven, width):
+            codes = kept(name + "_codes", [P, width], U32)
+            plane = kept(name + "_plane", [P, width], U8)
+            nc.vector.quantize_mx(
+                out=codes[:].bitcast(FP8X4), scales=plane[:], in_=woven[:].rearrange("p m t -> p (m t)")
+            )
+            return codes, plane
+
+        w2_q = {}
+
+        def prepare_w2(b):
+            woven = kept("w2_woven%d" % b, [P, N, 4], BF16)
+            weave(nc.scalar.copy, woven[:], w2_raw[b][:])
+            w2_q[b] = quantise("w2_%d" % b, woven, N)
+
+        def pick_couples(j, m0, width):
+            cols = slice(m0 // 16, (m0 + width) // 16)
+            left = ring.tile([P, width], F32, name="left")
+            nc.vector.tensor_copy(left[:], h[j][:].indirect(pos1_sb[:, cols]))
+            right = ring.tile([P, width], F32, name="right")
+            nc.vector.tensor_copy(right[:], h[j][:].indirect(pos2_sb[:, cols]))
+            mastery = ring.tile([P, width], F32, name="mastery")
+            nc.scalar.activation(mastery[:], left[:], ACT.Sigmoid)
+            return right, mastery
+
+        def combine(j, z_rows, right, mastery):
+            b, t = divmod(j, 4)
+            nc.vector.scalar_tensor_tensor(
+                z_rows[:, t, :], right[:], gain_sb[:, b, 4 * t : 4 * t + 1], mastery[:], ALU.mult, ALU.mult
+            )
+
+        groups = [(0, 0, PC)] + [(1, m0, width) for m0, width in LAST_CHUNKS]
+        steps = [(g, t) for g in range(len(groups)) for t in range(4)]
+        z_rows = [kept("z_rows%d" % g, [P, 4, width], BF16) for g, (b, m0, width) in enumerate(groups)]
+        z_q = {}
+        y = [kept("y%d" % j, [P, PC], F32) for j in range(4)]
+
+        def finish_group(g):
+            b, m0, width = groups[g]
+            woven = kept("z_woven%d" % g, [P, width, 4], BF16)
+            last = g == len(groups) - 1
+            weave(nc.vector.tensor_copy if last else nc.scalar.copy, woven[:], z_rows[g][:])
+            z_q[g] = quantise("z%d" % g, woven, width)
+            if b == 0:
+                return
+            cols = slice(m0, m0 + width)
+            for j in range(4):
+                acc = psum.tile([P, BANK], F32, name="acc")
+                n_cols = slice(P * j, P * j + P)
+                for bb in range(2):
+                    codes, plane = z_q[0] if bb == 0 else z_q[g]
+                    z_cols = cols if bb == 0 else slice(0, width)
+                    nc.tensor.matmul_mx(
+                        out=acc[:, 0:width],
+                        lhsT=w2_q[bb][0][:, n_cols].bitcast(FP8X4),
+                        lhsT_scale=w2_q[bb][1][:, n_cols],
+                        rhs=codes[:, z_cols].bitcast(FP8X4),
+                        rhs_scale=plane[:, z_cols],
+                        start=(bb == 0),
+                        stop=(bb == 1),
+                    )
+                nc.scalar.copy(y[j][:, cols], acc[:, 0:width])
+
+        first_product(0)
+        pending = None
+        for i, (g, t) in enumerate(steps):
+            b, m0, width = groups[g]
+            j = 4 * b + t
+            if i + 1 < 8:
+                first_product(i + 1)
+            picked = pick_couples(j, m0, width)
+            if pending is not None:
+                combine(*pending)
+                if t == 0:
+                    finish_group(g - 1)
+            pending = (j, z_rows[g]) + picked
+            if i == 0:
+                order_w4(1)
+            if i == 1:
+                prepare_w2(0)
+            if i == 5:
+                prepare_w2(1)
+        combine(*pending)
+        finish_group(len(groups) - 1)
+
+        for j in range(4):
+            first = ring.tile([P, PU], F32, name="first")
+            nc.vector.tensor_copy(first[:], y[j][:].indirect(pos3_sb[:]))
+            both = ring.tile([P, PU], F32, name="both")
+            nc.vector.tensor_tensor(both[:], y[j][:].indirect(pos4_sb[:]), first[:], ALU.add)
+            result = ring.tile([P, PU], F32, name="result")
+            nc.scalar.activation(result[:], both[:], ACT.Silu, bias=bias_sb[:, j : j + 1])
+            nc.sync.dma_start(out[P * j : P * j + P, :], result[:])

@@ -29,7 +29,7 @@ def tile_list_prerequisite_mastery_kernel(
         lists = ctx.enter_context(tc.tile_pool(name="lists", bufs=1))
         keep = ctx.enter_context(tc.tile_pool(name="keep", bufs=1))
         shared = ctx.enter_context(tc.tile_pool(name="shared", bufs=1))
-        ring = ctx.enter_context(tc.tile_pool(name="ring", bufs=3))
+        ring = ctx.enter_context(tc.tile_pool(name="ring", bufs=4))
         psum = ctx.enter_context(tc.psum_pool(name="psum", bufs=8))
 
         def load_list(name, dram):
@@ -41,6 +41,10 @@ def tile_list_prerequisite_mastery_kernel(
             return keep.tile(shape, dtype, name=name, align_bytes=64)
 
         offs_sb = load_list("offs_sb", offs)
+        scale_window = kept("scale_window", [P, T], U8)
+        nc.sync.dma_start(
+            scale_window[0:32, :].bitcast(I32), tab_scales.rearrange("a q t -> (a q) t").bitcast(I32)
+        )
         pos1_sb = load_list("pos1_sb", pos1)
         pos2_sb = load_list("pos2_sb", pos2)
         pos3_sb = load_list("pos3_sb", pos3)
@@ -53,17 +57,13 @@ def tile_list_prerequisite_mastery_kernel(
                 w4s_raw[32 * quad : 32 * quad + 4, :, :].bitcast(I32),
                 w4_scales[:, 4 * quad : 4 * quad + 4, :].rearrange("a r c -> r a c").bitcast(I32),
             )
-        scale_window = kept("scale_window", [P, T], U8)
         nc.vector.memset(scale_window[64:128, :].bitcast(I32), 0)
         nc.vector.memset(scale_window[32:64, :].bitcast(I32), 0)
-        nc.scalar.dma_start(
-            scale_window[0:32, :].bitcast(I32), tab_scales.rearrange("a q t -> (a q) t").bitcast(I32)
-        )
         v_planes = kept("v_planes", [P, 2, S], U8)
         nc.vector.memset(v_planes[:].bitcast(I32), 0)
 
         def load_table(a, words):
-            nc.scalar.dma_start(words[:].bitcast(I32), tab_words[a].rearrange("p t i -> p (t i)").bitcast(I32))
+            nc.sync.dma_start(words[:].bitcast(I32), tab_words[a].rearrange("p t i -> p (t i)").bitcast(I32))
             return words
 
         def load_w4(b, raw, queue):
@@ -73,16 +73,17 @@ def tile_list_prerequisite_mastery_kernel(
             )
             return raw
 
-        table = [load_table(0, shared.tile([P, T], U32, name="table0", offset=6144))]
-        w4_raw = [load_w4(0, kept("w4_raw0", [P, 2, H], U8), nc.scalar)]
-        table.append(load_table(1, kept("table1", [P, T], U32)))
+        table = [load_table(0, shared.tile([P, T], U32, name="table0", offset=7936))]
+        w4_raw = [load_w4(0, kept("w4_raw0", [P, 2, H], U8), nc.sync)]
+        table.append(load_table(1, shared.tile([P, T], U32, name="table1", offset=24064)))
 
         v_rows = kept("v_rows", [P, S], U8)
         nc.vector.tensor_copy(v_rows[:], scale_window[:].indirect(offs_sb[:]))
         for a in range(2):
             for quad in range(4):
                 first_row = 16 * a + 4 * quad
-                nc.sync.dma_start(
+                queue = nc.gpsimd if (a, quad) == (1, 3) else nc.scalar
+                queue.dma_start(
                     v_planes[32 * quad : 32 * quad + 4, a, :].bitcast(I32),
                     v_rows[first_row : first_row + 4, :].bitcast(I32),
                 )
@@ -98,12 +99,16 @@ def tile_list_prerequisite_mastery_kernel(
         w4_planes = {}
 
         def order_w4(b):
-            codes = kept("w4_codes%d" % b, [P, 2, 4, 2 * P], U8)
+            if b == 0:
+                codes = shared.tile([P, 2, 4, 2 * P], U8, name="w4_codes0", offset=10240, align_bytes=64)
+                planes = shared.tile([P, 2, 4, P], U8, name="w4_planes0", offset=12288, align_bytes=64)
+            else:
+                codes = shared.tile([P, 2, 4, 2 * P], U8, name="w4_codes1", offset=24064, align_bytes=64)
+                planes = shared.tile([P, 2, 4, P], U8, name="w4_planes1", offset=26112, align_bytes=64)
             nc.vector.tensor_copy(
                 codes[:].bitcast(I32).rearrange("p a t (q w) -> p a t q w", w=2),
                 w4_raw[b][:].bitcast(I32).rearrange("p a (q t w) -> p a t q w", t=4, w=2),
             )
-            planes = kept("w4_planes%d" % b, [P, 2, 4, P], U8)
             nc.vector.tensor_copy(
                 planes[:].bitcast(I32),
                 w4s_raw[:, :, 512 * b : 512 * b + 512].bitcast(I32).rearrange("p a (q t) -> p a t q", t=4),
@@ -115,23 +120,23 @@ def tile_list_prerequisite_mastery_kernel(
         gather_words(0, 1)
 
         w4_raw.append(load_w4(1, shared.tile([P, 2, H], U8, name="w4_raw1", offset=8192), nc.sync))
-        gain_sb = shared.tile([P, 2, 16], F32, name="gain_sb", offset=10240)
+        gain_sb = shared.tile([P, 2, 16], F32, name="gain_sb", offset=13312)
         gain_view = gain.rearrange("(b q c) -> q b c", b=2, c=16)
         for e in range(4):
             nc.sync.dma_start(gain_sb[e:P:4, :, 0:13], gain_view[:, :, e : e + 13])
         w2_raw = []
         w2_view = w2.rearrange("(b q t e) n -> b e q t n", b=2, t=4, e=4)
         for b in range(2):
-            raw = shared.tile([P, 4, N], F32, name="w2_raw%d" % b, offset=12288 * b)
+            raw = shared.tile([P, 4, N], F32, name="w2_raw%d" % b, offset=15872 * b)
             for e in range(4):
                 nc.sync.dma_start(raw[e:P:4, :, :], w2_view[b][e])
             w2_raw.append(raw)
-        bias_sb = shared.tile([P, 4], F32, name="bias_sb", offset=10368)
+        bias_sb = shared.tile([P, 4], F32, name="bias_sb", offset=13440)
         with nc.allow_non_contiguous_dma(reason="one value a partition"):
             nc.sync.dma_start(bias_sb[:], bias.rearrange("(j p) -> p j", p=P))
 
-        gather_words(1, 0)
         order_w4(0)
+        gather_words(1, 0)
         gather_words(1, 1)
         zero = kept("zero", [P, 1], F32)
         nc.gpsimd.memset(zero[:], 0.0)
@@ -146,15 +151,16 @@ def tile_list_prerequisite_mastery_kernel(
             for half in range(2):
                 cols = slice(BANK * half, BANK * half + BANK)
                 acc = psum.tile([P, BANK], F32, name="acc")
-                for a in range(2):
+                order = (0, 1) if j == 0 else (1, 0)
+                for a in order:
                     nc.tensor.matmul_mx(
                         out=acc[:],
                         lhsT=w4_codes[b][:, a, t, :].bitcast(FP4X4),
                         lhsT_scale=w4_planes[b][:, a, t, :],
                         rhs=v_words[a, half][:].bitcast(FP8X4),
                         rhs_scale=v_planes[:, a, cols],
-                        start=(a == 0),
-                        stop=(a == 1),
+                        start=(a == order[0]),
+                        stop=(a == order[1]),
                     )
                 nc.scalar.copy(rows[:, cols], acc[:])
             h[j] = rows
@@ -175,26 +181,31 @@ def tile_list_prerequisite_mastery_kernel(
 
         w2_q = {}
 
-        def prepare_w2(b):
-            woven = kept("w2_woven%d" % b, [P, N, 4], BF16)
-            weave(nc.scalar.copy, woven[:], w2_raw[b][:])
-            w2_q[b] = quantise("w2_%d" % b, woven, N)
+        def prepare_w2(i):
+            b, j = divmod(i, 4)
+            woven = keep.tile([P, P, 4], BF16, name="w2_woven%d" % i, tag="mastery%d" % i, align_bytes=64)
+            weave(nc.scalar.copy, woven[:], w2_raw[b][:, :, P * j : P * j + P])
+            w2_q[b, j] = quantise("w2_%d" % i, woven, P)
 
-        def pick_couples(j, m0, width):
+        def pick_couples(i, j, m0, width):
             cols = slice(m0 // 16, (m0 + width) // 16)
             left = ring.tile([P, width], F32, name="left")
             nc.vector.tensor_copy(left[:], h[j][:].indirect(pos1_sb[:, cols]))
             right = ring.tile([P, width], F32, name="right")
             nc.vector.tensor_copy(right[:], h[j][:].indirect(pos2_sb[:, cols]))
-            mastery = ring.tile([P, width], F32, name="mastery")
+            mastery = kept("mastery%d" % i, [P, width], F32)
             nc.scalar.activation(mastery[:], left[:], ACT.Sigmoid)
             return right, mastery
 
-        def combine(j, z_rows, right, mastery):
+        def combine(on_vector, j, z_rows, right, mastery):
             b, t = divmod(j, 4)
-            nc.vector.scalar_tensor_tensor(
-                z_rows[:, t, :], right[:], gain_sb[:, b, 4 * t : 4 * t + 1], mastery[:], ALU.mult, ALU.mult
-            )
+            factor = gain_sb[:, b, 4 * t : 4 * t + 1]
+            if on_vector:
+                nc.vector.scalar_tensor_tensor(z_rows[:, t, :], right[:], factor, mastery[:], ALU.mult, ALU.mult)
+            else:
+                scaled = ring.tile([P, right.shape[1]], F32, name="scaled")
+                nc.gpsimd.tensor_scalar(scaled[:], right[:], factor, 0.0, ALU.mult, ALU.add)
+                nc.gpsimd.tensor_tensor(z_rows[:, t, :], scaled[:], mastery[:], ALU.mult)
 
         groups = [(0, 0, PC)] + [(1, m0, width) for m0, width in LAST_CHUNKS]
         steps = [(g, t) for g in range(len(groups)) for t in range(4)]
@@ -213,14 +224,13 @@ def tile_list_prerequisite_mastery_kernel(
             cols = slice(m0, m0 + width)
             for j in range(4):
                 acc = psum.tile([P, BANK], F32, name="acc")
-                n_cols = slice(P * j, P * j + P)
                 for bb in range(2):
                     codes, plane = z_q[0] if bb == 0 else z_q[g]
                     z_cols = cols if bb == 0 else slice(0, width)
                     nc.tensor.matmul_mx(
                         out=acc[:, 0:width],
-                        lhsT=w2_q[bb][0][:, n_cols].bitcast(FP8X4),
-                        lhsT_scale=w2_q[bb][1][:, n_cols],
+                        lhsT=w2_q[bb, j][0][:].bitcast(FP8X4),
+                        lhsT_scale=w2_q[bb, j][1][:],
                         rhs=codes[:, z_cols].bitcast(FP8X4),
                         rhs_scale=plane[:, z_cols],
                         start=(bb == 0),
@@ -229,24 +239,23 @@ def tile_list_prerequisite_mastery_kernel(
                 nc.scalar.copy(y[j][:, cols], acc[:, 0:width])
 
         first_product(0)
+        first_product(1)
         pending = None
         for i, (g, t) in enumerate(steps):
             b, m0, width = groups[g]
             j = 4 * b + t
-            if i + 1 < 8:
-                first_product(i + 1)
-            picked = pick_couples(j, m0, width)
+            if i == 1:
+                order_w4(1)
+            picked = pick_couples(i, j, m0, width)
+            if i + 2 < 8:
+                first_product(i + 2)
             if pending is not None:
                 combine(*pending)
+                if i - 1 < 8:
+                    prepare_w2(i - 1)
                 if t == 0:
                     finish_group(g - 1)
-            pending = (j, z_rows[g]) + picked
-            if i == 0:
-                order_w4(1)
-            if i == 1:
-                prepare_w2(0)
-            if i == 5:
-                prepare_w2(1)
+            pending = (i == len(steps) - 1, j, z_rows[g]) + picked
         combine(*pending)
         finish_group(len(groups) - 1)
 

@@ -2,8 +2,10 @@ from contextlib import ExitStack
 
 import concourse.mybir as mybir
 
-K, H, N, T, S, PC, PU = 1024, 1024, 512, 2048, 1024, 512, 256
-FLOPS = 2 * K * H * S + 2 * H * N * PC
+K, H, N = 1024, 1024, 512
+T, S = 2048, 1024
+COUPLES, UNITS = 512, 256
+FLOPS = 2 * K * H * S + 2 * H * N * COUPLES
 
 F32 = mybir.dt.float32
 BF16 = mybir.dt.bfloat16
@@ -18,7 +20,24 @@ ALU = mybir.AluOpType
 
 P = 128
 BANK = 512
-LAST_CHUNKS = ((0, 256), (256, 256))
+PER_COLUMN = 16
+ROW_TILES = H // P
+OUT_TILES = N // P
+
+GROUPS = ((0, 0, COUPLES), (1, 0, COUPLES // 2), (1, COUPLES // 2, COUPLES // 2))
+LAST_ON_SCALAR = 64
+PASS0_FIRST = 2
+MASTERY_BUFS = 3
+W2_STEP = 3
+
+TABLE_AT = (7936, 24064)
+W4_CODES_AT = (8192, 24576)
+W4_PLANES_AT = 10240
+W2_ROWS_AT = (16320, 26624)
+BIAS_AT = 24512
+SCALE_WINDOW_AT = 32256
+PICKED_PASS1_AT = (35328, 37376)
+W4_SCALE_ROWS_AT = 36352
 
 
 def tile_list_prerequisite_mastery_kernel(
@@ -29,7 +48,7 @@ def tile_list_prerequisite_mastery_kernel(
         lists = ctx.enter_context(tc.tile_pool(name="lists", bufs=1))
         keep = ctx.enter_context(tc.tile_pool(name="keep", bufs=1))
         shared = ctx.enter_context(tc.tile_pool(name="shared", bufs=1))
-        ring = ctx.enter_context(tc.tile_pool(name="ring", bufs=4))
+        ring = ctx.enter_context(tc.tile_pool(name="ring", bufs=OUT_TILES))
         psum = ctx.enter_context(tc.psum_pool(name="psum", bufs=8))
 
         def load_list(name, dram):
@@ -40,8 +59,13 @@ def tile_list_prerequisite_mastery_kernel(
         def kept(name, shape, dtype):
             return keep.tile(shape, dtype, name=name, align_bytes=64)
 
+        warm_input = kept("warm_input", [P, 1], F32)
+        nc.vector.memset(warm_input[:], 0.0)
+        warm = kept("warm", [P, 1], F32)
+        nc.scalar.activation(warm[:], warm_input[:], ACT.Sigmoid)
+
         offs_sb = load_list("offs_sb", offs)
-        scale_window = kept("scale_window", [P, T], U8)
+        scale_window = shared.tile([P, T], U8, name="scale_window", offset=SCALE_WINDOW_AT, align_bytes=64)
         nc.sync.dma_start(
             scale_window[0:32, :].bitcast(I32), tab_scales.rearrange("a q t -> (a q) t").bitcast(I32)
         )
@@ -50,98 +74,90 @@ def tile_list_prerequisite_mastery_kernel(
         pos3_sb = load_list("pos3_sb", pos3)
         pos4_sb = load_list("pos4_sb", pos4)
 
-        w4s_raw = kept("w4s_raw", [P, 2, H], U8)
-        nc.vector.memset(w4s_raw[:].bitcast(I32), 0)
-        for quad in range(4):
-            nc.gpsimd.dma_start(
-                w4s_raw[32 * quad : 32 * quad + 4, :, :].bitcast(I32),
-                w4_scales[:, 4 * quad : 4 * quad + 4, :].rearrange("a r c -> r a c").bitcast(I32),
-            )
+        w4_scale_rows = shared.tile([P, 2, H], U8, name="w4_scale_rows", offset=W4_SCALE_ROWS_AT, align_bytes=64)
+        nc.vector.memset(w4_scale_rows[:].bitcast(I32), 0)
         nc.vector.memset(scale_window[64:128, :].bitcast(I32), 0)
         nc.vector.memset(scale_window[32:64, :].bitcast(I32), 0)
         v_planes = kept("v_planes", [P, 2, S], U8)
         nc.vector.memset(v_planes[:].bitcast(I32), 0)
 
-        def load_table(a, words):
+        def load_table(a):
+            words = shared.tile([P, T], U32, name="table%d" % a, offset=TABLE_AT[a])
             nc.sync.dma_start(words[:].bitcast(I32), tab_words[a].rearrange("p t i -> p (t i)").bitcast(I32))
             return words
 
-        def load_w4(b, raw, queue):
-            queue.dma_start(
-                raw[:].bitcast(I32),
-                w4_words[:, :, 1024 * b : 1024 * b + 1024].rearrange("a p c -> p a c").bitcast(I32),
+        table = [load_table(0)]
+        w4_raw = kept("w4_raw", [P, 2, 2 * H], U8)
+        nc.sync.dma_start(w4_raw[:].bitcast(I32), w4_words.rearrange("a p c -> p a c").bitcast(I32))
+        for quad in range(4):
+            nc.sync.dma_start(
+                w4_scale_rows[32 * quad : 32 * quad + 4, :, :].bitcast(I32),
+                w4_scales[:, 4 * quad : 4 * quad + 4, :].rearrange("a s c -> s a c").bitcast(I32),
             )
-            return raw
+        table.append(load_table(1))
 
-        table = [load_table(0, shared.tile([P, T], U32, name="table0", offset=7936))]
-        w4_raw = [load_w4(0, kept("w4_raw0", [P, 2, H], U8), nc.sync)]
-        table.append(load_table(1, shared.tile([P, T], U32, name="table1", offset=24064)))
-
-        v_rows = kept("v_rows", [P, S], U8)
-        nc.vector.tensor_copy(v_rows[:], scale_window[:].indirect(offs_sb[:]))
+        picked_scale_rows = kept("picked_scale_rows", [P, S], U8)
+        nc.vector.tensor_copy(picked_scale_rows[:], scale_window[:].indirect(offs_sb[:]))
         for a in range(2):
             for quad in range(4):
                 first_row = 16 * a + 4 * quad
-                queue = nc.gpsimd if (a, quad) == (1, 3) else nc.scalar
+                queue = nc.gpsimd if (a, quad) == (0, 3) else nc.scalar
                 queue.dma_start(
                     v_planes[32 * quad : 32 * quad + 4, a, :].bitcast(I32),
-                    v_rows[first_row : first_row + 4, :].bitcast(I32),
+                    picked_scale_rows[first_row : first_row + 4, :].bitcast(I32),
                 )
+
+        gain_sb = kept("gain_sb", [P, 2, 16], F32)
+        gain_view = gain.rearrange("(b q c) -> q b c", b=2, c=16)
+        for e in range(4):
+            nc.gpsimd.dma_start(gain_sb[e:P:4, :, 0:13], gain_view[:, :, e : e + 13])
 
         v_words = {}
 
         def gather_words(a, half):
-            picked = kept("v_words%d%d" % (a, half), [P, BANK], U32)
-            nc.vector.tensor_copy(picked[:], table[a][:].indirect(offs_sb[:, 32 * half : 32 * half + 32]))
+            name = "v_words%d%d" % (a, half)
+            if a == 0:
+                picked = kept(name, [P, BANK], U32)
+            else:
+                picked = shared.tile([P, BANK], U32, name=name, offset=PICKED_PASS1_AT[half], align_bytes=64)
+            entries = offs_sb[:, BANK // PER_COLUMN * half : BANK // PER_COLUMN * (half + 1)]
+            nc.vector.tensor_copy(picked[:], table[a][:].indirect(entries))
             v_words[a, half] = picked
 
         w4_codes = {}
-        w4_planes = {}
 
-        def order_w4(b):
-            if b == 0:
-                codes = shared.tile([P, 2, 4, 2 * P], U8, name="w4_codes0", offset=10240, align_bytes=64)
-                planes = shared.tile([P, 2, 4, P], U8, name="w4_planes0", offset=12288, align_bytes=64)
-            else:
-                codes = shared.tile([P, 2, 4, 2 * P], U8, name="w4_codes1", offset=24064, align_bytes=64)
-                planes = shared.tile([P, 2, 4, P], U8, name="w4_planes1", offset=26112, align_bytes=64)
+        def order_w4_codes(b):
+            codes = shared.tile(
+                [P, 2, 4, 2 * P], U8, name="w4_codes%d" % b, offset=W4_CODES_AT[b], align_bytes=64
+            )
             nc.vector.tensor_copy(
                 codes[:].bitcast(I32).rearrange("p a t (q w) -> p a t q w", w=2),
-                w4_raw[b][:].bitcast(I32).rearrange("p a (q t w) -> p a t q w", t=4, w=2),
-            )
-            nc.vector.tensor_copy(
-                planes[:].bitcast(I32),
-                w4s_raw[:, :, 512 * b : 512 * b + 512].bitcast(I32).rearrange("p a (q t) -> p a t q", t=4),
+                w4_raw[:, :, H * b : H * (b + 1)].bitcast(I32).rearrange("p a (q t w) -> p a t q w", t=4, w=2),
             )
             w4_codes[b] = codes
-            w4_planes[b] = planes
 
         gather_words(0, 0)
         gather_words(0, 1)
-
-        w4_raw.append(load_w4(1, shared.tile([P, 2, H], U8, name="w4_raw1", offset=8192), nc.sync))
-        gain_sb = shared.tile([P, 2, 16], F32, name="gain_sb", offset=13312)
-        gain_view = gain.rearrange("(b q c) -> q b c", b=2, c=16)
-        for e in range(4):
-            nc.sync.dma_start(gain_sb[e:P:4, :, 0:13], gain_view[:, :, e : e + 13])
-        w2_raw = []
-        w2_view = w2.rearrange("(b q t e) n -> b e q t n", b=2, t=4, e=4)
-        for b in range(2):
-            raw = shared.tile([P, 4, N], F32, name="w2_raw%d" % b, offset=15872 * b)
-            for e in range(4):
-                nc.sync.dma_start(raw[e:P:4, :, :], w2_view[b][e])
-            w2_raw.append(raw)
-        bias_sb = shared.tile([P, 4], F32, name="bias_sb", offset=13440)
-        with nc.allow_non_contiguous_dma(reason="one value a partition"):
-            nc.sync.dma_start(bias_sb[:], bias.rearrange("(j p) -> p j", p=P))
-
-        order_w4(0)
+        order_w4_codes(0)
+        w4_planes = shared.tile([P, 4, 4, P], U8, name="w4_planes", offset=W4_PLANES_AT, align_bytes=64)
+        nc.vector.tensor_copy(
+            w4_planes[:].bitcast(I32),
+            w4_scale_rows[:].bitcast(I32).rearrange("p a (b q t) -> p (a b) t q", b=2, t=4),
+        )
         gather_words(1, 0)
         gather_words(1, 1)
-        zero = kept("zero", [P, 1], F32)
-        nc.gpsimd.memset(zero[:], 0.0)
-        warm = kept("warm", [P, 1], F32)
-        nc.scalar.activation(warm[:], zero[:], ACT.Sigmoid)
+        order_w4_codes(1)
+
+        w2_rows = []
+        w2_view = w2.rearrange("(b q t e) n -> b e q t n", b=2, t=4, e=4)
+        for b in range(2):
+            raw = shared.tile([P, 4, N], F32, name="w2_rows%d" % b, offset=W2_ROWS_AT[b])
+            for e in range(4):
+                nc.sync.dma_start(raw[e:P:4, :, :], w2_view[b][e])
+            w2_rows.append(raw)
+        bias_sb = shared.tile([P, OUT_TILES], F32, name="bias_sb", offset=BIAS_AT)
+        with nc.allow_non_contiguous_dma(reason="one value a partition"):
+            nc.sync.dma_start(bias_sb[:], bias.rearrange("(j p) -> p j", p=P))
 
         h = {}
 
@@ -149,14 +165,14 @@ def tile_list_prerequisite_mastery_kernel(
             b, t = divmod(j, 4)
             rows = kept("h%d" % j, [P, S], F32)
             for half in range(2):
-                cols = slice(BANK * half, BANK * half + BANK)
+                cols = slice(BANK * half, BANK * (half + 1))
                 acc = psum.tile([P, BANK], F32, name="acc")
-                order = (0, 1) if j == 0 else (1, 0)
+                order = (0, 1) if j < PASS0_FIRST else (1, 0)
                 for a in order:
                     nc.tensor.matmul_mx(
                         out=acc[:],
                         lhsT=w4_codes[b][:, a, t, :].bitcast(FP4X4),
-                        lhsT_scale=w4_planes[b][:, a, t, :],
+                        lhsT_scale=w4_planes[:, 2 * a + b, t, :],
                         rhs=v_words[a, half][:].bitcast(FP8X4),
                         rhs_scale=v_planes[:, a, cols],
                         start=(a == order[0]),
@@ -179,91 +195,87 @@ def tile_list_prerequisite_mastery_kernel(
             )
             return codes, plane
 
-        w2_q = {}
+        w2_mx = {}
 
-        def prepare_w2(i):
-            b, j = divmod(i, 4)
-            woven = keep.tile([P, P, 4], BF16, name="w2_woven%d" % i, tag="mastery%d" % i, align_bytes=64)
-            weave(nc.scalar.copy, woven[:], w2_raw[b][:, :, P * j : P * j + P])
-            w2_q[b, j] = quantise("w2_%d" % i, woven, P)
+        def quantise_w2(b):
+            woven = keep.tile([P, N, 4], BF16, name="w2_woven%d" % b, tag="h%d" % (W2_STEP - 1 + b), align_bytes=64)
+            weave(nc.vector.tensor_copy, woven[:], w2_rows[b][:])
+            w2_mx[b] = quantise("w2_%d" % b, woven, N)
 
-        def pick_couples(i, j, m0, width):
-            cols = slice(m0 // 16, (m0 + width) // 16)
-            left = ring.tile([P, width], F32, name="left")
-            nc.vector.tensor_copy(left[:], h[j][:].indirect(pos1_sb[:, cols]))
-            right = ring.tile([P, width], F32, name="right")
-            nc.vector.tensor_copy(right[:], h[j][:].indirect(pos2_sb[:, cols]))
-            mastery = kept("mastery%d" % i, [P, width], F32)
-            nc.scalar.activation(mastery[:], left[:], ACT.Sigmoid)
-            return right, mastery
-
-        def combine(on_vector, j, z_rows, right, mastery):
+        def pick_mastery(step, j, entries, width):
             b, t = divmod(j, 4)
             factor = gain_sb[:, b, 4 * t : 4 * t + 1]
-            if on_vector:
-                nc.vector.scalar_tensor_tensor(z_rows[:, t, :], right[:], factor, mastery[:], ALU.mult, ALU.mult)
+            mastery = ring.tile([P, width], F32, name="mastery", bufs=MASTERY_BUFS)
+            nc.vector.tensor_copy(mastery[:], h[j][:].indirect(pos1_sb[:, entries]))
+            nc.scalar.activation(mastery[:], mastery[:], ACT.Sigmoid)
+            if step == 0:
+                nc.vector.tensor_scalar(mastery[:], mastery[:], factor, None, ALU.mult)
             else:
-                scaled = ring.tile([P, right.shape[1]], F32, name="scaled")
-                nc.gpsimd.tensor_scalar(scaled[:], right[:], factor, 0.0, ALU.mult, ALU.add)
-                nc.gpsimd.tensor_tensor(z_rows[:, t, :], scaled[:], mastery[:], ALU.mult)
+                nc.scalar.activation(mastery[:], mastery[:], ACT.Copy, scale=factor)
+            return mastery
 
-        groups = [(0, 0, PC)] + [(1, m0, width) for m0, width in LAST_CHUNKS]
-        steps = [(g, t) for g in range(len(groups)) for t in range(4)]
-        z_rows = [kept("z_rows%d" % g, [P, 4, width], BF16) for g, (b, m0, width) in enumerate(groups)]
-        z_q = {}
-        y = [kept("y%d" % j, [P, PC], F32) for j in range(4)]
+        def pick_features(j, entries, z_slot, mastery):
+            nc.vector.tensor_tensor(z_slot, h[j][:].indirect(pos2_sb[:, entries]), mastery[:], ALU.mult)
+
+        z_rows = [kept("z_rows%d" % g, [P, 4, width], F32) for g, (b, first, width) in enumerate(GROUPS)]
+        z_mx = {}
+        y = [kept("y%d" % j, [P, COUPLES], F32) for j in range(OUT_TILES)]
 
         def finish_group(g):
-            b, m0, width = groups[g]
+            b, first, width = GROUPS[g]
             woven = kept("z_woven%d" % g, [P, width, 4], BF16)
-            last = g == len(groups) - 1
-            weave(nc.vector.tensor_copy if last else nc.scalar.copy, woven[:], z_rows[g][:])
-            z_q[g] = quantise("z%d" % g, woven, width)
+            if g == len(GROUPS) - 1:
+                cut = width - LAST_ON_SCALAR
+                weave(nc.vector.tensor_copy, woven[:, 0:cut, :], z_rows[g][:, :, 0:cut])
+                weave(nc.scalar.copy, woven[:, cut:width, :], z_rows[g][:, :, cut:width])
+            else:
+                weave(nc.scalar.copy, woven[:], z_rows[g][:])
+            z_mx[g] = quantise("z%d" % g, woven, width)
             if b == 0:
                 return
-            cols = slice(m0, m0 + width)
-            for j in range(4):
+            couples = slice(first, first + width)
+            moving = [(z_mx[0][0][:, couples], z_mx[0][1][:, couples]), (z_mx[g][0][:], z_mx[g][1][:])]
+            for j in range(OUT_TILES):
                 acc = psum.tile([P, BANK], F32, name="acc")
-                for bb in range(2):
-                    codes, plane = z_q[0] if bb == 0 else z_q[g]
-                    z_cols = cols if bb == 0 else slice(0, width)
+                n_cols = slice(P * j, P * (j + 1))
+                for second_pass in range(2):
                     nc.tensor.matmul_mx(
                         out=acc[:, 0:width],
-                        lhsT=w2_q[bb, j][0][:].bitcast(FP8X4),
-                        lhsT_scale=w2_q[bb, j][1][:],
-                        rhs=codes[:, z_cols].bitcast(FP8X4),
-                        rhs_scale=plane[:, z_cols],
-                        start=(bb == 0),
-                        stop=(bb == 1),
+                        lhsT=w2_mx[second_pass][0][:, n_cols].bitcast(FP8X4),
+                        lhsT_scale=w2_mx[second_pass][1][:, n_cols],
+                        rhs=moving[second_pass][0].bitcast(FP8X4),
+                        rhs_scale=moving[second_pass][1],
+                        start=(second_pass == 0),
+                        stop=(second_pass == 1),
                     )
-                nc.scalar.copy(y[j][:, cols], acc[:, 0:width])
+                nc.scalar.copy(y[j][:, couples], acc[:, 0:width])
 
+        steps = [(g, t) for g in range(len(GROUPS)) for t in range(4)]
         first_product(0)
         first_product(1)
         pending = None
-        for i, (g, t) in enumerate(steps):
-            b, m0, width = groups[g]
+        for step, (g, t) in enumerate(steps):
+            b, first, width = GROUPS[g]
             j = 4 * b + t
-            if i == 1:
-                order_w4(1)
-            picked = pick_couples(i, j, m0, width)
-            if i + 2 < 8:
-                first_product(i + 2)
+            entries = slice(first // PER_COLUMN, (first + width) // PER_COLUMN)
+            mastery = pick_mastery(step, j, entries, width)
+            if step + 2 < ROW_TILES:
+                first_product(step + 2)
             if pending is not None:
-                combine(*pending)
-                if i - 1 < 8:
-                    prepare_w2(i - 1)
+                pick_features(*pending)
                 if t == 0:
                     finish_group(g - 1)
-            pending = (i == len(steps) - 1, j, z_rows[g]) + picked
-        combine(*pending)
-        finish_group(len(groups) - 1)
+                if step - W2_STEP in (0, 1):
+                    quantise_w2(step - W2_STEP)
+            pending = (j, entries, z_rows[g][:, t, :], mastery)
+        pick_features(*pending)
+        finish_group(len(GROUPS) - 1)
 
-        for j in range(4):
-            first = ring.tile([P, PU], F32, name="first")
-            nc.vector.tensor_copy(first[:], y[j][:].indirect(pos3_sb[:]))
-            both = ring.tile([P, PU], F32, name="both")
-            nc.vector.tensor_tensor(both[:], y[j][:].indirect(pos4_sb[:]), first[:], ALU.add)
-            result = ring.tile([P, PU], F32, name="result")
+        for j in range(OUT_TILES):
+            one_couple = ring.tile([P, UNITS], F32, name="one_couple")
+            nc.vector.tensor_copy(one_couple[:], y[j][:].indirect(pos3_sb[:]))
+            both = ring.tile([P, UNITS], F32, name="both")
+            nc.vector.tensor_tensor(both[:], y[j][:].indirect(pos4_sb[:]), one_couple[:], ALU.add)
+            result = ring.tile([P, UNITS], F32, name="result")
             nc.scalar.activation(result[:], both[:], ACT.Silu, bias=bias_sb[:, j : j + 1])
-            nc.sync.dma_start(out[P * j : P * j + P, :], result[:])
+            nc.sync.dma_start(out[P * j : P * (j + 1), :], result[:])

@@ -20,13 +20,14 @@ ALU = mybir.AluOpType
 
 P = 128
 BANK = 512
+PSUM_BANKS = 8
 PER_COLUMN = 16
 ROW_TILES = H // P
 OUT_TILES = N // P
 
 GROUPS = ((0, 0, COUPLES), (1, 0, COUPLES // 2), (1, COUPLES // 2, COUPLES // 2))
 LAST_ON_SCALAR = 64
-PASS0_FIRST = 2
+PASS0_FIRST = 1
 MASTERY_BUFS = 3
 W2_STEP = 3
 
@@ -35,7 +36,9 @@ W4_CODES_AT = (8192, 24576)
 W4_PLANES_AT = 10240
 W2_ROWS_AT = (16320, 26624)
 BIAS_AT = 24512
-SCALE_WINDOW_AT = 32256
+SCALE_WINDOW_AT = 39424
+GAIN_AT = 39424
+W4_RAW1_AT = 14080
 PICKED_PASS1_AT = (35328, 37376)
 W4_SCALE_ROWS_AT = 36352
 
@@ -49,7 +52,7 @@ def tile_list_prerequisite_mastery_kernel(
         keep = ctx.enter_context(tc.tile_pool(name="keep", bufs=1))
         shared = ctx.enter_context(tc.tile_pool(name="shared", bufs=1))
         ring = ctx.enter_context(tc.tile_pool(name="ring", bufs=OUT_TILES))
-        psum = ctx.enter_context(tc.psum_pool(name="psum", bufs=8))
+        psum = ctx.enter_context(tc.psum_pool(name="psum", bufs=PSUM_BANKS))
 
         def load_list(name, dram):
             tile = lists.tile([P, dram.shape[1]], U16, name=name)
@@ -76,6 +79,11 @@ def tile_list_prerequisite_mastery_kernel(
 
         w4_scale_rows = shared.tile([P, 2, H], U8, name="w4_scale_rows", offset=W4_SCALE_ROWS_AT, align_bytes=64)
         nc.vector.memset(w4_scale_rows[:].bitcast(I32), 0)
+        for quad in range(4):
+            nc.gpsimd.dma_start(
+                w4_scale_rows[32 * quad : 32 * quad + 4, :, :].bitcast(I32),
+                w4_scales[:, 4 * quad : 4 * quad + 4, :].rearrange("a s c -> s a c").bitcast(I32),
+            )
         nc.vector.memset(scale_window[64:128, :].bitcast(I32), 0)
         nc.vector.memset(scale_window[32:64, :].bitcast(I32), 0)
         v_planes = kept("v_planes", [P, 2, S], U8)
@@ -86,14 +94,14 @@ def tile_list_prerequisite_mastery_kernel(
             nc.sync.dma_start(words[:].bitcast(I32), tab_words[a].rearrange("p t i -> p (t i)").bitcast(I32))
             return words
 
-        table = [load_table(0)]
-        w4_raw = kept("w4_raw", [P, 2, 2 * H], U8)
-        nc.sync.dma_start(w4_raw[:].bitcast(I32), w4_words.rearrange("a p c -> p a c").bitcast(I32))
-        for quad in range(4):
+        def load_w4_words(b, raw):
             nc.sync.dma_start(
-                w4_scale_rows[32 * quad : 32 * quad + 4, :, :].bitcast(I32),
-                w4_scales[:, 4 * quad : 4 * quad + 4, :].rearrange("a s c -> s a c").bitcast(I32),
+                raw[:].bitcast(I32), w4_words[:, :, H * b : H * (b + 1)].rearrange("a p c -> p a c").bitcast(I32)
             )
+            return raw
+
+        table = [load_table(0)]
+        w4_raw = [load_w4_words(0, kept("w4_raw0", [P, 2, H], U8))]
         table.append(load_table(1))
 
         picked_scale_rows = kept("picked_scale_rows", [P, S], U8)
@@ -101,16 +109,16 @@ def tile_list_prerequisite_mastery_kernel(
         for a in range(2):
             for quad in range(4):
                 first_row = 16 * a + 4 * quad
-                queue = nc.gpsimd if (a, quad) == (0, 3) else nc.scalar
+                queue = nc.gpsimd if (a, quad) == (1, 3) else nc.scalar
                 queue.dma_start(
                     v_planes[32 * quad : 32 * quad + 4, a, :].bitcast(I32),
                     picked_scale_rows[first_row : first_row + 4, :].bitcast(I32),
                 )
 
-        gain_sb = kept("gain_sb", [P, 2, 16], F32)
+        gain_sb = shared.tile([P, 2, 16], F32, name="gain_sb", offset=GAIN_AT)
         gain_view = gain.rearrange("(b q c) -> q b c", b=2, c=16)
         for e in range(4):
-            nc.gpsimd.dma_start(gain_sb[e:P:4, :, 0:13], gain_view[:, :, e : e + 13])
+            nc.scalar.dma_start(gain_sb[e:P:4, :, 0:13], gain_view[:, :, e : e + 13])
 
         v_words = {}
 
@@ -132,12 +140,13 @@ def tile_list_prerequisite_mastery_kernel(
             )
             nc.vector.tensor_copy(
                 codes[:].bitcast(I32).rearrange("p a t (q w) -> p a t q w", w=2),
-                w4_raw[:, :, H * b : H * (b + 1)].bitcast(I32).rearrange("p a (q t w) -> p a t q w", t=4, w=2),
+                w4_raw[b][:].bitcast(I32).rearrange("p a (q t w) -> p a t q w", t=4, w=2),
             )
             w4_codes[b] = codes
 
         gather_words(0, 0)
         gather_words(0, 1)
+        w4_raw.append(load_w4_words(1, shared.tile([P, 2, H], U8, name="w4_raw1", offset=W4_RAW1_AT)))
         order_w4_codes(0)
         w4_planes = shared.tile([P, 4, 4, P], U8, name="w4_planes", offset=W4_PLANES_AT, align_bytes=64)
         nc.vector.tensor_copy(

@@ -25,22 +25,17 @@ PER_COLUMN = 16
 ROW_TILES = H // P
 OUT_TILES = N // P
 
-GROUPS = ((0, 0, COUPLES), (1, 0, COUPLES // 2), (1, COUPLES // 2, COUPLES // 2))
-LAST_ON_SCALAR = 64
-PASS0_FIRST = 1
-MASTERY_BUFS = 3
-W2_STEP = 3
+HALF = COUPLES // 2
+LEAD = 3
+PASS0_FIRST = 3
+EARLY_OUT = 2
 
-TABLE_AT = (7936, 24064)
-W4_CODES_AT = (8192, 24576)
-W4_PLANES_AT = 10240
-W2_ROWS_AT = (16320, 26624)
-BIAS_AT = 24512
-SCALE_WINDOW_AT = 39424
-GAIN_AT = 39424
-W4_RAW1_AT = 14080
-PICKED_PASS1_AT = (35328, 37376)
-W4_SCALE_ROWS_AT = 36352
+W2_ROWS_AT = 0
+TABLE_AT = (16320, 24512)
+W4_CODES1_AT = 24512
+W4_PLANES1_AT = 26624
+BIAS_AT = 26560
+SCALE_WINDOW_AT = 32704
 
 
 def tile_list_prerequisite_mastery_kernel(
@@ -51,7 +46,6 @@ def tile_list_prerequisite_mastery_kernel(
         lists = ctx.enter_context(tc.tile_pool(name="lists", bufs=1))
         keep = ctx.enter_context(tc.tile_pool(name="keep", bufs=1))
         shared = ctx.enter_context(tc.tile_pool(name="shared", bufs=1))
-        ring = ctx.enter_context(tc.tile_pool(name="ring", bufs=OUT_TILES))
         psum = ctx.enter_context(tc.psum_pool(name="psum", bufs=PSUM_BANKS))
 
         def load_list(name, dram):
@@ -59,49 +53,47 @@ def tile_list_prerequisite_mastery_kernel(
             nc.sync.dma_start(tile[:], dram)
             return tile
 
-        def kept(name, shape, dtype):
-            return keep.tile(shape, dtype, name=name, align_bytes=64)
+        def kept(name, shape, dtype, over=None):
+            return keep.tile(shape, dtype, name=name, tag=over or name, align_bytes=64)
+
+        def placed(name, shape, dtype, offset):
+            return shared.tile(shape, dtype, name=name, offset=offset, align_bytes=64)
+
+        scale_window = placed("scale_window", [P, T], U8, SCALE_WINDOW_AT)
+        nc.scalar.dma_start(
+            scale_window[0:32, :].bitcast(I32), tab_scales.rearrange("a q t -> (a q) t").bitcast(I32)
+        )
+        offs_sb = load_list("offs_sb", offs)
+
+        w4_scale_rows = kept("w4_scale_rows", [P, 2, H], U8)
+        nc.gpsimd.memset(w4_scale_rows[:].bitcast(I32), 0)
+        for quad in range(4):
+            nc.scalar.dma_start(
+                w4_scale_rows[32 * quad : 32 * quad + 4, :, :].bitcast(I32),
+                w4_scales[:, 4 * quad : 4 * quad + 4, :].rearrange("a s c -> s a c").bitcast(I32),
+            )
+        gain_sb = kept("gain_sb", [P, 2, 16], F32)
+        gain_view = gain.rearrange("(b q c) -> q b c", b=2, c=16)
+        for e in range(4):
+            nc.gpsimd.dma_start(gain_sb[e:P:4, :, 0:13], gain_view[:, :, e : e + 13])
 
         warm_input = kept("warm_input", [P, 1], F32)
         nc.vector.memset(warm_input[:], 0.0)
         warm = kept("warm", [P, 1], F32)
         nc.scalar.activation(warm[:], warm_input[:], ACT.Sigmoid)
-
-        offs_sb = load_list("offs_sb", offs)
-        scale_window = shared.tile([P, T], U8, name="scale_window", offset=SCALE_WINDOW_AT, align_bytes=64)
-        nc.sync.dma_start(
-            scale_window[0:32, :].bitcast(I32), tab_scales.rearrange("a q t -> (a q) t").bitcast(I32)
-        )
-        pos1_sb = load_list("pos1_sb", pos1)
-        pos2_sb = load_list("pos2_sb", pos2)
-        pos3_sb = load_list("pos3_sb", pos3)
-        pos4_sb = load_list("pos4_sb", pos4)
-
-        w4_scale_rows = shared.tile([P, 2, H], U8, name="w4_scale_rows", offset=W4_SCALE_ROWS_AT, align_bytes=64)
-        nc.vector.memset(w4_scale_rows[:].bitcast(I32), 0)
-        for quad in range(4):
-            nc.gpsimd.dma_start(
-                w4_scale_rows[32 * quad : 32 * quad + 4, :, :].bitcast(I32),
-                w4_scales[:, 4 * quad : 4 * quad + 4, :].rearrange("a s c -> s a c").bitcast(I32),
-            )
         nc.vector.memset(scale_window[64:128, :].bitcast(I32), 0)
         nc.vector.memset(scale_window[32:64, :].bitcast(I32), 0)
         v_planes = kept("v_planes", [P, 2, S], U8)
         nc.vector.memset(v_planes[:].bitcast(I32), 0)
 
         def load_table(a):
-            words = shared.tile([P, T], U32, name="table%d" % a, offset=TABLE_AT[a])
+            words = placed("table%d" % a, [P, T], U32, TABLE_AT[a])
             nc.sync.dma_start(words[:].bitcast(I32), tab_words[a].rearrange("p t i -> p (t i)").bitcast(I32))
             return words
 
-        def load_w4_words(b, raw):
-            nc.sync.dma_start(
-                raw[:].bitcast(I32), w4_words[:, :, H * b : H * (b + 1)].rearrange("a p c -> p a c").bitcast(I32)
-            )
-            return raw
-
         table = [load_table(0)]
-        w4_raw = [load_w4_words(0, kept("w4_raw0", [P, 2, H], U8))]
+        w4_raw = kept("w4_raw", [P, 2, 2 * H], U8)
+        nc.sync.dma_start(w4_raw[:].bitcast(I32), w4_words.rearrange("a p c -> p a c").bitcast(I32))
         table.append(load_table(1))
 
         picked_scale_rows = kept("picked_scale_rows", [P, S], U8)
@@ -109,62 +101,55 @@ def tile_list_prerequisite_mastery_kernel(
         for a in range(2):
             for quad in range(4):
                 first_row = 16 * a + 4 * quad
-                queue = nc.gpsimd if (a, quad) == (1, 3) else nc.scalar
-                queue.dma_start(
-                    v_planes[32 * quad : 32 * quad + 4, a, :].bitcast(I32),
-                    picked_scale_rows[first_row : first_row + 4, :].bitcast(I32),
-                )
+                if first_row > 0:
+                    nc.sync.dma_start(
+                        v_planes[32 * quad : 32 * quad + 4, a, :].bitcast(I32),
+                        picked_scale_rows[first_row : first_row + 4, :].bitcast(I32),
+                    )
+        nc.vector.tensor_copy(v_planes[0:32, 0, :].bitcast(I32), picked_scale_rows[0:32, :].bitcast(I32))
 
-        gain_sb = shared.tile([P, 2, 16], F32, name="gain_sb", offset=GAIN_AT)
-        gain_view = gain.rearrange("(b q c) -> q b c", b=2, c=16)
-        for e in range(4):
-            nc.scalar.dma_start(gain_sb[e:P:4, :, 0:13], gain_view[:, :, e : e + 13])
+        pos1_sb = load_list("pos1_sb", pos1)
+        pos2_sb = load_list("pos2_sb", pos2)
+        pos3_sb = load_list("pos3_sb", pos3)
+        pos4_sb = load_list("pos4_sb", pos4)
 
         v_words = {}
 
         def gather_words(a, half):
-            name = "v_words%d%d" % (a, half)
-            if a == 0:
-                picked = kept(name, [P, BANK], U32)
-            else:
-                picked = shared.tile([P, BANK], U32, name=name, offset=PICKED_PASS1_AT[half], align_bytes=64)
+            picked = kept("v_words%d%d" % (a, half), [P, BANK], U32)
             entries = offs_sb[:, BANK // PER_COLUMN * half : BANK // PER_COLUMN * (half + 1)]
             nc.vector.tensor_copy(picked[:], table[a][:].indirect(entries))
             v_words[a, half] = picked
 
-        w4_codes = {}
+        w4_codes, w4_planes = {}, {}
 
-        def order_w4_codes(b):
-            codes = shared.tile(
-                [P, 2, 4, 2 * P], U8, name="w4_codes%d" % b, offset=W4_CODES_AT[b], align_bytes=64
-            )
+        def order_w4_planes(b, tile):
+            rows = w4_scale_rows[:, :, BANK * b : BANK * (b + 1)].bitcast(I32)
+            nc.vector.tensor_copy(tile[:].bitcast(I32), rows.rearrange("p a (q t) -> p a t q", t=4))
+            w4_planes[b] = tile
+
+        def order_w4_codes(b, tile):
             nc.vector.tensor_copy(
-                codes[:].bitcast(I32).rearrange("p a t (q w) -> p a t q w", w=2),
-                w4_raw[b][:].bitcast(I32).rearrange("p a (q t w) -> p a t q w", t=4, w=2),
+                tile[:].bitcast(I32).rearrange("p a t (q w) -> p a t q w", w=2),
+                w4_raw[:, :, H * b : H * (b + 1)].bitcast(I32).rearrange("p a (q t w) -> p a t q w", t=4, w=2),
             )
-            w4_codes[b] = codes
+            w4_codes[b] = tile
 
+        order_w4_planes(0, kept("w4_planes0", [P, 2, 4, P], U8))
         gather_words(0, 0)
+        order_w4_codes(0, kept("w4_codes0", [P, 2, 4, 2 * P], U8))
         gather_words(0, 1)
-        w4_raw.append(load_w4_words(1, shared.tile([P, 2, H], U8, name="w4_raw1", offset=W4_RAW1_AT)))
-        order_w4_codes(0)
-        w4_planes = shared.tile([P, 4, 4, P], U8, name="w4_planes", offset=W4_PLANES_AT, align_bytes=64)
-        nc.vector.tensor_copy(
-            w4_planes[:].bitcast(I32),
-            w4_scale_rows[:].bitcast(I32).rearrange("p a (b q t) -> p (a b) t q", b=2, t=4),
-        )
         gather_words(1, 0)
         gather_words(1, 1)
-        order_w4_codes(1)
+        order_w4_codes(1, placed("w4_codes1", [P, 2, 4, 2 * P], U8, W4_CODES1_AT))
+        order_w4_planes(1, placed("w4_planes1", [P, 2, 4, P], U8, W4_PLANES1_AT))
 
-        w2_rows = []
+        w2_rows = placed("w2_rows", [P, 2, 4, N], F32, W2_ROWS_AT)
         w2_view = w2.rearrange("(b q t e) n -> b e q t n", b=2, t=4, e=4)
         for b in range(2):
-            raw = shared.tile([P, 4, N], F32, name="w2_rows%d" % b, offset=W2_ROWS_AT[b])
             for e in range(4):
-                nc.sync.dma_start(raw[e:P:4, :, :], w2_view[b][e])
-            w2_rows.append(raw)
-        bias_sb = shared.tile([P, OUT_TILES], F32, name="bias_sb", offset=BIAS_AT)
+                nc.sync.dma_start(w2_rows[e:P:4, b, :, :], w2_view[b][e])
+        bias_sb = placed("bias_sb", [P, OUT_TILES], F32, BIAS_AT)
         with nc.allow_non_contiguous_dma(reason="one value a partition"):
             nc.sync.dma_start(bias_sb[:], bias.rearrange("(j p) -> p j", p=P))
 
@@ -176,12 +161,12 @@ def tile_list_prerequisite_mastery_kernel(
             for half in range(2):
                 cols = slice(BANK * half, BANK * (half + 1))
                 acc = psum.tile([P, BANK], F32, name="acc")
-                order = (0, 1) if j < PASS0_FIRST else (1, 0)
+                order = (0, 1) if 2 * j + half < PASS0_FIRST else (1, 0)
                 for a in order:
                     nc.tensor.matmul_mx(
                         out=acc[:],
                         lhsT=w4_codes[b][:, a, t, :].bitcast(FP4X4),
-                        lhsT_scale=w4_planes[:, 2 * a + b, t, :],
+                        lhsT_scale=w4_planes[b][:, a, t, :],
                         rhs=v_words[a, half][:].bitcast(FP8X4),
                         rhs_scale=v_planes[:, a, cols],
                         start=(a == order[0]),
@@ -190,101 +175,111 @@ def tile_list_prerequisite_mastery_kernel(
                 nc.scalar.copy(rows[:, cols], acc[:])
             h[j] = rows
 
-        def weave(engine_copy, woven, rows):
-            engine_copy(
-                woven.rearrange("p (c i) t -> p c t i", i=4),
-                rows.rearrange("p t (c i) -> p c t i", i=4),
-            )
-
-        def quantise(name, woven, width):
-            codes = kept(name + "_codes", [P, width], U32)
-            plane = kept(name + "_plane", [P, width], U8)
-            nc.vector.quantize_mx(
-                out=codes[:].bitcast(FP8X4), scales=plane[:], in_=woven[:].rearrange("p m t -> p (m t)")
-            )
-            return codes, plane
+        def quantise(codes, plane, woven):
+            nc.vector.quantize_mx(out=codes.bitcast(FP8X4), scales=plane, in_=woven)
 
         w2_mx = {}
 
-        def quantise_w2(b):
-            woven = keep.tile([P, N, 4], BF16, name="w2_woven%d" % b, tag="h%d" % (W2_STEP - 1 + b), align_bytes=64)
-            weave(nc.vector.tensor_copy, woven[:], w2_rows[b][:])
-            w2_mx[b] = quantise("w2_%d" % b, woven, N)
+        def quantise_w2(j, over):
+            woven = kept("w2_woven%d" % j, [P, 2, P, 4], BF16, over)
+            nc.vector.tensor_copy(
+                woven[:].rearrange("p b (c i) t -> p b c t i", i=4),
+                w2_rows[:, :, :, P * j : P * (j + 1)].rearrange("p b t (c i) -> p b c t i", i=4),
+            )
+            codes = kept("w2_codes%d" % j, [P, 2, P], U32)
+            plane = kept("w2_plane%d" % j, [P, 2, P], U8)
+            quantise(
+                codes[:].rearrange("p b n -> p (b n)"),
+                plane[:].rearrange("p b n -> p (b n)"),
+                woven[:].rearrange("p b n t -> p (b n t)"),
+            )
+            w2_mx[j] = (codes, plane)
 
-        def pick_mastery(step, j, entries, width):
+        left = {}
+
+        def pick_left(j):
+            left[j] = kept("left%d" % j, [P, COUPLES], F32)
+            nc.vector.tensor_copy(left[j][:], h[j][:].indirect(pos1_sb[:]))
+
+        mastery = {}
+
+        def gate(j):
             b, t = divmod(j, 4)
-            factor = gain_sb[:, b, 4 * t : 4 * t + 1]
-            mastery = ring.tile([P, width], F32, name="mastery", bufs=MASTERY_BUFS)
-            nc.vector.tensor_copy(mastery[:], h[j][:].indirect(pos1_sb[:, entries]))
-            nc.scalar.activation(mastery[:], mastery[:], ACT.Sigmoid)
-            if step == 0:
-                nc.vector.tensor_scalar(mastery[:], mastery[:], factor, None, ALU.mult)
-            else:
-                nc.scalar.activation(mastery[:], mastery[:], ACT.Copy, scale=factor)
-            return mastery
+            nc.scalar.activation(left[j][:], left[j][:], ACT.Sigmoid)
+            mastery[j] = kept("mastery%d" % j, [P, COUPLES], F32)
+            nc.scalar.activation(mastery[j][:], left[j][:], ACT.Copy, scale=gain_sb[:, b, 4 * t : 4 * t + 1])
 
-        def pick_features(j, entries, z_slot, mastery):
-            nc.vector.tensor_tensor(z_slot, h[j][:].indirect(pos2_sb[:, entries]), mastery[:], ALU.mult)
+        def pick_right(j, z_slot, first, width):
+            entries = pos2_sb[:, first // PER_COLUMN : (first + width) // PER_COLUMN]
+            nc.vector.tensor_tensor(z_slot, h[j][:].indirect(entries), mastery[j][:, first : first + width], ALU.mult)
 
-        z_rows = [kept("z_rows%d" % g, [P, 4, width], F32) for g, (b, first, width) in enumerate(GROUPS)]
-        z_mx = {}
+        def weave_z(name, rows, width):
+            woven = kept(name, [P, width, 4], BF16)
+            nc.scalar.copy(
+                woven[:].rearrange("p (c i) t -> p c t i", i=4), rows[:].rearrange("p t (c i) -> p c t i", i=4)
+            )
+            return woven[:].rearrange("p m t -> p (m t)")
+
+        z_codes = [kept("z_codes%d" % b, [P, COUPLES], U32) for b in range(2)]
+        z_plane = [kept("z_plane%d" % b, [P, COUPLES], U8) for b in range(2)]
         y = [kept("y%d" % j, [P, COUPLES], F32) for j in range(OUT_TILES)]
 
-        def finish_group(g):
-            b, first, width = GROUPS[g]
-            woven = kept("z_woven%d" % g, [P, width, 4], BF16)
-            if g == len(GROUPS) - 1:
-                cut = width - LAST_ON_SCALAR
-                weave(nc.vector.tensor_copy, woven[:, 0:cut, :], z_rows[g][:, :, 0:cut])
-                weave(nc.scalar.copy, woven[:, cut:width, :], z_rows[g][:, :, cut:width])
-            else:
-                weave(nc.scalar.copy, woven[:], z_rows[g][:])
-            z_mx[g] = quantise("z%d" % g, woven, width)
-            if b == 0:
-                return
-            couples = slice(first, first + width)
-            moving = [(z_mx[0][0][:, couples], z_mx[0][1][:, couples]), (z_mx[g][0][:], z_mx[g][1][:])]
-            for j in range(OUT_TILES):
-                acc = psum.tile([P, BANK], F32, name="acc")
-                n_cols = slice(P * j, P * (j + 1))
-                for second_pass in range(2):
-                    nc.tensor.matmul_mx(
-                        out=acc[:, 0:width],
-                        lhsT=w2_mx[second_pass][0][:, n_cols].bitcast(FP8X4),
-                        lhsT_scale=w2_mx[second_pass][1][:, n_cols],
-                        rhs=moving[second_pass][0].bitcast(FP8X4),
-                        rhs_scale=moving[second_pass][1],
-                        start=(second_pass == 0),
-                        stop=(second_pass == 1),
-                    )
-                nc.scalar.copy(y[j][:, couples], acc[:, 0:width])
+        def second_product(j, couples):
+            acc = psum.tile([P, BANK], F32, name="acc")
+            width = couples.stop - couples.start
+            for b in range(2):
+                nc.tensor.matmul_mx(
+                    out=acc[:, 0:width],
+                    lhsT=w2_mx[j][0][:, b, :].bitcast(FP8X4),
+                    lhsT_scale=w2_mx[j][1][:, b, :],
+                    rhs=z_codes[b][:, couples].bitcast(FP8X4),
+                    rhs_scale=z_plane[b][:, couples],
+                    start=(b == 0),
+                    stop=(b == 1),
+                )
+            nc.scalar.copy(y[j][:, couples], acc[:, 0:width])
 
-        steps = [(g, t) for g in range(len(GROUPS)) for t in range(4)]
-        first_product(0)
-        first_product(1)
-        pending = None
-        for step, (g, t) in enumerate(steps):
-            b, first, width = GROUPS[g]
-            j = 4 * b + t
-            entries = slice(first // PER_COLUMN, (first + width) // PER_COLUMN)
-            mastery = pick_mastery(step, j, entries, width)
-            if step + 2 < ROW_TILES:
-                first_product(step + 2)
-            if pending is not None:
-                pick_features(*pending)
-                if t == 0:
-                    finish_group(g - 1)
-                if step - W2_STEP in (0, 1):
-                    quantise_w2(step - W2_STEP)
-            pending = (j, entries, z_rows[g][:, t, :], mastery)
-        pick_features(*pending)
-        finish_group(len(GROUPS) - 1)
+        z_rows0 = kept("z_rows0", [P, 4, COUPLES], F32)
+        z_rows_low = kept("z_rows_low", [P, 4, HALF], F32)
+        for j in range(LEAD):
+            first_product(j)
+            pick_left(j)
+        for j in range(ROW_TILES):
+            b, t = divmod(j, 4)
+            gate(j)
+            if b == 0:
+                pick_right(j, z_rows0[:, t, :], 0, COUPLES)
+            else:
+                pick_right(j, z_rows_low[:, t, :], 0, HALF)
+            if j + LEAD < ROW_TILES:
+                first_product(j + LEAD)
+                pick_left(j + LEAD)
+            elif j + 1 < ROW_TILES:
+                quantise_w2(j + LEAD - ROW_TILES, "left%d" % j)
+
+        low, high = slice(0, HALF), slice(HALF, COUPLES)
+        woven0 = weave_z("z_woven0", z_rows0, COUPLES)
+        woven_low = weave_z("z_woven_low", z_rows_low, HALF)
+        quantise(z_codes[0][:], z_plane[0][:], woven0)
+        quantise(z_codes[1][:, low], z_plane[1][:, low], woven_low)
+        z_rows_high = kept("z_rows_high", [P, 4, HALF], F32, "z_woven0")
+        for t in range(4):
+            pick_right(4 + t, z_rows_high[:, t, :], HALF, HALF)
+        woven_high = weave_z("z_woven_high", z_rows_high, HALF)
+        quantise(z_codes[1][:, high], z_plane[1][:, high], woven_high)
+        quantise_w2(2, "h%d" % (ROW_TILES - 1))
+        quantise_w2(3, "z_woven_high")
+        for couples in (low, high):
+            for j in range(EARLY_OUT):
+                second_product(j, couples)
+        for j in range(EARLY_OUT, OUT_TILES):
+            second_product(j, slice(0, COUPLES))
 
         for j in range(OUT_TILES):
-            one_couple = ring.tile([P, UNITS], F32, name="one_couple")
+            one_couple = kept("one_couple%d" % j, [P, UNITS], F32)
             nc.vector.tensor_copy(one_couple[:], y[j][:].indirect(pos3_sb[:]))
-            both = ring.tile([P, UNITS], F32, name="both")
+            both = kept("both%d" % j, [P, UNITS], F32)
             nc.vector.tensor_tensor(both[:], y[j][:].indirect(pos4_sb[:]), one_couple[:], ALU.add)
-            result = ring.tile([P, UNITS], F32, name="result")
+            result = kept("result%d" % j, [P, UNITS], F32)
             nc.scalar.activation(result[:], both[:], ACT.Silu, bias=bias_sb[:, j : j + 1])
             nc.sync.dma_start(out[P * j : P * (j + 1), :], result[:])

@@ -148,7 +148,7 @@ def tile_list_prerequisite_mastery_kernel(
         w2_view = w2.rearrange("(b q t e) n -> b e q t n", b=2, t=4, e=4)
         for b in range(2):
             for e in range(4):
-                nc.sync.dma_start(w2_rows[e:P:4, b, :, :], w2_view[b][e])
+                (nc.sync, nc.gpsimd)[b].dma_start(w2_rows[e:P:4, b, :, :], w2_view[b][e])
         bias_sb = placed("bias_sb", [P, OUT_TILES], F32, BIAS_AT)
         with nc.allow_non_contiguous_dma(reason="one value a partition"):
             nc.sync.dma_start(bias_sb[:], bias.rearrange("(j p) -> p j", p=P))
@@ -220,24 +220,34 @@ def tile_list_prerequisite_mastery_kernel(
             )
             return woven[:].rearrange("p m t -> p (m t)")
 
-        z_codes = [kept("z_codes%d" % b, [P, COUPLES], U32) for b in range(2)]
-        z_plane = [kept("z_plane%d" % b, [P, COUPLES], U8) for b in range(2)]
+        low, high, whole = slice(0, HALF), slice(HALF, COUPLES), slice(0, COUPLES)
+        z_mx = {}
+
+        def quantise_z(name, woven, width):
+            codes = kept(name + "_codes", [P, width], U32)
+            plane = kept(name + "_plane", [P, width], U8)
+            quantise(codes[:], plane[:], woven)
+            z_mx[name] = (codes, plane)
+
         y = [kept("y%d" % j, [P, COUPLES], F32) for j in range(OUT_TILES)]
 
         def second_product(j, couples):
             acc = psum.tile([P, BANK], F32, name="acc")
-            width = couples.stop - couples.start
-            for b in range(2):
+            passes = [(0, couples, z_mx["z0"][0][:, couples], z_mx["z0"][1][:, couples])]
+            for name, part in (("z_low", low), ("z_high", high)):
+                if couples.start <= part.start and part.stop <= couples.stop:
+                    passes.append((1, part, z_mx[name][0][:], z_mx[name][1][:]))
+            for i, (b, part, codes, plane) in enumerate(passes):
                 nc.tensor.matmul_mx(
-                    out=acc[:, 0:width],
+                    out=acc[:, part],
                     lhsT=w2_mx[j][0][:, b, :].bitcast(FP8X4),
                     lhsT_scale=w2_mx[j][1][:, b, :],
-                    rhs=z_codes[b][:, couples].bitcast(FP8X4),
-                    rhs_scale=z_plane[b][:, couples],
-                    start=(b == 0),
-                    stop=(b == 1),
+                    rhs=codes.bitcast(FP8X4),
+                    rhs_scale=plane,
+                    start=(i == 0),
+                    stop=(i == len(passes) - 1),
                 )
-            nc.scalar.copy(y[j][:, couples], acc[:, 0:width])
+            nc.scalar.copy(y[j][:, couples], acc[:, couples])
 
         z_rows0 = kept("z_rows0", [P, 4, COUPLES], F32)
         z_rows_low = kept("z_rows_low", [P, 4, HALF], F32)
@@ -257,23 +267,22 @@ def tile_list_prerequisite_mastery_kernel(
             elif j + 1 < ROW_TILES:
                 quantise_w2(j + LEAD - ROW_TILES, "left%d" % j)
 
-        low, high = slice(0, HALF), slice(HALF, COUPLES)
         woven0 = weave_z("z_woven0", z_rows0, COUPLES)
         woven_low = weave_z("z_woven_low", z_rows_low, HALF)
-        quantise(z_codes[0][:], z_plane[0][:], woven0)
-        quantise(z_codes[1][:, low], z_plane[1][:, low], woven_low)
+        quantise_z("z0", woven0, COUPLES)
+        quantise_z("z_low", woven_low, HALF)
         z_rows_high = kept("z_rows_high", [P, 4, HALF], F32, "z_woven0")
         for t in range(4):
             pick_right(4 + t, z_rows_high[:, t, :], HALF, HALF)
         woven_high = weave_z("z_woven_high", z_rows_high, HALF)
-        quantise(z_codes[1][:, high], z_plane[1][:, high], woven_high)
+        quantise_z("z_high", woven_high, HALF)
         quantise_w2(2, "h%d" % (ROW_TILES - 1))
         quantise_w2(3, "z_woven_high")
         for couples in (low, high):
             for j in range(EARLY_OUT):
                 second_product(j, couples)
         for j in range(EARLY_OUT, OUT_TILES):
-            second_product(j, slice(0, COUPLES))
+            second_product(j, whole)
 
         for j in range(OUT_TILES):
             one_couple = kept("one_couple%d" % j, [P, UNITS], F32)

@@ -28,7 +28,8 @@ OUT_TILES = N // P
 HALF = COUPLES // 2
 LEAD = 3
 PASS0_FIRST = 3
-EARLY_OUT = 2
+
+LAST_ON_VECTOR = 176
 
 W2_ROWS_AT = 0
 TABLE_AT = (16320, 24512)
@@ -180,20 +181,18 @@ def tile_list_prerequisite_mastery_kernel(
 
         w2_mx = {}
 
-        def quantise_w2(j, over):
-            woven = kept("w2_woven%d" % j, [P, 2, P, 4], BF16, over)
-            nc.vector.tensor_copy(
-                woven[:].rearrange("p b (c i) t -> p b c t i", i=4),
-                w2_rows[:, :, :, P * j : P * (j + 1)].rearrange("p b t (c i) -> p b c t i", i=4),
-            )
-            codes = kept("w2_codes%d" % j, [P, 2, P], U32)
-            plane = kept("w2_plane%d" % j, [P, 2, P], U8)
-            quantise(
-                codes[:].rearrange("p b n -> p (b n)"),
-                plane[:].rearrange("p b n -> p (b n)"),
-                woven[:].rearrange("p b n t -> p (b n t)"),
-            )
-            w2_mx[j] = (codes, plane)
+        def round_w2(b, j, woven):
+            rows = w2_rows[:, b, :, P * j : P * (j + 1)]
+            nc.gpsimd.tensor_scalar(woven, rows.rearrange("p t n -> p n t"), 1.0, 0.0, ALU.mult, ALU.add)
+
+        def quantise_w2(b, parts, over):
+            codes = kept("w2_codes%d" % b, [P, N], U32, over)
+            plane = kept("w2_plane%d" % b, [P, N], U8)
+            width = N // len(parts)
+            for i, woven in enumerate(parts):
+                cols = slice(width * i, width * (i + 1))
+                quantise(codes[:, cols], plane[:, cols], woven[:].rearrange("p n t -> p (n t)"))
+            w2_mx[b] = (codes, plane)
 
         left = {}
 
@@ -213,11 +212,14 @@ def tile_list_prerequisite_mastery_kernel(
             entries = pos2_sb[:, first // PER_COLUMN : (first + width) // PER_COLUMN]
             nc.vector.tensor_tensor(z_slot, h[j][:].indirect(entries), mastery[j][:, first : first + width], ALU.mult)
 
-        def weave_z(name, rows, width):
+        def weave_z(name, rows, width, on_vector=0):
             woven = kept(name, [P, width, 4], BF16)
-            nc.scalar.copy(
-                woven[:].rearrange("p (c i) t -> p c t i", i=4), rows[:].rearrange("p t (c i) -> p c t i", i=4)
-            )
+            for copy, cols in ((nc.vector.tensor_copy, slice(0, on_vector)), (nc.scalar.copy, slice(on_vector, width))):
+                if cols.start < cols.stop:
+                    copy(
+                        woven[:, cols, :].rearrange("p (c i) t -> p c t i", i=4),
+                        rows[:, :, cols].rearrange("p t (c i) -> p c t i", i=4),
+                    )
             return woven[:].rearrange("p m t -> p (m t)")
 
         low, high, whole = slice(0, HALF), slice(HALF, COUPLES), slice(0, COUPLES)
@@ -231,58 +233,57 @@ def tile_list_prerequisite_mastery_kernel(
 
         y = [kept("y%d" % j, [P, COUPLES], F32) for j in range(OUT_TILES)]
 
-        def second_product(j, couples):
+        def second_product(j):
             acc = psum.tile([P, BANK], F32, name="acc")
-            passes = [(0, couples, z_mx["z0"][0][:, couples], z_mx["z0"][1][:, couples])]
-            for name, part in (("z_low", low), ("z_high", high)):
-                if couples.start <= part.start and part.stop <= couples.stop:
-                    passes.append((1, part, z_mx[name][0][:], z_mx[name][1][:]))
-            for i, (b, part, codes, plane) in enumerate(passes):
+            n_cols = slice(P * j, P * (j + 1))
+            passes = ((0, whole, "z0"), (1, low, "z_low"), (1, high, "z_high"))
+            for i, (b, couples, name) in enumerate(passes):
                 nc.tensor.matmul_mx(
-                    out=acc[:, part],
-                    lhsT=w2_mx[j][0][:, b, :].bitcast(FP8X4),
-                    lhsT_scale=w2_mx[j][1][:, b, :],
-                    rhs=codes.bitcast(FP8X4),
-                    rhs_scale=plane,
+                    out=acc[:, couples],
+                    lhsT=w2_mx[b][0][:, n_cols].bitcast(FP8X4),
+                    lhsT_scale=w2_mx[b][1][:, n_cols],
+                    rhs=z_mx[name][0][:].bitcast(FP8X4),
+                    rhs_scale=z_mx[name][1][:],
                     start=(i == 0),
                     stop=(i == len(passes) - 1),
                 )
-            nc.scalar.copy(y[j][:, couples], acc[:, couples])
+            nc.scalar.copy(y[j][:], acc[:])
 
         z_rows0 = kept("z_rows0", [P, 4, COUPLES], F32)
         z_rows_low = kept("z_rows_low", [P, 4, HALF], F32)
         for j in range(LEAD):
             first_product(j)
             pick_left(j)
+        w2_woven = [[kept("w2_woven0", [P, N, 4], BF16)], []]
+        for j in range(OUT_TILES):
+            round_w2(0, j, w2_woven[0][0][:, P * j : P * (j + 1), :])
         for j in range(ROW_TILES):
             b, t = divmod(j, 4)
             gate(j)
             if b == 0:
                 pick_right(j, z_rows0[:, t, :], 0, COUPLES)
+                w2_woven[1].append(kept("w2_woven1%d" % t, [P, P, 4], BF16, "mastery%d" % j))
+                round_w2(1, t, w2_woven[1][t][:])
             else:
                 pick_right(j, z_rows_low[:, t, :], 0, HALF)
             if j + LEAD < ROW_TILES:
                 first_product(j + LEAD)
                 pick_left(j + LEAD)
             elif j + 1 < ROW_TILES:
-                quantise_w2(j + LEAD - ROW_TILES, "left%d" % j)
+                late = j + LEAD - ROW_TILES
+                quantise_w2(late, w2_woven[late], "left%d" % j)
 
         woven0 = weave_z("z_woven0", z_rows0, COUPLES)
         woven_low = weave_z("z_woven_low", z_rows_low, HALF)
         quantise_z("z0", woven0, COUPLES)
         quantise_z("z_low", woven_low, HALF)
-        z_rows_high = kept("z_rows_high", [P, 4, HALF], F32, "z_woven0")
+        z_rows_high = kept("z_rows_high", [P, 4, HALF], F32, "left%d" % (ROW_TILES - 1))
         for t in range(4):
             pick_right(4 + t, z_rows_high[:, t, :], HALF, HALF)
-        woven_high = weave_z("z_woven_high", z_rows_high, HALF)
+        woven_high = weave_z("z_woven_high", z_rows_high, HALF, LAST_ON_VECTOR)
         quantise_z("z_high", woven_high, HALF)
-        quantise_w2(2, "h%d" % (ROW_TILES - 1))
-        quantise_w2(3, "z_woven_high")
-        for couples in (low, high):
-            for j in range(EARLY_OUT):
-                second_product(j, couples)
-        for j in range(EARLY_OUT, OUT_TILES):
-            second_product(j, whole)
+        for j in range(OUT_TILES):
+            second_product(j)
 
         for j in range(OUT_TILES):
             one_couple = kept("one_couple%d" % j, [P, UNITS], F32)

@@ -31,12 +31,12 @@ PASS0_FIRST = 3
 
 LAST_ON_VECTOR = 176
 
-W2_ROWS_AT = 0
-TABLE_AT = (16320, 24512)
-W4_CODES1_AT = 24512
-W4_PLANES1_AT = 26624
-BIAS_AT = 26560
-SCALE_WINDOW_AT = 32704
+W2_ROWS_AT = (0, 24448)
+TABLE_AT = (8128, 16320)
+W4_CODES1_AT = 16320
+BIAS_AT = 18368
+W4_PLANES1_AT = 18432
+SCALE_WINDOW_AT = 32640
 
 
 def tile_list_prerequisite_mastery_kernel(
@@ -145,11 +145,11 @@ def tile_list_prerequisite_mastery_kernel(
         order_w4_codes(1, placed("w4_codes1", [P, 2, 4, 2 * P], U8, W4_CODES1_AT))
         order_w4_planes(1, placed("w4_planes1", [P, 2, 4, P], U8, W4_PLANES1_AT))
 
-        w2_rows = placed("w2_rows", [P, 2, 4, N], F32, W2_ROWS_AT)
+        w2_rows = [placed("w2_rows%d" % b, [P, 4, N], F32, W2_ROWS_AT[b]) for b in range(2)]
         w2_view = w2.rearrange("(b q t e) n -> b e q t n", b=2, t=4, e=4)
         for b in range(2):
             for e in range(4):
-                (nc.sync, nc.gpsimd)[b].dma_start(w2_rows[e:P:4, b, :, :], w2_view[b][e])
+                (nc.gpsimd, nc.sync)[b].dma_start(w2_rows[b][e:P:4, :, :], w2_view[b][e])
         bias_sb = placed("bias_sb", [P, OUT_TILES], F32, BIAS_AT)
         with nc.allow_non_contiguous_dma(reason="one value a partition"):
             nc.sync.dma_start(bias_sb[:], bias.rearrange("(j p) -> p j", p=P))
@@ -182,17 +182,18 @@ def tile_list_prerequisite_mastery_kernel(
         w2_mx = {}
 
         def round_w2(b, j, woven):
-            rows = w2_rows[:, b, :, P * j : P * (j + 1)]
+            rows = w2_rows[b][:, :, P * j : P * (j + 1)]
             nc.gpsimd.tensor_scalar(woven, rows.rearrange("p t n -> p n t"), 1.0, 0.0, ALU.mult, ALU.add)
 
-        def quantise_w2(b, parts, over):
-            codes = kept("w2_codes%d" % b, [P, N], U32, over)
-            plane = kept("w2_plane%d" % b, [P, N], U8)
-            width = N // len(parts)
+        def quantise_w2(b, first, parts, over):
+            widths = [woven.shape[1] for woven in parts]
+            codes = kept("w2_codes%d%d" % (b, first), [P, sum(widths)], U32, over)
+            plane = kept("w2_plane%d%d" % (b, first), [P, sum(widths)], U8)
             for i, woven in enumerate(parts):
-                cols = slice(width * i, width * (i + 1))
+                cols = slice(sum(widths[:i]), sum(widths[: i + 1]))
                 quantise(codes[:, cols], plane[:, cols], woven[:].rearrange("p n t -> p (n t)"))
-            w2_mx[b] = (codes, plane)
+            for i in range(sum(widths) // P):
+                w2_mx[b, first + i] = (codes[:, P * i : P * (i + 1)], plane[:, P * i : P * (i + 1)])
 
         left = {}
 
@@ -235,13 +236,12 @@ def tile_list_prerequisite_mastery_kernel(
 
         def second_product(j):
             acc = psum.tile([P, BANK], F32, name="acc")
-            n_cols = slice(P * j, P * (j + 1))
             passes = ((0, whole, "z0"), (1, low, "z_low"), (1, high, "z_high"))
             for i, (b, couples, name) in enumerate(passes):
                 nc.tensor.matmul_mx(
                     out=acc[:, couples],
-                    lhsT=w2_mx[b][0][:, n_cols].bitcast(FP8X4),
-                    lhsT_scale=w2_mx[b][1][:, n_cols],
+                    lhsT=w2_mx[b, j][0].bitcast(FP8X4),
+                    lhsT_scale=w2_mx[b, j][1],
                     rhs=z_mx[name][0][:].bitcast(FP8X4),
                     rhs_scale=z_mx[name][1][:],
                     start=(i == 0),
@@ -262,8 +262,9 @@ def tile_list_prerequisite_mastery_kernel(
             gate(j)
             if b == 0:
                 pick_right(j, z_rows0[:, t, :], 0, COUPLES)
-                w2_woven[1].append(kept("w2_woven1%d" % t, [P, P, 4], BF16, "mastery%d" % j))
-                round_w2(1, t, w2_woven[1][t][:])
+                if t > 0:
+                    w2_woven[1].append(kept("w2_woven1%d" % t, [P, P, 4], BF16, "mastery%d" % j))
+                    round_w2(1, t - 1, w2_woven[1][-1][:])
             else:
                 pick_right(j, z_rows_low[:, t, :], 0, HALF)
             if j + LEAD < ROW_TILES:
@@ -271,7 +272,7 @@ def tile_list_prerequisite_mastery_kernel(
                 pick_left(j + LEAD)
             elif j + 1 < ROW_TILES:
                 late = j + LEAD - ROW_TILES
-                quantise_w2(late, w2_woven[late], "left%d" % j)
+                quantise_w2(late, 0, w2_woven[late], "left%d" % j)
 
         woven0 = weave_z("z_woven0", z_rows0, COUPLES)
         woven_low = weave_z("z_woven_low", z_rows_low, HALF)
@@ -282,6 +283,12 @@ def tile_list_prerequisite_mastery_kernel(
             pick_right(4 + t, z_rows_high[:, t, :], HALF, HALF)
         woven_high = weave_z("z_woven_high", z_rows_high, HALF, LAST_ON_VECTOR)
         quantise_z("z_high", woven_high, HALF)
+        last_woven = kept("w2_woven_last", [P, P, 4], BF16, "z_woven_high")
+        nc.vector.tensor_copy(
+            last_woven[:].rearrange("p (c i) t -> p c t i", i=4),
+            w2_rows[1][:, :, N - P : N].rearrange("p t (c i) -> p c t i", i=4),
+        )
+        quantise_w2(1, OUT_TILES - 1, [last_woven], None)
         for j in range(OUT_TILES):
             second_product(j)
 

@@ -27,9 +27,11 @@ OUT_TILES = N // P
 
 HALF = COUPLES // 2
 LEAD = 3
-PASS0_FIRST = 3
+PASS0_FIRST = 4
 
 LAST_ON_VECTOR = 176
+
+WARM_PASSES = 4
 
 W2_ROWS_AT = (0, 24448)
 TABLE_AT = (8128, 16320)
@@ -137,6 +139,17 @@ def tile_list_prerequisite_mastery_kernel(
             w4_codes[b] = tile
 
         order_w4_planes(0, kept("w4_planes0", [P, 2, 4, P], U8))
+        idle = psum.tile([P, BANK], F32, name="acc")
+        for i in range(WARM_PASSES):
+            nc.tensor.matmul_mx(
+                out=idle[:],
+                lhsT=w4_raw[:, 0, 2 * P * i : 2 * P * (i + 1)].bitcast(FP4X4),
+                lhsT_scale=w4_scale_rows[:, 0, P * i : P * (i + 1)],
+                rhs=table[0][:, 0:BANK].bitcast(FP8X4),
+                rhs_scale=w4_scale_rows[:, 1, 0:BANK],
+                start=True,
+                stop=True,
+            )
         gather_words(0, 0)
         order_w4_codes(0, kept("w4_codes0", [P, 2, 4, 2 * P], U8))
         gather_words(0, 1)
@@ -156,10 +169,12 @@ def tile_list_prerequisite_mastery_kernel(
 
         h = {}
 
-        def first_product(j):
+        def first_product(j, halves=(0, 1)):
             b, t = divmod(j, 4)
-            rows = kept("h%d" % j, [P, S], F32)
-            for half in range(2):
+            if j not in h:
+                h[j] = kept("h%d" % j, [P, S], F32)
+            rows = h[j]
+            for half in halves:
                 cols = slice(BANK * half, BANK * (half + 1))
                 acc = psum.tile([P, BANK], F32, name="acc")
                 order = (0, 1) if 2 * j + half < PASS0_FIRST else (1, 0)
@@ -174,7 +189,6 @@ def tile_list_prerequisite_mastery_kernel(
                         stop=(a == order[1]),
                     )
                 nc.scalar.copy(rows[:, cols], acc[:])
-            h[j] = rows
 
         def quantise(codes, plane, woven):
             nc.vector.quantize_mx(out=codes.bitcast(FP8X4), scales=plane, in_=woven)
@@ -234,24 +248,32 @@ def tile_list_prerequisite_mastery_kernel(
 
         y = [kept("y%d" % j, [P, COUPLES], F32) for j in range(OUT_TILES)]
 
-        def second_product(j):
+        def second_product(j, couples):
             acc = psum.tile([P, BANK], F32, name="acc")
-            passes = ((0, whole, "z0"), (1, low, "z_low"), (1, high, "z_high"))
-            for i, (b, couples, name) in enumerate(passes):
+            passes = [(0, couples, z_mx["z0"][0][:, couples], z_mx["z0"][1][:, couples])]
+            for name, part in (("z_low", low), ("z_high", high)):
+                if couples.start <= part.start and part.stop <= couples.stop:
+                    passes.append((1, part, z_mx[name][0][:], z_mx[name][1][:]))
+            for i, (b, part, codes, plane) in enumerate(passes):
                 nc.tensor.matmul_mx(
-                    out=acc[:, couples],
+                    out=acc[:, part],
                     lhsT=w2_mx[b, j][0].bitcast(FP8X4),
                     lhsT_scale=w2_mx[b, j][1],
-                    rhs=z_mx[name][0][:].bitcast(FP8X4),
-                    rhs_scale=z_mx[name][1][:],
+                    rhs=codes.bitcast(FP8X4),
+                    rhs_scale=plane,
                     start=(i == 0),
                     stop=(i == len(passes) - 1),
                 )
-            nc.scalar.copy(y[j][:], acc[:])
+            nc.scalar.copy(y[j][:, couples], acc[:, couples])
 
         z_rows0 = kept("z_rows0", [P, 4, COUPLES], F32)
         z_rows_low = kept("z_rows_low", [P, 4, HALF], F32)
-        for j in range(LEAD):
+        for half in range(2):
+            for j in range(2):
+                first_product(j, (half,))
+        pick_left(0)
+        pick_left(1)
+        for j in range(2, LEAD):
             first_product(j)
             pick_left(j)
         w2_woven = [[kept("w2_woven0", [P, N, 4], BF16)], []]
@@ -289,14 +311,23 @@ def tile_list_prerequisite_mastery_kernel(
             w2_rows[1][:, :, N - P : N].rearrange("p t (c i) -> p c t i", i=4),
         )
         quantise_w2(1, OUT_TILES - 1, [last_woven], None)
-        for j in range(OUT_TILES):
-            second_product(j)
+        second_product(0, low)
+        second_product(0, high)
+        for j in range(1, OUT_TILES):
+            second_product(j, whole)
 
         for j in range(OUT_TILES):
             one_couple = kept("one_couple%d" % j, [P, UNITS], F32)
-            nc.vector.tensor_copy(one_couple[:], y[j][:].indirect(pos3_sb[:]))
             both = kept("both%d" % j, [P, UNITS], F32)
-            nc.vector.tensor_tensor(both[:], y[j][:].indirect(pos4_sb[:]), one_couple[:], ALU.add)
+            parts = [slice(UNITS // 2 * i, UNITS // 2 * (i + 1)) for i in range(2)]
+            entries = [slice(part.start // PER_COLUMN, part.stop // PER_COLUMN) for part in parts]
+            for i in range(2):
+                nc.vector.tensor_copy(one_couple[:, parts[i]], y[j][:].indirect(pos3_sb[:, entries[i]]))
+            for i in range(2):
+                nc.vector.tensor_tensor(
+                    both[:, parts[i]], y[j][:].indirect(pos4_sb[:, entries[i]]), one_couple[:, parts[i]], ALU.add
+                )
             result = kept("result%d" % j, [P, UNITS], F32)
-            nc.scalar.activation(result[:], both[:], ACT.Silu, bias=bias_sb[:, j : j + 1])
-            nc.sync.dma_start(out[P * j : P * (j + 1), :], result[:])
+            for part in parts if j == OUT_TILES - 1 else [slice(0, UNITS)]:
+                nc.scalar.activation(result[:, part], both[:, part], ACT.Silu, bias=bias_sb[:, j : j + 1])
+                nc.sync.dma_start(out[P * j : P * (j + 1), part], result[:, part])

@@ -25,20 +25,20 @@ PER_COLUMN = 16
 ROW_TILES = H // P
 OUT_TILES = N // P
 
-HALF = COUPLES // 2
-LEAD = 3
+LEAD = 5
+PIECES = (slice(0, 256), slice(256, 384), slice(384, 512))
 PASS0_FIRST = 4
-
-LAST_ON_VECTOR = 176
-
 WARM_PASSES = 4
+PAIR = 2 * P
 
-W2_ROWS_AT = (0, 24448)
-TABLE_AT = (8128, 16320)
-W4_CODES1_AT = 16320
-BIAS_AT = 18368
-W4_PLANES1_AT = 18432
-SCALE_WINDOW_AT = 32640
+W2_ROWS_AT = (0, 10240)
+SCALE_WINDOW_AT = 8128
+MASTERY_RING_AT = 10240
+W2_WOVEN0_AT = 18432
+W4_RAW1_AT = 22464
+FIRST_LEFT_AT = 22528
+Z_ROWS0_AT = 24576
+W2_CODES_AT = (24576, 25600)
 
 
 def tile_list_prerequisite_mastery_kernel(
@@ -49,7 +49,7 @@ def tile_list_prerequisite_mastery_kernel(
         lists = ctx.enter_context(tc.tile_pool(name="lists", bufs=1))
         keep = ctx.enter_context(tc.tile_pool(name="keep", bufs=1))
         shared = ctx.enter_context(tc.tile_pool(name="shared", bufs=1))
-        psum = ctx.enter_context(tc.psum_pool(name="psum", bufs=PSUM_BANKS))
+        psum = ctx.enter_context(tc.psum_pool(name="psum", bufs=1))
 
         def load_list(name, dram):
             tile = lists.tile([P, dram.shape[1]], U16, name=name)
@@ -58,6 +58,9 @@ def tile_list_prerequisite_mastery_kernel(
 
         def kept(name, shape, dtype, over=None):
             return keep.tile(shape, dtype, name=name, tag=over or name, align_bytes=64)
+
+        def bank(i):
+            return psum.tile([P, BANK], F32, name="bank%d" % (i % PSUM_BANKS))
 
         def placed(name, shape, dtype, offset):
             return shared.tile(shape, dtype, name=name, offset=offset, align_bytes=64)
@@ -70,33 +73,33 @@ def tile_list_prerequisite_mastery_kernel(
 
         w4_scale_rows = kept("w4_scale_rows", [P, 2, H], U8)
         nc.gpsimd.memset(w4_scale_rows[:].bitcast(I32), 0)
-        for quad in range(4):
-            nc.scalar.dma_start(
-                w4_scale_rows[32 * quad : 32 * quad + 4, :, :].bitcast(I32),
-                w4_scales[:, 4 * quad : 4 * quad + 4, :].rearrange("a s c -> s a c").bitcast(I32),
-            )
-        gain_sb = kept("gain_sb", [P, 2, 16], F32)
-        gain_view = gain.rearrange("(b q c) -> q b c", b=2, c=16)
-        for e in range(4):
-            nc.gpsimd.dma_start(gain_sb[e:P:4, :, 0:13], gain_view[:, :, e : e + 13])
 
         warm_input = kept("warm_input", [P, 1], F32)
         nc.vector.memset(warm_input[:], 0.0)
         warm = kept("warm", [P, 1], F32)
-        nc.scalar.activation(warm[:], warm_input[:], ACT.Sigmoid)
+        nc.scalar.activation(warm[:], warm_input[:], ACT.Silu)
         nc.vector.memset(scale_window[64:128, :].bitcast(I32), 0)
         nc.vector.memset(scale_window[32:64, :].bitcast(I32), 0)
         v_planes = kept("v_planes", [P, 2, S], U8)
         nc.vector.memset(v_planes[:].bitcast(I32), 0)
 
         def load_table(a):
-            words = placed("table%d" % a, [P, T], U32, TABLE_AT[a])
+            words = kept("table%d" % a, [P, T], U32)
             nc.sync.dma_start(words[:].bitcast(I32), tab_words[a].rearrange("p t i -> p (t i)").bitcast(I32))
             return words
 
+        def load_w4(b, tile):
+            columns = w4_words[:, :, H * b : H * (b + 1)]
+            nc.sync.dma_start(tile[:].bitcast(I32), columns.rearrange("a p c -> p a c").bitcast(I32))
+            return tile
+
         table = [load_table(0)]
-        w4_raw = kept("w4_raw", [P, 2, 2 * H], U8)
-        nc.sync.dma_start(w4_raw[:].bitcast(I32), w4_words.rearrange("a p c -> p a c").bitcast(I32))
+        for quad in range(4):
+            nc.sync.dma_start(
+                w4_scale_rows[32 * quad : 32 * quad + 4, :, :].bitcast(I32),
+                w4_scales[:, 4 * quad : 4 * quad + 4, :].rearrange("a s c -> s a c").bitcast(I32),
+            )
+        w4_raw = [load_w4(0, kept("w4_raw0", [P, 2, H], U8))]
         table.append(load_table(1))
 
         picked_scale_rows = kept("picked_scale_rows", [P, S], U8)
@@ -104,17 +107,28 @@ def tile_list_prerequisite_mastery_kernel(
         for a in range(2):
             for quad in range(4):
                 first_row = 16 * a + 4 * quad
-                if first_row > 0:
-                    nc.sync.dma_start(
-                        v_planes[32 * quad : 32 * quad + 4, a, :].bitcast(I32),
-                        picked_scale_rows[first_row : first_row + 4, :].bitcast(I32),
-                    )
-        nc.vector.tensor_copy(v_planes[0:32, 0, :].bitcast(I32), picked_scale_rows[0:32, :].bitcast(I32))
-
+                (nc.sync if first_row > 0 else nc.gpsimd).dma_start(
+                    v_planes[32 * quad : 32 * quad + 4, a, :].bitcast(I32),
+                    picked_scale_rows[first_row : first_row + 4, :].bitcast(I32),
+                )
+        w4_raw.append(load_w4(1, placed("w4_raw1", [P, 2, H], U8, W4_RAW1_AT)))
         pos1_sb = load_list("pos1_sb", pos1)
+
+        w2_rows = [placed("w2_rows%d" % b, [P, 4, N], F32, W2_ROWS_AT[b]) for b in range(2)]
+        w2_view = w2.rearrange("(b q t e) n -> b e q t n", b=2, t=4, e=4)
+        for b in range(2):
+            for e in range(4):
+                (nc.gpsimd, nc.sync)[b].dma_start(w2_rows[b][e:P:4, :, :], w2_view[b][e])
+        gain_runs = kept("gain_runs", [P, 2, 16], F32)
+        gain_view = gain.rearrange("(b q c) -> q b c", b=2, c=16)
+        for e in range(4):
+            nc.sync.dma_start(gain_runs[e:P:4, :, 0:13], gain_view[:, :, e : e + 13])
         pos2_sb = load_list("pos2_sb", pos2)
         pos3_sb = load_list("pos3_sb", pos3)
         pos4_sb = load_list("pos4_sb", pos4)
+        bias_sb = kept("bias_sb", [P, OUT_TILES], F32)
+        with nc.allow_non_contiguous_dma(reason="one value a partition"):
+            nc.sync.dma_start(bias_sb[:], bias.rearrange("(j p) -> p j", p=P))
 
         v_words = {}
 
@@ -124,26 +138,21 @@ def tile_list_prerequisite_mastery_kernel(
             nc.vector.tensor_copy(picked[:], table[a][:].indirect(entries))
             v_words[a, half] = picked
 
-        w4_codes, w4_planes = {}, {}
+        w4_codes = {}
 
-        def order_w4_planes(b, tile):
-            rows = w4_scale_rows[:, :, BANK * b : BANK * (b + 1)].bitcast(I32)
-            nc.vector.tensor_copy(tile[:].bitcast(I32), rows.rearrange("p a (q t) -> p a t q", t=4))
-            w4_planes[b] = tile
-
-        def order_w4_codes(b, tile):
+        def order_w4_codes(b):
+            tile = kept("w4_codes%d" % b, [P, 2, 4, 2 * P], U8)
             nc.vector.tensor_copy(
                 tile[:].bitcast(I32).rearrange("p a t (q w) -> p a t q w", w=2),
-                w4_raw[:, :, H * b : H * (b + 1)].bitcast(I32).rearrange("p a (q t w) -> p a t q w", t=4, w=2),
+                w4_raw[b][:].bitcast(I32).rearrange("p a (q t w) -> p a t q w", t=4, w=2),
             )
             w4_codes[b] = tile
 
-        order_w4_planes(0, kept("w4_planes0", [P, 2, 4, P], U8))
-        idle = psum.tile([P, BANK], F32, name="acc")
+        idle = bank(PSUM_BANKS - 1)
         for i in range(WARM_PASSES):
             nc.tensor.matmul_mx(
                 out=idle[:],
-                lhsT=w4_raw[:, 0, 2 * P * i : 2 * P * (i + 1)].bitcast(FP4X4),
+                lhsT=w4_raw[0][:, 0, 2 * P * i : 2 * P * (i + 1)].bitcast(FP4X4),
                 lhsT_scale=w4_scale_rows[:, 0, P * i : P * (i + 1)],
                 rhs=table[0][:, 0:BANK].bitcast(FP8X4),
                 rhs_scale=w4_scale_rows[:, 1, 0:BANK],
@@ -151,171 +160,168 @@ def tile_list_prerequisite_mastery_kernel(
                 stop=True,
             )
         gather_words(0, 0)
-        order_w4_codes(0, kept("w4_codes0", [P, 2, 4, 2 * P], U8))
+        w4_planes = kept("w4_planes", [P, 4, 4, P], U8)
+        nc.vector.tensor_copy(
+            w4_planes[:].bitcast(I32),
+            w4_scale_rows[:].bitcast(I32).rearrange("p a c -> p (a c)").rearrange("p (g q t) -> p g t q", g=4, t=4),
+        )
+        order_w4_codes(0)
         gather_words(0, 1)
         gather_words(1, 0)
         gather_words(1, 1)
-        order_w4_codes(1, placed("w4_codes1", [P, 2, 4, 2 * P], U8, W4_CODES1_AT))
-        order_w4_planes(1, placed("w4_planes1", [P, 2, 4, P], U8, W4_PLANES1_AT))
+        order_w4_codes(1)
 
-        w2_rows = [placed("w2_rows%d" % b, [P, 4, N], F32, W2_ROWS_AT[b]) for b in range(2)]
-        w2_view = w2.rearrange("(b q t e) n -> b e q t n", b=2, t=4, e=4)
-        for b in range(2):
-            for e in range(4):
-                (nc.gpsimd, nc.sync)[b].dma_start(w2_rows[b][e:P:4, :, :], w2_view[b][e])
-        bias_sb = placed("bias_sb", [P, OUT_TILES], F32, BIAS_AT)
-        with nc.allow_non_contiguous_dma(reason="one value a partition"):
-            nc.sync.dma_start(bias_sb[:], bias.rearrange("(j p) -> p j", p=P))
+        h = [kept("h%d" % j, [P, S], F32) for j in range(ROW_TILES)]
 
-        h = {}
-
-        def first_product(j, halves=(0, 1)):
+        def first_product(j, half, copy=nc.scalar.copy):
             b, t = divmod(j, 4)
-            if j not in h:
-                h[j] = kept("h%d" % j, [P, S], F32)
-            rows = h[j]
-            for half in halves:
-                cols = slice(BANK * half, BANK * (half + 1))
-                acc = psum.tile([P, BANK], F32, name="acc")
-                order = (0, 1) if 2 * j + half < PASS0_FIRST else (1, 0)
-                for a in order:
-                    nc.tensor.matmul_mx(
-                        out=acc[:],
-                        lhsT=w4_codes[b][:, a, t, :].bitcast(FP4X4),
-                        lhsT_scale=w4_planes[b][:, a, t, :],
-                        rhs=v_words[a, half][:].bitcast(FP8X4),
-                        rhs_scale=v_planes[:, a, cols],
-                        start=(a == order[0]),
-                        stop=(a == order[1]),
-                    )
-                nc.scalar.copy(rows[:, cols], acc[:])
+            cols = slice(BANK * half, BANK * (half + 1))
+            acc = bank(2 * j + half)
+            order = (0, 1) if 2 * j + half < PASS0_FIRST else (1, 0)
+            for a in order:
+                nc.tensor.matmul_mx(
+                    out=acc[:],
+                    lhsT=w4_codes[b][:, a, t, :].bitcast(FP4X4),
+                    lhsT_scale=w4_planes[:, 2 * a + b, t, :],
+                    rhs=v_words[a, half][:].bitcast(FP8X4),
+                    rhs_scale=v_planes[:, a, cols],
+                    start=(a == order[0]),
+                    stop=(a == order[1]),
+                )
+            copy(h[j][:, cols], acc[:])
 
-        def quantise(codes, plane, woven):
-            nc.vector.quantize_mx(out=codes.bitcast(FP8X4), scales=plane, in_=woven)
+        def quantise(name, woven, codes):
+            plane = kept(name + "_plane", [P, codes.shape[1]], U8)
+            nc.vector.quantize_mx(
+                out=codes[:].bitcast(FP8X4), scales=plane[:], in_=woven.rearrange("p m t -> p (m t)")
+            )
+            return codes, plane
 
-        w2_mx = {}
+        w2_woven, w2_mx = {}, {}
 
-        def round_w2(b, j, woven):
-            rows = w2_rows[b][:, :, P * j : P * (j + 1)]
-            nc.gpsimd.tensor_scalar(woven, rows.rearrange("p t n -> p n t"), 1.0, 0.0, ALU.mult, ALU.add)
+        def round_w2(b, woven):
+            rows = w2_rows[b][:].rearrange("p t n -> p n t")
+            nc.gpsimd.tensor_scalar(woven[:], rows, 1.0, 0.0, ALU.mult, ALU.add)
+            w2_woven[b] = woven
 
-        def quantise_w2(b, first, parts, over):
-            widths = [woven.shape[1] for woven in parts]
-            codes = kept("w2_codes%d%d" % (b, first), [P, sum(widths)], U32, over)
-            plane = kept("w2_plane%d%d" % (b, first), [P, sum(widths)], U8)
-            for i, woven in enumerate(parts):
-                cols = slice(sum(widths[:i]), sum(widths[: i + 1]))
-                quantise(codes[:, cols], plane[:, cols], woven[:].rearrange("p n t -> p (n t)"))
-            for i in range(sum(widths) // P):
-                w2_mx[b, first + i] = (codes[:, P * i : P * (i + 1)], plane[:, P * i : P * (i + 1)])
+        def quantise_w2(b, pair, codes):
+            woven = w2_woven[b][:, PAIR * pair : PAIR * (pair + 1), :]
+            w2_mx[b, pair] = quantise("w2_%d%d" % (b, pair), woven, codes)
 
-        left = {}
+        left, mastery = {}, {}
 
         def pick_left(j):
-            left[j] = kept("left%d" % j, [P, COUPLES], F32)
+            if j % LEAD == 0:
+                left[j] = placed("left%d" % j, [P, COUPLES], F32, FIRST_LEFT_AT)
+            else:
+                left[j] = kept("left%d" % j, [P, COUPLES], F32, "left%d" % (j % LEAD))
             nc.vector.tensor_copy(left[j][:], h[j][:].indirect(pos1_sb[:]))
-
-        mastery = {}
 
         def gate(j):
             b, t = divmod(j, 4)
-            nc.scalar.activation(left[j][:], left[j][:], ACT.Sigmoid)
-            mastery[j] = kept("mastery%d" % j, [P, COUPLES], F32)
-            nc.scalar.activation(mastery[j][:], left[j][:], ACT.Copy, scale=gain_sb[:, b, 4 * t : 4 * t + 1])
+            factor = gain_runs[:, b, 4 * t : 4 * t + 1]
+            nc.scalar.activation(left[j][:], left[j][:], ACT.Tanh, scale=0.5)
+            if b == 0:
+                mastery[j] = placed("mastery%d" % j, [P, COUPLES], F32, MASTERY_RING_AT)
+                nc.gpsimd.tensor_scalar(mastery[j][:], left[j][:], factor, factor, ALU.mult, ALU.add)
+            else:
+                mastery[j] = kept("mastery%d" % j, [P, COUPLES], F32)
+                nc.scalar.activation(mastery[j][:], left[j][:], ACT.Identity, bias=factor, scale=factor)
 
-        def pick_right(j, z_slot, first, width):
-            entries = pos2_sb[:, first // PER_COLUMN : (first + width) // PER_COLUMN]
-            nc.vector.tensor_tensor(z_slot, h[j][:].indirect(entries), mastery[j][:, first : first + width], ALU.mult)
+        def pick_right(j, z_slot, couples):
+            entries = pos2_sb[:, couples.start // PER_COLUMN : couples.stop // PER_COLUMN]
+            nc.vector.tensor_tensor(z_slot, h[j][:].indirect(entries), mastery[j][:, couples], ALU.mult)
 
-        def weave_z(name, rows, width, on_vector=0):
-            woven = kept(name, [P, width, 4], BF16)
-            for copy, cols in ((nc.vector.tensor_copy, slice(0, on_vector)), (nc.scalar.copy, slice(on_vector, width))):
-                if cols.start < cols.stop:
-                    copy(
-                        woven[:, cols, :].rearrange("p (c i) t -> p c t i", i=4),
-                        rows[:, :, cols].rearrange("p t (c i) -> p c t i", i=4),
-                    )
-            return woven[:].rearrange("p m t -> p (m t)")
+        def weave_z(name, rows):
+            woven = kept(name, [P, rows.shape[2], 4], BF16)
+            nc.scalar.activation(
+                woven[:].rearrange("p (c i) t -> p c t i", i=4),
+                rows[:].rearrange("p t (c i) -> p c t i", i=4),
+                ACT.Copy,
+                scale=0.5,
+            )
+            return woven
 
-        low, high, whole = slice(0, HALF), slice(HALF, COUPLES), slice(0, COUPLES)
-        z_mx = {}
+        def quantise_z(name, woven):
+            return quantise(name, woven[:], kept(name + "_codes", [P, woven.shape[1]], U32))
 
-        def quantise_z(name, woven, width):
-            codes = kept(name + "_codes", [P, width], U32)
-            plane = kept(name + "_plane", [P, width], U8)
-            quantise(codes[:], plane[:], woven)
-            z_mx[name] = (codes, plane)
+        first_product(0, 0)
+        first_product(1, 0)
+        first_product(0, 1, nc.vector.tensor_copy)
+        first_product(1, 1)
+        pick_left(0)
+        pick_left(1)
+        for j in range(2, LEAD):
+            first_product(j, 0)
+            first_product(j, 1)
+            pick_left(j)
+        round_w2(0, placed("w2_woven0", [P, N, 4], BF16, W2_WOVEN0_AT))
+        round_w2(1, kept("w2_woven1", [P, N, 4], BF16))
+
+        whole = slice(0, COUPLES)
+        z_rows0 = placed("z_rows0", [P, 4, COUPLES], F32, Z_ROWS0_AT)
+        for j in range(4):
+            gate(j)
+            pick_right(j, z_rows0[:, j, :], whole)
+            if j + LEAD < ROW_TILES:
+                first_product(j + LEAD, 0)
+                first_product(j + LEAD, 1)
+                pick_left(j + LEAD)
+
+        def piece_rows(i, over):
+            width = PIECES[i].stop - PIECES[i].start
+            return kept("z_rows1%d" % i, [P, 4, width], F32, over)
+
+        rows_a = piece_rows(0, "left3")
+        for t in range(4):
+            gate(4 + t)
+            pick_right(4 + t, rows_a[:, t, :], PIECES[0])
+        last_left = "left%d" % ((ROW_TILES - 1) % LEAD)
+        rows_b = piece_rows(1, last_left)
+        for t in range(4):
+            pick_right(4 + t, rows_b[:, t, :], PIECES[1])
+        woven0 = weave_z("z_woven0", z_rows0)
+        woven_a = weave_z("z_woven_a", rows_a)
+        woven_b = weave_z("z_woven_b", rows_b)
+        z0 = quantise_z("z0", woven0)
+        for b in range(2):
+            quantise_w2(b, 0, placed("w2_codes%d0" % b, [P, PAIR], U32, W2_CODES_AT[b]))
+        rows_c = piece_rows(2, "z_woven0")
+        for t in range(4):
+            pick_right(4 + t, rows_c[:, t, :], PIECES[2])
+        woven_c = weave_z("z_woven_c", rows_c)
+        z1 = [quantise_z("z_a", woven_a), quantise_z("z_b", woven_b)]
+        quantise_w2(0, 1, kept("w2_codes01", [P, PAIR], U32, last_left))
+        z1.append(quantise_z("z_c", woven_c))
+        quantise_w2(1, 1, kept("w2_codes11", [P, PAIR], U32, "z_woven0"))
 
         y = [kept("y%d" % j, [P, COUPLES], F32) for j in range(OUT_TILES)]
 
-        def second_product(j, couples):
-            acc = psum.tile([P, BANK], F32, name="acc")
-            passes = [(0, couples, z_mx["z0"][0][:, couples], z_mx["z0"][1][:, couples])]
-            for name, part in (("z_low", low), ("z_high", high)):
-                if couples.start <= part.start and part.stop <= couples.stop:
-                    passes.append((1, part, z_mx[name][0][:], z_mx[name][1][:]))
+        def second_product(j, pieces, acc):
+            span = slice(PIECES[pieces[0]].start, PIECES[pieces[-1]].stop)
+            first = [span] if len(pieces) != 2 else [PIECES[i] for i in pieces]
+            passes = [(0, part, z0[0][:, part], z0[1][:, part]) for part in first]
+            passes += [(1, PIECES[i], z1[i][0][:], z1[i][1][:]) for i in pieces]
+            columns = slice(P * (j % 2), P * (j % 2 + 1))
             for i, (b, part, codes, plane) in enumerate(passes):
                 nc.tensor.matmul_mx(
                     out=acc[:, part],
-                    lhsT=w2_mx[b, j][0].bitcast(FP8X4),
-                    lhsT_scale=w2_mx[b, j][1],
+                    lhsT=w2_mx[b, j // 2][0][:, columns].bitcast(FP8X4),
+                    lhsT_scale=w2_mx[b, j // 2][1][:, columns],
                     rhs=codes.bitcast(FP8X4),
                     rhs_scale=plane,
                     start=(i == 0),
                     stop=(i == len(passes) - 1),
                 )
-            nc.scalar.copy(y[j][:, couples], acc[:, couples])
+            nc.scalar.copy(y[j][:, span], acc[:, span])
 
-        z_rows0 = kept("z_rows0", [P, 4, COUPLES], F32)
-        z_rows_low = kept("z_rows_low", [P, 4, HALF], F32)
-        for half in range(2):
-            for j in range(2):
-                first_product(j, (half,))
-        pick_left(0)
-        pick_left(1)
-        for j in range(2, LEAD):
-            first_product(j)
-            pick_left(j)
-        w2_woven = [[kept("w2_woven0", [P, N, 4], BF16)], []]
-        for j in range(OUT_TILES):
-            round_w2(0, j, w2_woven[0][0][:, P * j : P * (j + 1), :])
-        for j in range(ROW_TILES):
-            b, t = divmod(j, 4)
-            gate(j)
-            if b == 0:
-                pick_right(j, z_rows0[:, t, :], 0, COUPLES)
-                if t > 0:
-                    w2_woven[1].append(kept("w2_woven1%d" % t, [P, P, 4], BF16, "mastery%d" % j))
-                    round_w2(1, t - 1, w2_woven[1][-1][:])
-            else:
-                pick_right(j, z_rows_low[:, t, :], 0, HALF)
-            if j + LEAD < ROW_TILES:
-                first_product(j + LEAD)
-                pick_left(j + LEAD)
-            elif j + 1 < ROW_TILES:
-                late = j + LEAD - ROW_TILES
-                quantise_w2(late, 0, w2_woven[late], "left%d" % j)
+        second_product(0, (0, 1), bank(0))
+        second_product(0, (2,), bank(1))
+        second_product(1, (0, 1, 2), bank(2))
+        second_product(2, (0, 1, 2), bank(0))
+        second_product(3, (0, 1, 2), bank(1))
 
-        woven0 = weave_z("z_woven0", z_rows0, COUPLES)
-        woven_low = weave_z("z_woven_low", z_rows_low, HALF)
-        quantise_z("z0", woven0, COUPLES)
-        quantise_z("z_low", woven_low, HALF)
-        z_rows_high = kept("z_rows_high", [P, 4, HALF], F32, "left%d" % (ROW_TILES - 1))
-        for t in range(4):
-            pick_right(4 + t, z_rows_high[:, t, :], HALF, HALF)
-        woven_high = weave_z("z_woven_high", z_rows_high, HALF, LAST_ON_VECTOR)
-        quantise_z("z_high", woven_high, HALF)
-        last_woven = kept("w2_woven_last", [P, P, 4], BF16, "z_woven_high")
-        nc.vector.tensor_copy(
-            last_woven[:].rearrange("p (c i) t -> p c t i", i=4),
-            w2_rows[1][:, :, N - P : N].rearrange("p t (c i) -> p c t i", i=4),
-        )
-        quantise_w2(1, OUT_TILES - 1, [last_woven], None)
-        second_product(0, low)
-        second_product(0, high)
-        for j in range(1, OUT_TILES):
-            second_product(j, whole)
-
+        result = kept("result", [P, OUT_TILES, UNITS], F32, "z_woven0")
         for j in range(OUT_TILES):
             one_couple = kept("one_couple%d" % j, [P, UNITS], F32)
             both = kept("both%d" % j, [P, UNITS], F32)
@@ -327,7 +333,6 @@ def tile_list_prerequisite_mastery_kernel(
                 nc.vector.tensor_tensor(
                     both[:, parts[i]], y[j][:].indirect(pos4_sb[:, entries[i]]), one_couple[:, parts[i]], ALU.add
                 )
-            result = kept("result%d" % j, [P, UNITS], F32)
             for part in parts if j == OUT_TILES - 1 else [slice(0, UNITS)]:
-                nc.scalar.activation(result[:, part], both[:, part], ACT.Silu, bias=bias_sb[:, j : j + 1])
-                nc.sync.dma_start(out[P * j : P * (j + 1), part], result[:, part])
+                nc.scalar.activation(result[:, j, part], both[:, part], ACT.Silu, bias=bias_sb[:, j : j + 1])
+                nc.sync.dma_start(out[P * j : P * (j + 1), part], result[:, j, part])

@@ -25,20 +25,23 @@ PER_COLUMN = 16
 ROW_TILES = H // P
 OUT_TILES = N // P
 
-LEAD = 5
+LEAD = 3
 PIECES = (slice(0, 256), slice(256, 384), slice(384, 512))
 PASS0_FIRST = 4
 WARM_PASSES = 4
-PAIR = 2 * P
 
-W2_ROWS_AT = (0, 10240)
-SCALE_WINDOW_AT = 8128
-MASTERY_RING_AT = 10240
-W2_WOVEN0_AT = 18432
-W4_RAW1_AT = 22464
-FIRST_LEFT_AT = 22528
-Z_ROWS0_AT = 24576
-W2_CODES_AT = (24576, 25600)
+W2_ROWS0_AT = 18432
+SCALE_WINDOW_AT = 26560
+TABLE1_AT = 28672
+W4_CODES1_AT = 28672
+W4_PLANES1_AT = 30720
+W2_ROWS1_AT = 36800
+Z_ROWS0_AT = 4096
+W2_CODES_AT = 4096
+Z_WOVEN0_AT = 12288
+LAST_ROWS_AT = 12288
+W2_LATE_CODES_AT = 13312
+RESULT_AT = 13312
 
 
 def tile_list_prerequisite_mastery_kernel(
@@ -73,6 +76,11 @@ def tile_list_prerequisite_mastery_kernel(
 
         w4_scale_rows = kept("w4_scale_rows", [P, 2, H], U8)
         nc.gpsimd.memset(w4_scale_rows[:].bitcast(I32), 0)
+        for quad in range(4):
+            nc.scalar.dma_start(
+                w4_scale_rows[32 * quad : 32 * quad + 4, :, :].bitcast(I32),
+                w4_scales[:, 4 * quad : 4 * quad + 4, :].rearrange("a s c -> s a c").bitcast(I32),
+            )
 
         warm_input = kept("warm_input", [P, 1], F32)
         nc.vector.memset(warm_input[:], 0.0)
@@ -80,26 +88,18 @@ def tile_list_prerequisite_mastery_kernel(
         nc.scalar.activation(warm[:], warm_input[:], ACT.Silu)
         nc.vector.memset(scale_window[64:128, :].bitcast(I32), 0)
         nc.vector.memset(scale_window[32:64, :].bitcast(I32), 0)
-        v_planes = kept("v_planes", [P, 2, S], U8)
-        nc.vector.memset(v_planes[:].bitcast(I32), 0)
+        v_planes = [kept("v_plane%d" % a, [P, S], U8) for a in range(2)]
+        for plane in v_planes:
+            nc.vector.memset(plane[:].bitcast(I32), 0)
 
         def load_table(a):
-            words = kept("table%d" % a, [P, T], U32)
+            words = placed("table1", [P, T], U32, TABLE1_AT) if a else kept("table0", [P, T], U32)
             nc.sync.dma_start(words[:].bitcast(I32), tab_words[a].rearrange("p t i -> p (t i)").bitcast(I32))
             return words
 
-        def load_w4(b, tile):
-            columns = w4_words[:, :, H * b : H * (b + 1)]
-            nc.sync.dma_start(tile[:].bitcast(I32), columns.rearrange("a p c -> p a c").bitcast(I32))
-            return tile
-
         table = [load_table(0)]
-        for quad in range(4):
-            nc.sync.dma_start(
-                w4_scale_rows[32 * quad : 32 * quad + 4, :, :].bitcast(I32),
-                w4_scales[:, 4 * quad : 4 * quad + 4, :].rearrange("a s c -> s a c").bitcast(I32),
-            )
-        w4_raw = [load_w4(0, kept("w4_raw0", [P, 2, H], U8))]
+        w4_raw = kept("w4_raw", [P, 2, 2 * H], U8)
+        nc.sync.dma_start(w4_raw[:].bitcast(I32), w4_words.rearrange("a p c -> p a c").bitcast(I32))
         table.append(load_table(1))
 
         picked_scale_rows = kept("picked_scale_rows", [P, S], U8)
@@ -107,23 +107,23 @@ def tile_list_prerequisite_mastery_kernel(
         for a in range(2):
             for quad in range(4):
                 first_row = 16 * a + 4 * quad
-                (nc.sync if first_row > 0 else nc.gpsimd).dma_start(
-                    v_planes[32 * quad : 32 * quad + 4, a, :].bitcast(I32),
+                (nc.sync if first_row < 28 else nc.gpsimd).dma_start(
+                    v_planes[a][32 * quad : 32 * quad + 4, :].bitcast(I32),
                     picked_scale_rows[first_row : first_row + 4, :].bitcast(I32),
                 )
-        w4_raw.append(load_w4(1, placed("w4_raw1", [P, 2, H], U8, W4_RAW1_AT)))
         pos1_sb = load_list("pos1_sb", pos1)
-
-        w2_rows = [placed("w2_rows%d" % b, [P, 4, N], F32, W2_ROWS_AT[b]) for b in range(2)]
-        w2_view = w2.rearrange("(b q t e) n -> b e q t n", b=2, t=4, e=4)
-        for b in range(2):
-            for e in range(4):
-                (nc.gpsimd, nc.sync)[b].dma_start(w2_rows[b][e:P:4, :, :], w2_view[b][e])
+        pos2_sb = load_list("pos2_sb", pos2)
         gain_runs = kept("gain_runs", [P, 2, 16], F32)
         gain_view = gain.rearrange("(b q c) -> q b c", b=2, c=16)
         for e in range(4):
             nc.sync.dma_start(gain_runs[e:P:4, :, 0:13], gain_view[:, :, e : e + 13])
-        pos2_sb = load_list("pos2_sb", pos2)
+
+        w2_rows = [placed("w2_rows0", [P, 4, N], F32, W2_ROWS0_AT), placed("w2_rows1", [P, 4, N], F32, W2_ROWS1_AT)]
+        w2_view = w2.rearrange("(b q t e) n -> b e q t n", b=2, t=4, e=4)
+        for e in range(4):
+            nc.gpsimd.dma_start(w2_rows[0][e:P:4, :, :], w2_view[0][e])
+        for e in range(4):
+            nc.sync.dma_start(w2_rows[1][e:P:4, :, :], w2_view[1][e])
         pos3_sb = load_list("pos3_sb", pos3)
         pos4_sb = load_list("pos4_sb", pos4)
         bias_sb = kept("bias_sb", [P, OUT_TILES], F32)
@@ -138,21 +138,26 @@ def tile_list_prerequisite_mastery_kernel(
             nc.vector.tensor_copy(picked[:], table[a][:].indirect(entries))
             v_words[a, half] = picked
 
-        w4_codes = {}
+        w4_codes, w4_planes = {}, {}
 
-        def order_w4_codes(b):
-            tile = kept("w4_codes%d" % b, [P, 2, 4, 2 * P], U8)
+        def order_w4_planes(b, tile):
+            rows = w4_scale_rows[:, :, BANK * b : BANK * (b + 1)].bitcast(I32)
+            nc.vector.tensor_copy(tile[:].bitcast(I32), rows.rearrange("p a (q t) -> p a t q", t=4))
+            w4_planes[b] = tile
+
+        def order_w4_codes(b, tile):
             nc.vector.tensor_copy(
                 tile[:].bitcast(I32).rearrange("p a t (q w) -> p a t q w", w=2),
-                w4_raw[b][:].bitcast(I32).rearrange("p a (q t w) -> p a t q w", t=4, w=2),
+                w4_raw[:, :, H * b : H * (b + 1)].bitcast(I32).rearrange("p a (q t w) -> p a t q w", t=4, w=2),
             )
             w4_codes[b] = tile
 
+        order_w4_planes(0, kept("w4_planes0", [P, 2, 4, P], U8))
         idle = bank(PSUM_BANKS - 1)
         for i in range(WARM_PASSES):
             nc.tensor.matmul_mx(
                 out=idle[:],
-                lhsT=w4_raw[0][:, 0, 2 * P * i : 2 * P * (i + 1)].bitcast(FP4X4),
+                lhsT=w4_raw[:, 0, 2 * P * i : 2 * P * (i + 1)].bitcast(FP4X4),
                 lhsT_scale=w4_scale_rows[:, 0, P * i : P * (i + 1)],
                 rhs=table[0][:, 0:BANK].bitcast(FP8X4),
                 rhs_scale=w4_scale_rows[:, 1, 0:BANK],
@@ -160,20 +165,16 @@ def tile_list_prerequisite_mastery_kernel(
                 stop=True,
             )
         gather_words(0, 0)
-        w4_planes = kept("w4_planes", [P, 4, 4, P], U8)
-        nc.vector.tensor_copy(
-            w4_planes[:].bitcast(I32),
-            w4_scale_rows[:].bitcast(I32).rearrange("p a c -> p (a c)").rearrange("p (g q t) -> p g t q", g=4, t=4),
-        )
-        order_w4_codes(0)
+        order_w4_codes(0, kept("w4_codes0", [P, 2, 4, 2 * P], U8))
         gather_words(0, 1)
         gather_words(1, 0)
         gather_words(1, 1)
-        order_w4_codes(1)
+        order_w4_codes(1, placed("w4_codes1", [P, 2, 4, 2 * P], U8, W4_CODES1_AT))
+        order_w4_planes(1, placed("w4_planes1", [P, 2, 4, P], U8, W4_PLANES1_AT))
 
         h = [kept("h%d" % j, [P, S], F32) for j in range(ROW_TILES)]
 
-        def first_product(j, half, copy=nc.scalar.copy):
+        def first_product(j, half):
             b, t = divmod(j, 4)
             cols = slice(BANK * half, BANK * (half + 1))
             acc = bank(2 * j + half)
@@ -182,118 +183,120 @@ def tile_list_prerequisite_mastery_kernel(
                 nc.tensor.matmul_mx(
                     out=acc[:],
                     lhsT=w4_codes[b][:, a, t, :].bitcast(FP4X4),
-                    lhsT_scale=w4_planes[:, 2 * a + b, t, :],
+                    lhsT_scale=w4_planes[b][:, a, t, :],
                     rhs=v_words[a, half][:].bitcast(FP8X4),
-                    rhs_scale=v_planes[:, a, cols],
+                    rhs_scale=v_planes[a][:, cols],
                     start=(a == order[0]),
                     stop=(a == order[1]),
                 )
-            copy(h[j][:, cols], acc[:])
+            nc.scalar.copy(h[j][:, cols], acc[:])
 
         def quantise(name, woven, codes):
             plane = kept(name + "_plane", [P, codes.shape[1]], U8)
             nc.vector.quantize_mx(
-                out=codes[:].bitcast(FP8X4), scales=plane[:], in_=woven.rearrange("p m t -> p (m t)")
+                out=codes.bitcast(FP8X4), scales=plane[:], in_=woven.rearrange("p m t -> p (m t)")
             )
             return codes, plane
 
         w2_woven, w2_mx = {}, {}
 
-        def round_w2(b, woven):
-            rows = w2_rows[b][:].rearrange("p t n -> p n t")
-            nc.gpsimd.tensor_scalar(woven[:], rows, 1.0, 0.0, ALU.mult, ALU.add)
-            w2_woven[b] = woven
+        def round_w2(b, j, woven):
+            rows = w2_rows[b][:, :, P * j : P * (j + 1)].rearrange("p t n -> p n t")
+            nc.gpsimd.tensor_scalar(woven, rows, 1.0, 0.0, ALU.mult, ALU.add)
+            w2_woven[b, j] = woven
 
-        def quantise_w2(b, pair, codes):
-            woven = w2_woven[b][:, PAIR * pair : PAIR * (pair + 1), :]
-            w2_mx[b, pair] = quantise("w2_%d%d" % (b, pair), woven, codes)
+        def quantise_w2(b, j, codes):
+            w2_mx[b, j] = quantise("w2_%d%d" % (b, j), w2_woven[b, j], codes)
 
         left, mastery = {}, {}
+        whole = slice(0, COUPLES)
 
         def pick_left(j):
-            if j % LEAD == 0:
-                left[j] = placed("left%d" % j, [P, COUPLES], F32, FIRST_LEFT_AT)
-            else:
-                left[j] = kept("left%d" % j, [P, COUPLES], F32, "left%d" % (j % LEAD))
+            left[j] = kept("left%d" % j, [P, COUPLES], F32)
             nc.vector.tensor_copy(left[j][:], h[j][:].indirect(pos1_sb[:]))
+
+        def squash(j):
+            nc.scalar.activation(left[j][:], left[j][:], ACT.Tanh, scale=0.5)
 
         def gate(j):
             b, t = divmod(j, 4)
             factor = gain_runs[:, b, 4 * t : 4 * t + 1]
-            nc.scalar.activation(left[j][:], left[j][:], ACT.Tanh, scale=0.5)
-            if b == 0:
-                mastery[j] = placed("mastery%d" % j, [P, COUPLES], F32, MASTERY_RING_AT)
-                nc.gpsimd.tensor_scalar(mastery[j][:], left[j][:], factor, factor, ALU.mult, ALU.add)
-            else:
-                mastery[j] = kept("mastery%d" % j, [P, COUPLES], F32)
-                nc.scalar.activation(mastery[j][:], left[j][:], ACT.Identity, bias=factor, scale=factor)
+            mastery[j] = kept("mastery%d" % j, [P, COUPLES], F32)
+            nc.scalar.activation(mastery[j][:], left[j][:], ACT.Identity, bias=factor, scale=factor)
 
         def pick_right(j, z_slot, couples):
             entries = pos2_sb[:, couples.start // PER_COLUMN : couples.stop // PER_COLUMN]
             nc.vector.tensor_tensor(z_slot, h[j][:].indirect(entries), mastery[j][:, couples], ALU.mult)
 
-        def weave_z(name, rows):
-            woven = kept(name, [P, rows.shape[2], 4], BF16)
+        def weave_z(woven, rows):
             nc.scalar.activation(
-                woven[:].rearrange("p (c i) t -> p c t i", i=4),
-                rows[:].rearrange("p t (c i) -> p c t i", i=4),
+                woven.rearrange("p (c i) t -> p c t i", i=4),
+                rows.rearrange("p t (c i) -> p c t i", i=4),
                 ACT.Copy,
                 scale=0.5,
             )
             return woven
 
         def quantise_z(name, woven):
-            return quantise(name, woven[:], kept(name + "_codes", [P, woven.shape[1]], U32))
+            return quantise(name, woven, kept(name + "_codes", [P, woven.shape[1]], U32)[:])
 
-        first_product(0, 0)
-        first_product(1, 0)
-        first_product(0, 1, nc.vector.tensor_copy)
-        first_product(1, 1)
+        for half in range(2):
+            for j in range(2):
+                first_product(j, half)
         pick_left(0)
         pick_left(1)
         for j in range(2, LEAD):
             first_product(j, 0)
             first_product(j, 1)
             pick_left(j)
-        round_w2(0, placed("w2_woven0", [P, N, 4], BF16, W2_WOVEN0_AT))
-        round_w2(1, kept("w2_woven1", [P, N, 4], BF16))
+        w2_woven0 = kept("w2_woven0", [P, N, 4], BF16, "w4_raw")
+        for j in range(OUT_TILES):
+            round_w2(0, j, w2_woven0[:, P * j : P * (j + 1), :])
 
-        whole = slice(0, COUPLES)
         z_rows0 = placed("z_rows0", [P, 4, COUPLES], F32, Z_ROWS0_AT)
-        for j in range(4):
+        woven0 = placed("z_woven0", [P, COUPLES, 4], BF16, Z_WOVEN0_AT)
+        rows_a = kept("z_rows10", [P, 4, 2 * P], F32)
+        for j in range(ROW_TILES):
+            b, t = divmod(j, 4)
+            ahead = j + LEAD
+            squash(j)
+            if ahead < ROW_TILES:
+                first_product(ahead, 0)
+            else:
+                quarter = slice(P * (ahead - ROW_TILES), P * (ahead - ROW_TILES + 1))
+                weave_z(woven0[:, quarter, :], z_rows0[:, :, quarter])
             gate(j)
-            pick_right(j, z_rows0[:, j, :], whole)
-            if j + LEAD < ROW_TILES:
-                first_product(j + LEAD, 0)
-                first_product(j + LEAD, 1)
-                pick_left(j + LEAD)
+            if b == 0:
+                pick_right(j, z_rows0[:, t, :], whole)
+                round_w2(1, t, kept("w2_woven1%d" % t, [P, P, 4], BF16, "mastery%d" % j)[:])
+            else:
+                pick_right(j, rows_a[:, t, :], PIECES[0])
+            if ahead < ROW_TILES:
+                first_product(ahead, 1)
+                pick_left(ahead)
 
-        def piece_rows(i, over):
-            width = PIECES[i].stop - PIECES[i].start
-            return kept("z_rows1%d" % i, [P, 4, width], F32, over)
-
-        rows_a = piece_rows(0, "left3")
-        for t in range(4):
-            gate(4 + t)
-            pick_right(4 + t, rows_a[:, t, :], PIECES[0])
-        last_left = "left%d" % ((ROW_TILES - 1) % LEAD)
-        rows_b = piece_rows(1, last_left)
+        spent_left = "left%d" % (ROW_TILES - 2)
+        rows_b = kept("z_rows11", [P, 4, P], F32, spent_left)
         for t in range(4):
             pick_right(4 + t, rows_b[:, t, :], PIECES[1])
-        woven0 = weave_z("z_woven0", z_rows0)
-        woven_a = weave_z("z_woven_a", rows_a)
-        woven_b = weave_z("z_woven_b", rows_b)
-        z0 = quantise_z("z0", woven0)
-        for b in range(2):
-            quantise_w2(b, 0, placed("w2_codes%d0" % b, [P, PAIR], U32, W2_CODES_AT[b]))
-        rows_c = piece_rows(2, "z_woven0")
+        weave_z(woven0[:, LEAD * P :, :], z_rows0[:, :, LEAD * P :])
+        woven_a = weave_z(kept("z_woven_a", [P, 2 * P, 4], BF16)[:], rows_a[:])
+        woven_b = weave_z(kept("z_woven_b", [P, P, 4], BF16)[:], rows_b[:])
+        z0 = quantise_z("z0", woven0[:])
+        for i, (b, j) in enumerate([(0, 0), (0, 1), (1, 0), (1, 1)]):
+            quantise_w2(b, j, placed("w2_codes%d%d" % (b, j), [P, P], U32, W2_CODES_AT + 512 * i)[:])
+        rows_c = placed("z_rows12", [P, 4, P], F32, LAST_ROWS_AT)
         for t in range(4):
             pick_right(4 + t, rows_c[:, t, :], PIECES[2])
-        woven_c = weave_z("z_woven_c", rows_c)
+        woven_c = weave_z(kept("z_woven_c", [P, P, 4], BF16)[:], rows_c[:])
         z1 = [quantise_z("z_a", woven_a), quantise_z("z_b", woven_b)]
-        quantise_w2(0, 1, kept("w2_codes01", [P, PAIR], U32, last_left))
+        middle_codes = kept("w2_middle_codes", [P, 2, P], U32, spent_left)
+        for b in range(2):
+            quantise_w2(b, 2, middle_codes[:, b, :])
         z1.append(quantise_z("z_c", woven_c))
-        quantise_w2(1, 1, kept("w2_codes11", [P, PAIR], U32, "z_woven0"))
+        late_codes = placed("w2_late_codes", [P, 2, P], U32, W2_LATE_CODES_AT)
+        for b in range(2):
+            quantise_w2(b, 3, late_codes[:, b, :])
 
         y = [kept("y%d" % j, [P, COUPLES], F32) for j in range(OUT_TILES)]
 
@@ -301,13 +304,12 @@ def tile_list_prerequisite_mastery_kernel(
             span = slice(PIECES[pieces[0]].start, PIECES[pieces[-1]].stop)
             first = [span] if len(pieces) != 2 else [PIECES[i] for i in pieces]
             passes = [(0, part, z0[0][:, part], z0[1][:, part]) for part in first]
-            passes += [(1, PIECES[i], z1[i][0][:], z1[i][1][:]) for i in pieces]
-            columns = slice(P * (j % 2), P * (j % 2 + 1))
+            passes += [(1, PIECES[i], z1[i][0], z1[i][1][:]) for i in pieces]
             for i, (b, part, codes, plane) in enumerate(passes):
                 nc.tensor.matmul_mx(
                     out=acc[:, part],
-                    lhsT=w2_mx[b, j // 2][0][:, columns].bitcast(FP8X4),
-                    lhsT_scale=w2_mx[b, j // 2][1][:, columns],
+                    lhsT=w2_mx[b, j][0].bitcast(FP8X4),
+                    lhsT_scale=w2_mx[b, j][1][:],
                     rhs=codes.bitcast(FP8X4),
                     rhs_scale=plane,
                     start=(i == 0),
@@ -321,7 +323,7 @@ def tile_list_prerequisite_mastery_kernel(
         second_product(2, (0, 1, 2), bank(0))
         second_product(3, (0, 1, 2), bank(1))
 
-        result = kept("result", [P, OUT_TILES, UNITS], F32, "z_woven0")
+        result = placed("result", [P, OUT_TILES, UNITS], F32, RESULT_AT)
         for j in range(OUT_TILES):
             one_couple = kept("one_couple%d" % j, [P, UNITS], F32)
             both = kept("both%d" % j, [P, UNITS], F32)

@@ -27,7 +27,7 @@ OUT_TILES = N // P
 
 LEAD = 3
 PIECES = (slice(0, 256), slice(256, 384), slice(384, 512))
-PASS0_FIRST = 4
+PASS0_FIRST = 2
 WARM_PASSES = 4
 
 W2_ROWS0_AT = 18432
@@ -35,6 +35,7 @@ SCALE_WINDOW_AT = 26560
 TABLE1_AT = 28672
 W4_CODES1_AT = 28672
 W4_PLANES1_AT = 30720
+W4_CODES0_AT = 31744
 W2_ROWS1_AT = 36800
 Z_ROWS0_AT = 4096
 W2_CODES_AT = 4096
@@ -76,11 +77,6 @@ def tile_list_prerequisite_mastery_kernel(
 
         w4_scale_rows = kept("w4_scale_rows", [P, 2, H], U8)
         nc.gpsimd.memset(w4_scale_rows[:].bitcast(I32), 0)
-        for quad in range(4):
-            nc.scalar.dma_start(
-                w4_scale_rows[32 * quad : 32 * quad + 4, :, :].bitcast(I32),
-                w4_scales[:, 4 * quad : 4 * quad + 4, :].rearrange("a s c -> s a c").bitcast(I32),
-            )
 
         warm_input = kept("warm_input", [P, 1], F32)
         nc.vector.memset(warm_input[:], 0.0)
@@ -97,9 +93,19 @@ def tile_list_prerequisite_mastery_kernel(
             nc.sync.dma_start(words[:].bitcast(I32), tab_words[a].rearrange("p t i -> p (t i)").bitcast(I32))
             return words
 
+        def load_w4(b):
+            tile = kept("w4_raw%d" % b, [P, 2, H], U8)
+            columns = w4_words[:, :, H * b : H * (b + 1)]
+            nc.sync.dma_start(tile[:].bitcast(I32), columns.rearrange("a p c -> p a c").bitcast(I32))
+            return tile
+
         table = [load_table(0)]
-        w4_raw = kept("w4_raw", [P, 2, 2 * H], U8)
-        nc.sync.dma_start(w4_raw[:].bitcast(I32), w4_words.rearrange("a p c -> p a c").bitcast(I32))
+        for quad in range(4):
+            nc.sync.dma_start(
+                w4_scale_rows[32 * quad : 32 * quad + 4, :, :].bitcast(I32),
+                w4_scales[:, 4 * quad : 4 * quad + 4, :].rearrange("a s c -> s a c").bitcast(I32),
+            )
+        w4_raw = [load_w4(0)]
         table.append(load_table(1))
 
         picked_scale_rows = kept("picked_scale_rows", [P, S], U8)
@@ -111,6 +117,7 @@ def tile_list_prerequisite_mastery_kernel(
                     v_planes[a][32 * quad : 32 * quad + 4, :].bitcast(I32),
                     picked_scale_rows[first_row : first_row + 4, :].bitcast(I32),
                 )
+        w4_raw.append(load_w4(1))
         pos1_sb = load_list("pos1_sb", pos1)
         pos2_sb = load_list("pos2_sb", pos2)
         gain_runs = kept("gain_runs", [P, 2, 16], F32)
@@ -145,19 +152,20 @@ def tile_list_prerequisite_mastery_kernel(
             nc.vector.tensor_copy(tile[:].bitcast(I32), rows.rearrange("p a (q t) -> p a t q", t=4))
             w4_planes[b] = tile
 
-        def order_w4_codes(b, tile):
+        def order_w4_codes(b, slots, tile):
+            words = w4_raw[b][:].bitcast(I32).rearrange("p a (q t w) -> p a t q w", t=4, w=2)
             nc.vector.tensor_copy(
-                tile[:].bitcast(I32).rearrange("p a t (q w) -> p a t q w", w=2),
-                w4_raw[:, :, H * b : H * (b + 1)].bitcast(I32).rearrange("p a (q t w) -> p a t q w", t=4, w=2),
+                tile[:].bitcast(I32).rearrange("p a t (q w) -> p a t q w", w=2), words[:, :, slots, :, :]
             )
-            w4_codes[b] = tile
+            for t in range(slots.start, slots.stop):
+                w4_codes[b, t] = tile[:, :, t - slots.start, :]
 
         order_w4_planes(0, kept("w4_planes0", [P, 2, 4, P], U8))
         idle = bank(PSUM_BANKS - 1)
         for i in range(WARM_PASSES):
             nc.tensor.matmul_mx(
                 out=idle[:],
-                lhsT=w4_raw[:, 0, 2 * P * i : 2 * P * (i + 1)].bitcast(FP4X4),
+                lhsT=w4_raw[0][:, 0, 2 * P * i : 2 * P * (i + 1)].bitcast(FP4X4),
                 lhsT_scale=w4_scale_rows[:, 0, P * i : P * (i + 1)],
                 rhs=table[0][:, 0:BANK].bitcast(FP8X4),
                 rhs_scale=w4_scale_rows[:, 1, 0:BANK],
@@ -165,12 +173,13 @@ def tile_list_prerequisite_mastery_kernel(
                 stop=True,
             )
         gather_words(0, 0)
-        order_w4_codes(0, kept("w4_codes0", [P, 2, 4, 2 * P], U8))
+        order_w4_codes(0, slice(0, 2), kept("w4_codes_first", [P, 2, 2, 2 * P], U8))
         gather_words(0, 1)
         gather_words(1, 0)
         gather_words(1, 1)
-        order_w4_codes(1, placed("w4_codes1", [P, 2, 4, 2 * P], U8, W4_CODES1_AT))
+        order_w4_codes(0, slice(2, 4), placed("w4_codes_next", [P, 2, 2, 2 * P], U8, W4_CODES0_AT))
         order_w4_planes(1, placed("w4_planes1", [P, 2, 4, P], U8, W4_PLANES1_AT))
+        order_w4_codes(1, slice(0, 4), placed("w4_codes1", [P, 2, 4, 2 * P], U8, W4_CODES1_AT))
 
         h = [kept("h%d" % j, [P, S], F32) for j in range(ROW_TILES)]
 
@@ -182,7 +191,7 @@ def tile_list_prerequisite_mastery_kernel(
             for a in order:
                 nc.tensor.matmul_mx(
                     out=acc[:],
-                    lhsT=w4_codes[b][:, a, t, :].bitcast(FP4X4),
+                    lhsT=w4_codes[b, t][:, a, :].bitcast(FP4X4),
                     lhsT_scale=w4_planes[b][:, a, t, :],
                     rhs=v_words[a, half][:].bitcast(FP8X4),
                     rhs_scale=v_planes[a][:, cols],
@@ -249,7 +258,7 @@ def tile_list_prerequisite_mastery_kernel(
             first_product(j, 0)
             first_product(j, 1)
             pick_left(j)
-        w2_woven0 = kept("w2_woven0", [P, N, 4], BF16, "w4_raw")
+        w2_woven0 = kept("w2_woven0", [P, N, 4], BF16, "w4_raw1")
         for j in range(OUT_TILES):
             round_w2(0, j, w2_woven0[:, P * j : P * (j + 1), :])
 

@@ -32,11 +32,13 @@ WARM_PASSES = 4
 
 W2_ROWS0_AT = 18432
 SCALE_WINDOW_AT = 26560
-TABLE1_AT = 28672
-W4_CODES1_AT = 28672
-W4_PLANES1_AT = 30720
-W4_CODES0_AT = 31744
-W2_ROWS1_AT = 36800
+W4_RAW1_AT = 26624
+W2_WOVEN0_AT = 28608
+TABLE1_AT = 32768
+W4_CODES1_AT = 32768
+W4_PLANES1_AT = 34816
+W4_CODES0_AT = 35840
+W2_ROWS1_AT = 40896
 Z_ROWS0_AT = 4096
 W2_CODES_AT = 4096
 Z_WOVEN0_AT = 12288
@@ -93,10 +95,9 @@ def tile_list_prerequisite_mastery_kernel(
             nc.sync.dma_start(words[:].bitcast(I32), tab_words[a].rearrange("p t i -> p (t i)").bitcast(I32))
             return words
 
-        def load_w4(b):
-            tile = kept("w4_raw%d" % b, [P, 2, H], U8)
+        def load_w4(b, tile, queue):
             columns = w4_words[:, :, H * b : H * (b + 1)]
-            nc.sync.dma_start(tile[:].bitcast(I32), columns.rearrange("a p c -> p a c").bitcast(I32))
+            queue.dma_start(tile[:].bitcast(I32), columns.rearrange("a p c -> p a c").bitcast(I32))
             return tile
 
         table = [load_table(0)]
@@ -105,7 +106,7 @@ def tile_list_prerequisite_mastery_kernel(
                 w4_scale_rows[32 * quad : 32 * quad + 4, :, :].bitcast(I32),
                 w4_scales[:, 4 * quad : 4 * quad + 4, :].rearrange("a s c -> s a c").bitcast(I32),
             )
-        w4_raw = [load_w4(0)]
+        w4_raw = [load_w4(0, kept("w4_raw0", [P, 2, H], U8), nc.sync)]
         table.append(load_table(1))
 
         picked_scale_rows = kept("picked_scale_rows", [P, S], U8)
@@ -117,7 +118,7 @@ def tile_list_prerequisite_mastery_kernel(
                     v_planes[a][32 * quad : 32 * quad + 4, :].bitcast(I32),
                     picked_scale_rows[first_row : first_row + 4, :].bitcast(I32),
                 )
-        w4_raw.append(load_w4(1))
+        w4_raw.append(load_w4(1, placed("w4_raw1", [P, 2, H], U8, W4_RAW1_AT), nc.gpsimd))
         pos1_sb = load_list("pos1_sb", pos1)
         pos2_sb = load_list("pos2_sb", pos2)
         gain_runs = kept("gain_runs", [P, 2, 16], F32)
@@ -205,7 +206,7 @@ def tile_list_prerequisite_mastery_kernel(
             nc.vector.quantize_mx(
                 out=codes.bitcast(FP8X4), scales=plane[:], in_=woven.rearrange("p m t -> p (m t)")
             )
-            return codes, plane
+            return codes, plane[:]
 
         w2_woven, w2_mx = {}, {}
 
@@ -218,7 +219,7 @@ def tile_list_prerequisite_mastery_kernel(
             w2_mx[b, j] = quantise("w2_%d%d" % (b, j), w2_woven[b, j], codes)
 
         left, mastery = {}, {}
-        whole = slice(0, COUPLES)
+        whole, late = slice(0, COUPLES), slice(PIECES[0].stop, COUPLES)
 
         def pick_left(j):
             left[j] = kept("left%d" % j, [P, COUPLES], F32)
@@ -230,12 +231,16 @@ def tile_list_prerequisite_mastery_kernel(
         def gate(j):
             b, t = divmod(j, 4)
             factor = gain_runs[:, b, 4 * t : 4 * t + 1]
-            mastery[j] = kept("mastery%d" % j, [P, COUPLES], F32)
-            nc.scalar.activation(mastery[j][:], left[j][:], ACT.Identity, bias=factor, scale=factor)
+            for part in (PIECES[0], late) if j == 4 else (whole,):
+                tile = kept("mastery%d_%d" % (j, part.start), [P, part.stop - part.start], F32)
+                nc.scalar.activation(tile[:], left[j][:, part], ACT.Identity, bias=factor, scale=factor)
+                mastery[j, part.start] = tile
 
         def pick_right(j, z_slot, couples):
             entries = pos2_sb[:, couples.start // PER_COLUMN : couples.stop // PER_COLUMN]
-            nc.vector.tensor_tensor(z_slot, h[j][:].indirect(entries), mastery[j][:, couples], ALU.mult)
+            first = late.start if (j, late.start) in mastery and couples.start >= late.start else 0
+            factors = mastery[j, first][:, couples.start - first : couples.stop - first]
+            nc.vector.tensor_tensor(z_slot, h[j][:].indirect(entries), factors, ALU.mult)
 
         def weave_z(woven, rows):
             nc.scalar.activation(
@@ -258,12 +263,13 @@ def tile_list_prerequisite_mastery_kernel(
             first_product(j, 0)
             first_product(j, 1)
             pick_left(j)
-        w2_woven0 = kept("w2_woven0", [P, N, 4], BF16, "w4_raw1")
-        for j in range(OUT_TILES):
-            round_w2(0, j, w2_woven0[:, P * j : P * (j + 1), :])
+        w2_early = placed("w2_early", [P, LEAD * P, 4], BF16, W2_WOVEN0_AT)
+        for j in range(LEAD):
+            round_w2(0, j, w2_early[:, P * j : P * (j + 1), :])
+        w2_tied = [(0, 3), (1, 0), (1, 1), (1, 2), (1, 3)]
 
         z_rows0 = placed("z_rows0", [P, 4, COUPLES], F32, Z_ROWS0_AT)
-        woven0 = placed("z_woven0", [P, COUPLES, 4], BF16, Z_WOVEN0_AT)
+        woven0_low = kept("z_woven0_low", [P, 2 * P, 4], BF16)
         rows_a = kept("z_rows10", [P, 4, 2 * P], F32)
         for j in range(ROW_TILES):
             b, t = divmod(j, 4)
@@ -271,16 +277,20 @@ def tile_list_prerequisite_mastery_kernel(
             squash(j)
             if ahead < ROW_TILES:
                 first_product(ahead, 0)
+            elif ahead == ROW_TILES:
+                first_product(ROW_TILES - 1, 1)
+                pick_left(ROW_TILES - 1)
             else:
-                quarter = slice(P * (ahead - ROW_TILES), P * (ahead - ROW_TILES + 1))
-                weave_z(woven0[:, quarter, :], z_rows0[:, :, quarter])
+                quarter = slice(P * (ahead - ROW_TILES - 1), P * (ahead - ROW_TILES))
+                weave_z(woven0_low[:, quarter, :], z_rows0[:, :, quarter])
             gate(j)
             if b == 0:
                 pick_right(j, z_rows0[:, t, :], whole)
-                round_w2(1, t, kept("w2_woven1%d" % t, [P, P, 4], BF16, "mastery%d" % j)[:])
             else:
                 pick_right(j, rows_a[:, t, :], PIECES[0])
             if ahead < ROW_TILES:
+                round_w2(*w2_tied[j], kept("w2_tied%d" % j, [P, P, 4], BF16, "mastery%d_0" % j)[:])
+            if ahead < ROW_TILES - 1:
                 first_product(ahead, 1)
                 pick_left(ahead)
 
@@ -288,37 +298,45 @@ def tile_list_prerequisite_mastery_kernel(
         rows_b = kept("z_rows11", [P, 4, P], F32, spent_left)
         for t in range(4):
             pick_right(4 + t, rows_b[:, t, :], PIECES[1])
-        weave_z(woven0[:, LEAD * P :, :], z_rows0[:, :, LEAD * P :])
+        woven0_high = placed("z_woven0_high", [P, 2 * P, 4], BF16, Z_WOVEN0_AT)
+        weave_z(woven0_high[:], z_rows0[:, :, 2 * P :])
         woven_a = weave_z(kept("z_woven_a", [P, 2 * P, 4], BF16)[:], rows_a[:])
         woven_b = weave_z(kept("z_woven_b", [P, P, 4], BF16)[:], rows_b[:])
-        z0 = quantise_z("z0", woven0[:])
-        for i, (b, j) in enumerate([(0, 0), (0, 1), (1, 0), (1, 1)]):
-            quantise_w2(b, j, placed("w2_codes%d%d" % (b, j), [P, P], U32, W2_CODES_AT + 512 * i)[:])
+        codes0 = kept("w2_codes0", [P, N], U32, "left%d" % (ROW_TILES - 3))
+        codes, plane = quantise("w2_0", w2_early[:, 0 : 2 * P, :], codes0[:, 0 : 2 * P])
+        for j in range(2):
+            w2_mx[0, j] = (codes[:, P * j : P * (j + 1)], plane[:, P * j : P * (j + 1)])
+        for j in range(2, OUT_TILES):
+            quantise_w2(0, j, codes0[:, P * j : P * (j + 1)])
+        z0 = [quantise_z("z0_low", woven0_low[:]), quantise_z("z0_high", woven0_high[:])]
+        quantise_w2(1, 0, placed("w2_codes10", [P, P], U32, W2_CODES_AT)[:])
         rows_c = placed("z_rows12", [P, 4, P], F32, LAST_ROWS_AT)
         for t in range(4):
             pick_right(4 + t, rows_c[:, t, :], PIECES[2])
         woven_c = weave_z(kept("z_woven_c", [P, P, 4], BF16)[:], rows_c[:])
         z1 = [quantise_z("z_a", woven_a), quantise_z("z_b", woven_b)]
-        middle_codes = kept("w2_middle_codes", [P, 2, P], U32, spent_left)
-        for b in range(2):
-            quantise_w2(b, 2, middle_codes[:, b, :])
+        quantise_w2(1, 1, kept("w2_codes11", [P, P], U32, spent_left)[:])
         z1.append(quantise_z("z_c", woven_c))
         late_codes = placed("w2_late_codes", [P, 2, P], U32, W2_LATE_CODES_AT)
-        for b in range(2):
-            quantise_w2(b, 3, late_codes[:, b, :])
+        for j in (2, 3):
+            quantise_w2(1, j, late_codes[:, j - 2, :])
 
         y = [kept("y%d" % j, [P, COUPLES], F32) for j in range(OUT_TILES)]
 
         def second_product(j, pieces, acc):
             span = slice(PIECES[pieces[0]].start, PIECES[pieces[-1]].stop)
-            first = [span] if len(pieces) != 2 else [PIECES[i] for i in pieces]
-            passes = [(0, part, z0[0][:, part], z0[1][:, part]) for part in first]
-            passes += [(1, PIECES[i], z1[i][0], z1[i][1][:]) for i in pieces]
+            passes = []
+            for i, (codes, plane) in enumerate(z0):
+                part = slice(max(span.start, 2 * P * i), min(span.stop, 2 * P * (i + 1)))
+                if part.start < part.stop:
+                    within = slice(part.start - 2 * P * i, part.stop - 2 * P * i)
+                    passes.append((0, part, codes[:, within], plane[:, within]))
+            passes += [(1, PIECES[i], z1[i][0], z1[i][1]) for i in pieces]
             for i, (b, part, codes, plane) in enumerate(passes):
                 nc.tensor.matmul_mx(
                     out=acc[:, part],
                     lhsT=w2_mx[b, j][0].bitcast(FP8X4),
-                    lhsT_scale=w2_mx[b, j][1][:],
+                    lhsT_scale=w2_mx[b, j][1],
                     rhs=codes.bitcast(FP8X4),
                     rhs_scale=plane,
                     start=(i == 0),
@@ -328,22 +346,37 @@ def tile_list_prerequisite_mastery_kernel(
 
         second_product(0, (0, 1), bank(0))
         second_product(0, (2,), bank(1))
-        second_product(1, (0, 1, 2), bank(2))
-        second_product(2, (0, 1, 2), bank(0))
-        second_product(3, (0, 1, 2), bank(1))
+        for j in range(1, OUT_TILES):
+            second_product(j, (0, 1, 2), bank(j + 1))
 
         result = placed("result", [P, OUT_TILES, UNITS], F32, RESULT_AT)
-        for j in range(OUT_TILES):
-            one_couple = kept("one_couple%d" % j, [P, UNITS], F32)
-            both = kept("both%d" % j, [P, UNITS], F32)
-            parts = [slice(UNITS // 2 * i, UNITS // 2 * (i + 1)) for i in range(2)]
-            entries = [slice(part.start // PER_COLUMN, part.stop // PER_COLUMN) for part in parts]
-            for i in range(2):
-                nc.vector.tensor_copy(one_couple[:, parts[i]], y[j][:].indirect(pos3_sb[:, entries[i]]))
-            for i in range(2):
-                nc.vector.tensor_tensor(
-                    both[:, parts[i]], y[j][:].indirect(pos4_sb[:, entries[i]]), one_couple[:, parts[i]], ALU.add
-                )
-            for part in parts if j == OUT_TILES - 1 else [slice(0, UNITS)]:
-                nc.scalar.activation(result[:, j, part], both[:, part], ACT.Silu, bias=bias_sb[:, j : j + 1])
-                nc.sync.dma_start(out[P * j : P * (j + 1), part], result[:, j, part])
+        one_couple = [kept("one_couple%d" % j, [P, UNITS], F32) for j in range(OUT_TILES)]
+        both = [kept("both%d" % j, [P, UNITS], F32) for j in range(OUT_TILES)]
+        all_units = slice(0, UNITS)
+        halves = [slice(0, UNITS // 2), slice(UNITS // 2, UNITS)]
+
+        def pick_first(j, part):
+            entries = pos3_sb[:, part.start // PER_COLUMN : part.stop // PER_COLUMN]
+            nc.vector.tensor_copy(one_couple[j][:, part], y[j][:].indirect(entries))
+
+        def add_second(j, part):
+            entries = pos4_sb[:, part.start // PER_COLUMN : part.stop // PER_COLUMN]
+            nc.vector.tensor_tensor(both[j][:, part], y[j][:].indirect(entries), one_couple[j][:, part], ALU.add)
+
+        def finish(j, part):
+            nc.scalar.activation(result[:, j, part], both[j][:, part], ACT.Silu, bias=bias_sb[:, j : j + 1])
+            nc.sync.dma_start(out[P * j : P * (j + 1), part], result[:, j, part])
+
+        for part in halves:
+            pick_first(0, part)
+        for part in halves:
+            add_second(0, part)
+        finish(0, all_units)
+        pick_first(1, all_units)
+        for j in range(1, OUT_TILES - 1):
+            pick_first(j + 1, all_units)
+            add_second(j, all_units)
+            finish(j, all_units)
+        for part in halves:
+            add_second(OUT_TILES - 1, part)
+            finish(OUT_TILES - 1, part)

@@ -31,14 +31,11 @@ PASS0_FIRST = 2
 WARM_PASSES = 4
 
 W2_ROWS0_AT = 18432
-SCALE_WINDOW_AT = 26560
-W4_RAW1_AT = 26624
-W2_WOVEN0_AT = 28608
-TABLE1_AT = 32768
-W4_CODES1_AT = 32768
-W4_PLANES1_AT = 34816
-W4_CODES0_AT = 35840
-W2_ROWS1_AT = 40896
+TABLE_AT = (26560, 36864)
+W4_CODES1_AT = 36864
+W4_PLANES1_AT = 38912
+W4_CODES0_AT = 39936
+W2_ROWS1_AT = 44992
 Z_ROWS0_AT = 4096
 W2_CODES_AT = 4096
 Z_WOVEN0_AT = 12288
@@ -71,7 +68,7 @@ def tile_list_prerequisite_mastery_kernel(
         def placed(name, shape, dtype, offset):
             return shared.tile(shape, dtype, name=name, offset=offset, align_bytes=64)
 
-        scale_window = placed("scale_window", [P, T], U8, SCALE_WINDOW_AT)
+        scale_window = kept("scale_window", [P, T], U8)
         nc.scalar.dma_start(
             scale_window[0:32, :].bitcast(I32), tab_scales.rearrange("a q t -> (a q) t").bitcast(I32)
         )
@@ -91,13 +88,14 @@ def tile_list_prerequisite_mastery_kernel(
             nc.vector.memset(plane[:].bitcast(I32), 0)
 
         def load_table(a):
-            words = placed("table1", [P, T], U32, TABLE1_AT) if a else kept("table0", [P, T], U32)
+            words = placed("table%d" % a, [P, T], U32, TABLE_AT[a])
             nc.sync.dma_start(words[:].bitcast(I32), tab_words[a].rearrange("p t i -> p (t i)").bitcast(I32))
             return words
 
-        def load_w4(b, tile, queue):
+        def load_w4(b):
+            tile = kept("w4_raw%d" % b, [P, 2, H], U8)
             columns = w4_words[:, :, H * b : H * (b + 1)]
-            queue.dma_start(tile[:].bitcast(I32), columns.rearrange("a p c -> p a c").bitcast(I32))
+            nc.sync.dma_start(tile[:].bitcast(I32), columns.rearrange("a p c -> p a c").bitcast(I32))
             return tile
 
         table = [load_table(0)]
@@ -106,7 +104,7 @@ def tile_list_prerequisite_mastery_kernel(
                 w4_scale_rows[32 * quad : 32 * quad + 4, :, :].bitcast(I32),
                 w4_scales[:, 4 * quad : 4 * quad + 4, :].rearrange("a s c -> s a c").bitcast(I32),
             )
-        w4_raw = [load_w4(0, kept("w4_raw0", [P, 2, H], U8), nc.sync)]
+        w4_raw = [load_w4(0)]
         table.append(load_table(1))
 
         picked_scale_rows = kept("picked_scale_rows", [P, S], U8)
@@ -118,7 +116,7 @@ def tile_list_prerequisite_mastery_kernel(
                     v_planes[a][32 * quad : 32 * quad + 4, :].bitcast(I32),
                     picked_scale_rows[first_row : first_row + 4, :].bitcast(I32),
                 )
-        w4_raw.append(load_w4(1, placed("w4_raw1", [P, 2, H], U8, W4_RAW1_AT), nc.gpsimd))
+        w4_raw.append(load_w4(1))
         pos1_sb = load_list("pos1_sb", pos1)
         pos2_sb = load_list("pos2_sb", pos2)
         gain_runs = kept("gain_runs", [P, 2, 16], F32)
@@ -219,7 +217,7 @@ def tile_list_prerequisite_mastery_kernel(
             w2_mx[b, j] = quantise("w2_%d%d" % (b, j), w2_woven[b, j], codes)
 
         left, mastery = {}, {}
-        whole, late = slice(0, COUPLES), slice(PIECES[0].stop, COUPLES)
+        whole, early, late = slice(0, COUPLES), slice(0, PIECES[1].stop), PIECES[2]
 
         def pick_left(j):
             left[j] = kept("left%d" % j, [P, COUPLES], F32)
@@ -231,14 +229,14 @@ def tile_list_prerequisite_mastery_kernel(
         def gate(j):
             b, t = divmod(j, 4)
             factor = gain_runs[:, b, 4 * t : 4 * t + 1]
-            for part in (PIECES[0], late) if j == 4 else (whole,):
+            for part in (early, late) if j == 4 else (whole,):
                 tile = kept("mastery%d_%d" % (j, part.start), [P, part.stop - part.start], F32)
                 nc.scalar.activation(tile[:], left[j][:, part], ACT.Identity, bias=factor, scale=factor)
                 mastery[j, part.start] = tile
 
         def pick_right(j, z_slot, couples):
             entries = pos2_sb[:, couples.start // PER_COLUMN : couples.stop // PER_COLUMN]
-            first = late.start if (j, late.start) in mastery and couples.start >= late.start else 0
+            first = couples.start if (j, couples.start) in mastery else 0
             factors = mastery[j, first][:, couples.start - first : couples.stop - first]
             nc.vector.tensor_tensor(z_slot, h[j][:].indirect(entries), factors, ALU.mult)
 
@@ -263,14 +261,14 @@ def tile_list_prerequisite_mastery_kernel(
             first_product(j, 0)
             first_product(j, 1)
             pick_left(j)
-        w2_early = placed("w2_early", [P, LEAD * P, 4], BF16, W2_WOVEN0_AT)
+        w2_early = kept("w2_early", [P, LEAD * P, 4], BF16, "w4_raw1")
         for j in range(LEAD):
             round_w2(0, j, w2_early[:, P * j : P * (j + 1), :])
         w2_tied = [(0, 3), (1, 0), (1, 1), (1, 2), (1, 3)]
 
         z_rows0 = placed("z_rows0", [P, 4, COUPLES], F32, Z_ROWS0_AT)
         woven0_low = kept("z_woven0_low", [P, 2 * P, 4], BF16)
-        rows_a = kept("z_rows10", [P, 4, 2 * P], F32)
+        rows_early = kept("z_rows_early", [P, 4, early.stop], F32)
         for j in range(ROW_TILES):
             b, t = divmod(j, 4)
             ahead = j + LEAD
@@ -287,21 +285,17 @@ def tile_list_prerequisite_mastery_kernel(
             if b == 0:
                 pick_right(j, z_rows0[:, t, :], whole)
             else:
-                pick_right(j, rows_a[:, t, :], PIECES[0])
+                pick_right(j, rows_early[:, t, :], early)
             if ahead < ROW_TILES:
                 round_w2(*w2_tied[j], kept("w2_tied%d" % j, [P, P, 4], BF16, "mastery%d_0" % j)[:])
             if ahead < ROW_TILES - 1:
                 first_product(ahead, 1)
                 pick_left(ahead)
 
-        spent_left = "left%d" % (ROW_TILES - 2)
-        rows_b = kept("z_rows11", [P, 4, P], F32, spent_left)
-        for t in range(4):
-            pick_right(4 + t, rows_b[:, t, :], PIECES[1])
         woven0_high = placed("z_woven0_high", [P, 2 * P, 4], BF16, Z_WOVEN0_AT)
         weave_z(woven0_high[:], z_rows0[:, :, 2 * P :])
-        woven_a = weave_z(kept("z_woven_a", [P, 2 * P, 4], BF16)[:], rows_a[:])
-        woven_b = weave_z(kept("z_woven_b", [P, P, 4], BF16)[:], rows_b[:])
+        woven_a = weave_z(kept("z_woven_a", [P, 2 * P, 4], BF16)[:], rows_early[:, :, PIECES[0]])
+        woven_b = weave_z(kept("z_woven_b", [P, P, 4], BF16)[:], rows_early[:, :, PIECES[1]])
         codes0 = kept("w2_codes0", [P, N], U32, "left%d" % (ROW_TILES - 3))
         codes, plane = quantise("w2_0", w2_early[:, 0 : 2 * P, :], codes0[:, 0 : 2 * P])
         for j in range(2):
@@ -315,7 +309,7 @@ def tile_list_prerequisite_mastery_kernel(
             pick_right(4 + t, rows_c[:, t, :], PIECES[2])
         woven_c = weave_z(kept("z_woven_c", [P, P, 4], BF16)[:], rows_c[:])
         z1 = [quantise_z("z_a", woven_a), quantise_z("z_b", woven_b)]
-        quantise_w2(1, 1, kept("w2_codes11", [P, P], U32, spent_left)[:])
+        quantise_w2(1, 1, kept("w2_codes11", [P, P], U32, "z_rows_early")[:])
         z1.append(quantise_z("z_c", woven_c))
         late_codes = placed("w2_late_codes", [P, 2, P], U32, W2_LATE_CODES_AT)
         for j in (2, 3):

@@ -31,17 +31,20 @@ PASS0_FIRST = 2
 WARM_PASSES = 4
 
 W2_ROWS0_AT = 18432
-TABLE_AT = (26560, 36864)
+SCALE_WINDOW_AT = 26560
+TABLE1_AT = 36864
 W4_CODES1_AT = 36864
 W4_PLANES1_AT = 38912
 W4_CODES0_AT = 39936
+W4_PLANES0_AT = 40960
 W2_ROWS1_AT = 44992
+MASTERY4_AT = 53184
+Z_WOVEN0_HIGH_AT = 53120
 Z_ROWS0_AT = 4096
 W2_CODES_AT = 4096
-Z_WOVEN0_AT = 12288
-LAST_ROWS_AT = 12288
-W2_LATE_CODES_AT = 13312
-RESULT_AT = 13312
+LAST_ROWS_AT = 5120
+W2_LATE_CODES_AT = 5120
+RESULT_AT = 5120
 
 
 def tile_list_prerequisite_mastery_kernel(
@@ -68,7 +71,7 @@ def tile_list_prerequisite_mastery_kernel(
         def placed(name, shape, dtype, offset):
             return shared.tile(shape, dtype, name=name, offset=offset, align_bytes=64)
 
-        scale_window = kept("scale_window", [P, T], U8)
+        scale_window = placed("scale_window", [P, T], U8, SCALE_WINDOW_AT)
         nc.scalar.dma_start(
             scale_window[0:32, :].bitcast(I32), tab_scales.rearrange("a q t -> (a q) t").bitcast(I32)
         )
@@ -88,7 +91,7 @@ def tile_list_prerequisite_mastery_kernel(
             nc.vector.memset(plane[:].bitcast(I32), 0)
 
         def load_table(a):
-            words = placed("table%d" % a, [P, T], U32, TABLE_AT[a])
+            words = placed("table1", [P, T], U32, TABLE1_AT) if a else kept("table0", [P, T], U32)
             nc.sync.dma_start(words[:].bitcast(I32), tab_words[a].rearrange("p t i -> p (t i)").bitcast(I32))
             return words
 
@@ -146,10 +149,11 @@ def tile_list_prerequisite_mastery_kernel(
 
         w4_codes, w4_planes = {}, {}
 
-        def order_w4_planes(b, tile):
-            rows = w4_scale_rows[:, :, BANK * b : BANK * (b + 1)].bitcast(I32)
-            nc.vector.tensor_copy(tile[:].bitcast(I32), rows.rearrange("p a (q t) -> p a t q", t=4))
-            w4_planes[b] = tile
+        def order_w4_planes(b, slots, tile):
+            rows = w4_scale_rows[:, :, BANK * b : BANK * (b + 1)].bitcast(I32).rearrange("p a (q t) -> p a t q", t=4)
+            nc.vector.tensor_copy(tile[:].bitcast(I32), rows[:, :, slots, :])
+            for t in range(slots.start, slots.stop):
+                w4_planes[b, t] = tile[:, :, t - slots.start, :]
 
         def order_w4_codes(b, slots, tile):
             words = w4_raw[b][:].bitcast(I32).rearrange("p a (q t w) -> p a t q w", t=4, w=2)
@@ -159,7 +163,7 @@ def tile_list_prerequisite_mastery_kernel(
             for t in range(slots.start, slots.stop):
                 w4_codes[b, t] = tile[:, :, t - slots.start, :]
 
-        order_w4_planes(0, kept("w4_planes0", [P, 2, 4, P], U8))
+        order_w4_planes(0, slice(0, 2), kept("w4_planes_first", [P, 2, 2, P], U8))
         idle = bank(PSUM_BANKS - 1)
         for i in range(WARM_PASSES):
             nc.tensor.matmul_mx(
@@ -177,7 +181,8 @@ def tile_list_prerequisite_mastery_kernel(
         gather_words(1, 0)
         gather_words(1, 1)
         order_w4_codes(0, slice(2, 4), placed("w4_codes_next", [P, 2, 2, 2 * P], U8, W4_CODES0_AT))
-        order_w4_planes(1, placed("w4_planes1", [P, 2, 4, P], U8, W4_PLANES1_AT))
+        order_w4_planes(0, slice(2, 4), placed("w4_planes_next", [P, 2, 2, P], U8, W4_PLANES0_AT))
+        order_w4_planes(1, slice(0, 4), placed("w4_planes1", [P, 2, 4, P], U8, W4_PLANES1_AT))
         order_w4_codes(1, slice(0, 4), placed("w4_codes1", [P, 2, 4, 2 * P], U8, W4_CODES1_AT))
 
         h = [kept("h%d" % j, [P, S], F32) for j in range(ROW_TILES)]
@@ -191,7 +196,7 @@ def tile_list_prerequisite_mastery_kernel(
                 nc.tensor.matmul_mx(
                     out=acc[:],
                     lhsT=w4_codes[b, t][:, a, :].bitcast(FP4X4),
-                    lhsT_scale=w4_planes[b][:, a, t, :],
+                    lhsT_scale=w4_planes[b, t][:, a, :],
                     rhs=v_words[a, half][:].bitcast(FP8X4),
                     rhs_scale=v_planes[a][:, cols],
                     start=(a == order[0]),
@@ -230,7 +235,8 @@ def tile_list_prerequisite_mastery_kernel(
             b, t = divmod(j, 4)
             factor = gain_runs[:, b, 4 * t : 4 * t + 1]
             for part in (early, late) if j == 4 else (whole,):
-                tile = kept("mastery%d_%d" % (j, part.start), [P, part.stop - part.start], F32)
+                name, shape = "mastery%d_%d" % (j, part.start), [P, part.stop - part.start]
+                tile = placed(name, shape, F32, MASTERY4_AT) if part == early else kept(name, shape, F32)
                 nc.scalar.activation(tile[:], left[j][:, part], ACT.Identity, bias=factor, scale=factor)
                 mastery[j, part.start] = tile
 
@@ -261,13 +267,20 @@ def tile_list_prerequisite_mastery_kernel(
             first_product(j, 0)
             first_product(j, 1)
             pick_left(j)
-        w2_early = kept("w2_early", [P, LEAD * P, 4], BF16, "w4_raw1")
-        for j in range(LEAD):
+        w2_early = kept("w2_early", [P, N, 4], BF16, "w4_raw1")
+        for j in range(OUT_TILES):
             round_w2(0, j, w2_early[:, P * j : P * (j + 1), :])
-        w2_tied = [(0, 3), (1, 0), (1, 1), (1, 2), (1, 3)]
 
         z_rows0 = placed("z_rows0", [P, 4, COUPLES], F32, Z_ROWS0_AT)
-        woven0_low = kept("z_woven0_low", [P, 2 * P, 4], BF16)
+        woven0 = {}
+
+        def quarter_of_pass0(i):
+            half, within = divmod(i, 2)
+            if half not in woven0:
+                shape = [P, 2 * P, 4]
+                woven0[half] = placed("z_woven0_1", shape, BF16, Z_WOVEN0_HIGH_AT) if half else kept("z_woven0_0", shape, BF16)
+            return woven0[half][:, P * within : P * (within + 1), :], z_rows0[:, :, P * i : P * (i + 1)]
+
         rows_early = kept("z_rows_early", [P, 4, early.stop], F32)
         for j in range(ROW_TILES):
             b, t = divmod(j, 4)
@@ -279,41 +292,40 @@ def tile_list_prerequisite_mastery_kernel(
                 first_product(ROW_TILES - 1, 1)
                 pick_left(ROW_TILES - 1)
             else:
-                quarter = slice(P * (ahead - ROW_TILES - 1), P * (ahead - ROW_TILES))
-                weave_z(woven0_low[:, quarter, :], z_rows0[:, :, quarter])
+                weave_z(*quarter_of_pass0(ahead - ROW_TILES - 1))
             gate(j)
             if b == 0:
                 pick_right(j, z_rows0[:, t, :], whole)
             else:
                 pick_right(j, rows_early[:, t, :], early)
-            if ahead < ROW_TILES:
-                round_w2(*w2_tied[j], kept("w2_tied%d" % j, [P, P, 4], BF16, "mastery%d_0" % j)[:])
+            if b == 0:
+                round_w2(1, t, kept("w2_tied%d" % j, [P, P, 4], BF16, "mastery%d_0" % j)[:])
+            elif t == 0:
+                woven, rows = quarter_of_pass0(3)
+                nc.gpsimd.tensor_scalar(woven, rows.rearrange("p t c -> p c t"), 0.5, 0.0, ALU.mult, ALU.add)
             if ahead < ROW_TILES - 1:
                 first_product(ahead, 1)
                 pick_left(ahead)
 
-        woven0_high = placed("z_woven0_high", [P, 2 * P, 4], BF16, Z_WOVEN0_AT)
-        weave_z(woven0_high[:], z_rows0[:, :, 2 * P :])
+        weave_z(*quarter_of_pass0(2))
         woven_a = weave_z(kept("z_woven_a", [P, 2 * P, 4], BF16)[:], rows_early[:, :, PIECES[0]])
         woven_b = weave_z(kept("z_woven_b", [P, P, 4], BF16)[:], rows_early[:, :, PIECES[1]])
-        codes0 = kept("w2_codes0", [P, N], U32, "left%d" % (ROW_TILES - 3))
-        codes, plane = quantise("w2_0", w2_early[:, 0 : 2 * P, :], codes0[:, 0 : 2 * P])
+        codes0 = kept("w2_codes0", [P, 2 * P], U32, "left%d" % (ROW_TILES - 3))
+        codes, plane = quantise("w2_0", w2_early[:, 0 : 2 * P, :], codes0[:])
         for j in range(2):
             w2_mx[0, j] = (codes[:, P * j : P * (j + 1)], plane[:, P * j : P * (j + 1)])
-        for j in range(2, OUT_TILES):
-            quantise_w2(0, j, codes0[:, P * j : P * (j + 1)])
-        z0 = [quantise_z("z0_low", woven0_low[:]), quantise_z("z0_high", woven0_high[:])]
+        z0 = [quantise_z("z0_low", woven0[0][:])]
         quantise_w2(1, 0, placed("w2_codes10", [P, P], U32, W2_CODES_AT)[:])
         rows_c = placed("z_rows12", [P, 4, P], F32, LAST_ROWS_AT)
         for t in range(4):
             pick_right(4 + t, rows_c[:, t, :], PIECES[2])
         woven_c = weave_z(kept("z_woven_c", [P, P, 4], BF16)[:], rows_c[:])
-        z1 = [quantise_z("z_a", woven_a), quantise_z("z_b", woven_b)]
-        quantise_w2(1, 1, kept("w2_codes11", [P, P], U32, "z_rows_early")[:])
-        z1.append(quantise_z("z_c", woven_c))
-        late_codes = placed("w2_late_codes", [P, 2, P], U32, W2_LATE_CODES_AT)
-        for j in (2, 3):
-            quantise_w2(1, j, late_codes[:, j - 2, :])
+        z0.append(quantise("z0_high", woven0[1][:], kept("z0_high_codes", [P, 2 * P], U32, "h4")[:]))
+        z1 = [quantise_z("z_a", woven_a), quantise_z("z_b", woven_b), quantise_z("z_c", woven_c)]
+        late_pieces = [(1, 1), (0, 2), (1, 2), (0, 3), (1, 3)]
+        late_codes = placed("w2_late_codes", [P, len(late_pieces), P], U32, W2_LATE_CODES_AT)
+        for i, (b, j) in enumerate(late_pieces):
+            quantise_w2(b, j, late_codes[:, i, :])
 
         y = [kept("y%d" % j, [P, COUPLES], F32) for j in range(OUT_TILES)]
 
@@ -361,16 +373,10 @@ def tile_list_prerequisite_mastery_kernel(
             nc.scalar.activation(result[:, j, part], both[j][:, part], ACT.Silu, bias=bias_sb[:, j : j + 1])
             nc.sync.dma_start(out[P * j : P * (j + 1), part], result[:, j, part])
 
-        for part in halves:
-            pick_first(0, part)
-        for part in halves:
-            add_second(0, part)
-        finish(0, all_units)
-        pick_first(1, all_units)
-        for j in range(1, OUT_TILES - 1):
-            pick_first(j + 1, all_units)
-            add_second(j, all_units)
-            finish(j, all_units)
-        for part in halves:
-            add_second(OUT_TILES - 1, part)
-            finish(OUT_TILES - 1, part)
+        for j in range(OUT_TILES):
+            for part in halves:
+                pick_first(j, part)
+            for part in halves:
+                add_second(j, part)
+            for part in halves if j == OUT_TILES - 1 else [all_units]:
+                finish(j, part)

@@ -25,7 +25,7 @@ PER_COLUMN = 16
 ROW_TILES = H // P
 OUT_TILES = N // P
 
-LEAD = 3
+LEAD = 4
 PIECES = (slice(0, 256), slice(256, 384), slice(384, 512))
 PASS0_FIRST = 2
 WARM_PASSES = 4
@@ -38,7 +38,7 @@ W4_PLANES1_AT = 38912
 W4_CODES0_AT = 39936
 W4_PLANES0_AT = 40960
 W2_ROWS1_AT = 44992
-MASTERY4_AT = 53184
+MASTERY3_AT = 53184
 Z_WOVEN0_HIGH_AT = 53120
 Z_ROWS0_AT = 4096
 W2_CODES_AT = 4096
@@ -222,7 +222,7 @@ def tile_list_prerequisite_mastery_kernel(
             w2_mx[b, j] = quantise("w2_%d%d" % (b, j), w2_woven[b, j], codes)
 
         left, mastery = {}, {}
-        whole, early, late = slice(0, COUPLES), slice(0, PIECES[1].stop), PIECES[2]
+        whole = slice(0, COUPLES)
 
         def pick_left(j):
             left[j] = kept("left%d" % j, [P, COUPLES], F32)
@@ -234,17 +234,13 @@ def tile_list_prerequisite_mastery_kernel(
         def gate(j):
             b, t = divmod(j, 4)
             factor = gain_runs[:, b, 4 * t : 4 * t + 1]
-            for part in (early, late) if j == 4 else (whole,):
-                name, shape = "mastery%d_%d" % (j, part.start), [P, part.stop - part.start]
-                tile = placed(name, shape, F32, MASTERY4_AT) if part == early else kept(name, shape, F32)
-                nc.scalar.activation(tile[:], left[j][:, part], ACT.Identity, bias=factor, scale=factor)
-                mastery[j, part.start] = tile
+            name, shape = "mastery%d" % j, [P, COUPLES]
+            mastery[j] = placed(name, shape, F32, MASTERY3_AT) if j == 3 else kept(name, shape, F32)
+            nc.scalar.activation(mastery[j][:], left[j][:], ACT.Identity, bias=factor, scale=factor)
 
         def pick_right(j, z_slot, couples):
             entries = pos2_sb[:, couples.start // PER_COLUMN : couples.stop // PER_COLUMN]
-            first = couples.start if (j, couples.start) in mastery else 0
-            factors = mastery[j, first][:, couples.start - first : couples.stop - first]
-            nc.vector.tensor_tensor(z_slot, h[j][:].indirect(entries), factors, ALU.mult)
+            nc.vector.tensor_tensor(z_slot, h[j][:].indirect(entries), mastery[j][:, couples], ALU.mult)
 
         def weave_z(woven, rows):
             nc.scalar.activation(
@@ -270,6 +266,7 @@ def tile_list_prerequisite_mastery_kernel(
         w2_early = kept("w2_early", [P, N, 4], BF16, "w4_raw1")
         for j in range(OUT_TILES):
             round_w2(0, j, w2_early[:, P * j : P * (j + 1), :])
+        round_w2(1, 0, kept("w2_woven10", [P, P, 4], BF16)[:])
 
         z_rows0 = placed("z_rows0", [P, 4, COUPLES], F32, Z_ROWS0_AT)
         woven0 = {}
@@ -281,36 +278,34 @@ def tile_list_prerequisite_mastery_kernel(
                 woven0[half] = placed("z_woven0_1", shape, BF16, Z_WOVEN0_HIGH_AT) if half else kept("z_woven0_0", shape, BF16)
             return woven0[half][:, P * within : P * (within + 1), :], z_rows0[:, :, P * i : P * (i + 1)]
 
-        rows_early = kept("z_rows_early", [P, 4, early.stop], F32)
-        for j in range(ROW_TILES):
-            b, t = divmod(j, 4)
-            ahead = j + LEAD
+        for j in range(4):
             squash(j)
-            if ahead < ROW_TILES:
-                first_product(ahead, 0)
-            elif ahead == ROW_TILES:
-                first_product(ROW_TILES - 1, 1)
-                pick_left(ROW_TILES - 1)
-            else:
-                weave_z(*quarter_of_pass0(ahead - ROW_TILES - 1))
+            first_product(j + LEAD, 0)
             gate(j)
-            if b == 0:
-                pick_right(j, z_rows0[:, t, :], whole)
+            pick_right(j, z_rows0[:, j, :], whole)
+            if j < 3:
+                round_w2(1, j + 1, kept("w2_tied%d" % j, [P, P, 4], BF16, "mastery%d" % j)[:])
             else:
-                pick_right(j, rows_early[:, t, :], early)
-            if b == 0:
-                round_w2(1, t, kept("w2_tied%d" % j, [P, P, 4], BF16, "mastery%d_0" % j)[:])
-            elif t == 0:
                 woven, rows = quarter_of_pass0(3)
                 nc.gpsimd.tensor_scalar(woven, rows.rearrange("p t c -> p c t"), 0.5, 0.0, ALU.mult, ALU.add)
-            if ahead < ROW_TILES - 1:
-                first_product(ahead, 1)
-                pick_left(ahead)
+            first_product(j + LEAD, 1)
+            pick_left(j + LEAD)
 
-        weave_z(*quarter_of_pass0(2))
-        woven_a = weave_z(kept("z_woven_a", [P, 2 * P, 4], BF16)[:], rows_early[:, :, PIECES[0]])
-        woven_b = weave_z(kept("z_woven_b", [P, P, 4], BF16)[:], rows_early[:, :, PIECES[1]])
-        codes0 = kept("w2_codes0", [P, 2 * P], U32, "left%d" % (ROW_TILES - 3))
+        rows_a = kept("z_rows10", [P, 4, 2 * P], F32)
+        for pair in ((4, 5), (6, 7)):
+            for j in pair:
+                squash(j)
+            for j in pair:
+                gate(j)
+                pick_right(j, rows_a[:, j - 4, :], PIECES[0])
+        rows_b = kept("z_rows11", [P, 4, P], F32, "left5")
+        for t in range(4):
+            pick_right(4 + t, rows_b[:, t, :], PIECES[1])
+        for i in range(3):
+            weave_z(*quarter_of_pass0(i))
+        woven_a = weave_z(kept("z_woven_a", [P, 2 * P, 4], BF16)[:], rows_a[:])
+        woven_b = weave_z(kept("z_woven_b", [P, P, 4], BF16)[:], rows_b[:])
+        codes0 = kept("w2_codes0", [P, 2 * P], U32, "left6")
         codes, plane = quantise("w2_0", w2_early[:, 0 : 2 * P, :], codes0[:])
         for j in range(2):
             w2_mx[0, j] = (codes[:, P * j : P * (j + 1)], plane[:, P * j : P * (j + 1)])

@@ -38,8 +38,6 @@ W4_PLANES1_AT = 38912
 W4_CODES0_AT = 39936
 W4_PLANES0_AT = 40960
 W2_ROWS1_AT = 44992
-MASTERY3_AT = 53184
-Z_WOVEN0_HIGH_AT = 53120
 Z_ROWS0_AT = 4096
 W2_CODES_AT = 4096
 LAST_ROWS_AT = 5120
@@ -234,8 +232,7 @@ def tile_list_prerequisite_mastery_kernel(
         def gate(j):
             b, t = divmod(j, 4)
             factor = gain_runs[:, b, 4 * t : 4 * t + 1]
-            name, shape = "mastery%d" % j, [P, COUPLES]
-            mastery[j] = placed(name, shape, F32, MASTERY3_AT) if j == 3 else kept(name, shape, F32)
+            mastery[j] = kept("mastery%d" % j, [P, COUPLES], F32)
             nc.scalar.activation(mastery[j][:], left[j][:], ACT.Identity, bias=factor, scale=factor)
 
         def pick_right(j, z_slot, couples):
@@ -266,28 +263,14 @@ def tile_list_prerequisite_mastery_kernel(
         w2_early = kept("w2_early", [P, N, 4], BF16, "w4_raw1")
         for j in range(OUT_TILES):
             round_w2(0, j, w2_early[:, P * j : P * (j + 1), :])
-        round_w2(1, 0, kept("w2_woven10", [P, P, 4], BF16)[:])
 
         z_rows0 = placed("z_rows0", [P, 4, COUPLES], F32, Z_ROWS0_AT)
-        woven0 = {}
-
-        def quarter_of_pass0(i):
-            half, within = divmod(i, 2)
-            if half not in woven0:
-                shape = [P, 2 * P, 4]
-                woven0[half] = placed("z_woven0_1", shape, BF16, Z_WOVEN0_HIGH_AT) if half else kept("z_woven0_0", shape, BF16)
-            return woven0[half][:, P * within : P * (within + 1), :], z_rows0[:, :, P * i : P * (i + 1)]
-
         for j in range(4):
             squash(j)
             first_product(j + LEAD, 0)
             gate(j)
             pick_right(j, z_rows0[:, j, :], whole)
-            if j < 3:
-                round_w2(1, j + 1, kept("w2_tied%d" % j, [P, P, 4], BF16, "mastery%d" % j)[:])
-            else:
-                woven, rows = quarter_of_pass0(3)
-                nc.gpsimd.tensor_scalar(woven, rows.rearrange("p t c -> p c t"), 0.5, 0.0, ALU.mult, ALU.add)
+            round_w2(1, j, kept("w2_tied%d" % j, [P, P, 4], BF16, "mastery%d" % j)[:])
             first_product(j + LEAD, 1)
             pick_left(j + LEAD)
 
@@ -301,21 +284,23 @@ def tile_list_prerequisite_mastery_kernel(
         rows_b = kept("z_rows11", [P, 4, P], F32, "left5")
         for t in range(4):
             pick_right(4 + t, rows_b[:, t, :], PIECES[1])
-        for i in range(3):
-            weave_z(*quarter_of_pass0(i))
+        woven0 = [
+            weave_z(kept("z_woven0%d" % i, [P, 2 * P, 4], BF16)[:], z_rows0[:, :, 2 * P * i : 2 * P * (i + 1)])
+            for i in range(2)
+        ]
         woven_a = weave_z(kept("z_woven_a", [P, 2 * P, 4], BF16)[:], rows_a[:])
         woven_b = weave_z(kept("z_woven_b", [P, P, 4], BF16)[:], rows_b[:])
         codes0 = kept("w2_codes0", [P, 2 * P], U32, "left6")
         codes, plane = quantise("w2_0", w2_early[:, 0 : 2 * P, :], codes0[:])
         for j in range(2):
             w2_mx[0, j] = (codes[:, P * j : P * (j + 1)], plane[:, P * j : P * (j + 1)])
-        z0 = [quantise_z("z0_low", woven0[0][:])]
+        z0 = [quantise_z("z0_low", woven0[0])]
         quantise_w2(1, 0, placed("w2_codes10", [P, P], U32, W2_CODES_AT)[:])
         rows_c = placed("z_rows12", [P, 4, P], F32, LAST_ROWS_AT)
         for t in range(4):
             pick_right(4 + t, rows_c[:, t, :], PIECES[2])
         woven_c = weave_z(kept("z_woven_c", [P, P, 4], BF16)[:], rows_c[:])
-        z0.append(quantise("z0_high", woven0[1][:], kept("z0_high_codes", [P, 2 * P], U32, "h4")[:]))
+        z0.append(quantise("z0_high", woven0[1], kept("z0_high_codes", [P, 2 * P], U32, "h4")[:]))
         z1 = [quantise_z("z_a", woven_a), quantise_z("z_b", woven_b), quantise_z("z_c", woven_c)]
         late_pieces = [(1, 1), (0, 2), (1, 2), (0, 3), (1, 3)]
         late_codes = placed("w2_late_codes", [P, len(late_pieces), P], U32, W2_LATE_CODES_AT)
@@ -366,7 +351,8 @@ def tile_list_prerequisite_mastery_kernel(
 
         def finish(j, part):
             nc.scalar.activation(result[:, j, part], both[j][:, part], ACT.Silu, bias=bias_sb[:, j : j + 1])
-            nc.sync.dma_start(out[P * j : P * (j + 1), part], result[:, j, part])
+            last = j == OUT_TILES - 1 and part.stop == UNITS
+            (nc.scalar if last else nc.sync).dma_start(out[P * j : P * (j + 1), part], result[:, j, part])
 
         for j in range(OUT_TILES):
             for part in halves:

@@ -39,7 +39,6 @@ W4_CODES0_AT = 39936
 W4_PLANES0_AT = 40960
 W2_ROWS1_AT = 44992
 Z_ROWS0_AT = 4096
-W2_CODES_AT = 4096
 LAST_ROWS_AT = 5120
 W2_LATE_CODES_AT = 5120
 RESULT_AT = 5120
@@ -113,11 +112,12 @@ def tile_list_prerequisite_mastery_kernel(
         for a in range(2):
             for quad in range(4):
                 first_row = 16 * a + 4 * quad
-                (nc.sync if first_row < 28 else nc.gpsimd).dma_start(
+                (nc.sync if first_row < 24 else nc.gpsimd).dma_start(
                     v_planes[a][32 * quad : 32 * quad + 4, :].bitcast(I32),
                     picked_scale_rows[first_row : first_row + 4, :].bitcast(I32),
                 )
-        w4_raw.append(load_w4(1))
+            if a == 0:
+                w4_raw.append(load_w4(1))
         pos1_sb = load_list("pos1_sb", pos1)
         pos2_sb = load_list("pos2_sb", pos2)
         gain_runs = kept("gain_runs", [P, 2, 16], F32)
@@ -295,12 +295,12 @@ def tile_list_prerequisite_mastery_kernel(
         for j in range(2):
             w2_mx[0, j] = (codes[:, P * j : P * (j + 1)], plane[:, P * j : P * (j + 1)])
         z0 = [quantise_z("z0_low", woven0[0])]
-        quantise_w2(1, 0, placed("w2_codes10", [P, P], U32, W2_CODES_AT)[:])
         rows_c = placed("z_rows12", [P, 4, P], F32, LAST_ROWS_AT)
         for t in range(4):
             pick_right(4 + t, rows_c[:, t, :], PIECES[2])
         woven_c = weave_z(kept("z_woven_c", [P, P, 4], BF16)[:], rows_c[:])
-        z0.append(quantise("z0_high", woven0[1], kept("z0_high_codes", [P, 2 * P], U32, "h4")[:]))
+        quantise_w2(1, 0, kept("w2_codes10", [P, P], U32, "h4")[:])
+        z0.append(quantise("z0_high", woven0[1], kept("z0_high_codes", [P, 2 * P], U32, "h5")[:]))
         z1 = [quantise_z("z_a", woven_a), quantise_z("z_b", woven_b), quantise_z("z_c", woven_c)]
         late_pieces = [(1, 1), (0, 2), (1, 2), (0, 3), (1, 3)]
         late_codes = placed("w2_late_codes", [P, len(late_pieces), P], U32, W2_LATE_CODES_AT)

@@ -38,7 +38,7 @@ W4_PLANES1_AT = 38912
 W4_CODES0_AT = 39936
 W4_PLANES0_AT = 40960
 W2_ROWS1_AT = 44992
-Z_ROWS0_AT = 4096
+LAST_LEFT_AT = 5120
 LAST_ROWS_AT = 5120
 W2_LATE_CODES_AT = 5120
 RESULT_AT = 5120
@@ -161,7 +161,6 @@ def tile_list_prerequisite_mastery_kernel(
             for t in range(slots.start, slots.stop):
                 w4_codes[b, t] = tile[:, :, t - slots.start, :]
 
-        order_w4_planes(0, slice(0, 2), kept("w4_planes_first", [P, 2, 2, P], U8))
         idle = bank(PSUM_BANKS - 1)
         for i in range(WARM_PASSES):
             nc.tensor.matmul_mx(
@@ -174,6 +173,7 @@ def tile_list_prerequisite_mastery_kernel(
                 stop=True,
             )
         gather_words(0, 0)
+        order_w4_planes(0, slice(0, 2), kept("w4_planes_first", [P, 2, 2, P], U8))
         order_w4_codes(0, slice(0, 2), kept("w4_codes_first", [P, 2, 2, 2 * P], U8))
         gather_words(0, 1)
         gather_words(1, 0)
@@ -223,7 +223,8 @@ def tile_list_prerequisite_mastery_kernel(
         whole = slice(0, COUPLES)
 
         def pick_left(j):
-            left[j] = kept("left%d" % j, [P, COUPLES], F32)
+            name, shape = "left%d" % j, [P, COUPLES]
+            left[j] = placed(name, shape, F32, LAST_LEFT_AT) if j == ROW_TILES - 1 else kept(name, shape, F32)
             nc.vector.tensor_copy(left[j][:], h[j][:].indirect(pos1_sb[:]))
 
         def squash(j):
@@ -264,7 +265,7 @@ def tile_list_prerequisite_mastery_kernel(
         for j in range(OUT_TILES):
             round_w2(0, j, w2_early[:, P * j : P * (j + 1), :])
 
-        z_rows0 = placed("z_rows0", [P, 4, COUPLES], F32, Z_ROWS0_AT)
+        z_rows0 = kept("z_rows0", [P, 4, COUPLES], F32)
         for j in range(4):
             squash(j)
             first_product(j + LEAD, 0)
@@ -300,8 +301,9 @@ def tile_list_prerequisite_mastery_kernel(
             pick_right(4 + t, rows_c[:, t, :], PIECES[2])
         woven_c = weave_z(kept("z_woven_c", [P, P, 4], BF16)[:], rows_c[:])
         quantise_w2(1, 0, kept("w2_codes10", [P, P], U32, "h4")[:])
-        z0.append(quantise("z0_high", woven0[1], kept("z0_high_codes", [P, 2 * P], U32, "h5")[:]))
-        z1 = [quantise_z("z_a", woven_a), quantise_z("z_b", woven_b), quantise_z("z_c", woven_c)]
+        z1 = [quantise("z_a", woven_a, kept("z_a_codes", [P, 2 * P], U32, "h5")[:])]
+        z0.append(quantise("z0_high", woven0[1], kept("z0_high_codes", [P, 2 * P], U32, "h6")[:]))
+        z1 += [quantise_z("z_b", woven_b), quantise_z("z_c", woven_c)]
         late_pieces = [(1, 1), (0, 2), (1, 2), (0, 3), (1, 3)]
         late_codes = placed("w2_late_codes", [P, len(late_pieces), P], U32, W2_LATE_CODES_AT)
         for i, (b, j) in enumerate(late_pieces):
@@ -330,8 +332,8 @@ def tile_list_prerequisite_mastery_kernel(
                 )
             nc.scalar.copy(y[j][:, span], acc[:, span])
 
-        second_product(0, (0, 1), bank(0))
-        second_product(0, (2,), bank(1))
+        second_product(0, (0,), bank(0))
+        second_product(0, (1, 2), bank(1))
         for j in range(1, OUT_TILES):
             second_product(j, (0, 1, 2), bank(j + 1))
 

@@ -92,8 +92,8 @@ def tile_list_prerequisite_mastery_kernel(
             nc.sync.dma_start(words[:].bitcast(I32), tab_words[a].rearrange("p t i -> p (t i)").bitcast(I32))
             return words
 
-        def load_w4(b):
-            tile = kept("w4_raw%d" % b, [P, 2, H], U8)
+        def load_w4(name, b):
+            tile = kept(name, [P, 2, H], U8)
             columns = w4_words[:, :, H * b : H * (b + 1)]
             nc.sync.dma_start(tile[:].bitcast(I32), columns.rearrange("a p c -> p a c").bitcast(I32))
             return tile
@@ -104,20 +104,23 @@ def tile_list_prerequisite_mastery_kernel(
                 w4_scale_rows[32 * quad : 32 * quad + 4, :, :].bitcast(I32),
                 w4_scales[:, 4 * quad : 4 * quad + 4, :].rearrange("a s c -> s a c").bitcast(I32),
             )
-        w4_raw = [load_w4(0)]
+        w4_low = load_w4("w4_raw0", 0)
         table.append(load_table(1))
 
         picked_scale_rows = kept("picked_scale_rows", [P, S], U8)
         nc.vector.tensor_copy(picked_scale_rows[:], scale_window[:].indirect(offs_sb[:]))
-        for a in range(2):
-            for quad in range(4):
-                first_row = 16 * a + 4 * quad
-                (nc.sync if first_row < 24 else nc.gpsimd).dma_start(
-                    v_planes[a][32 * quad : 32 * quad + 4, :].bitcast(I32),
-                    picked_scale_rows[first_row : first_row + 4, :].bitcast(I32),
-                )
-            if a == 0:
-                w4_raw.append(load_w4(1))
+        def move_scale_rows(a, quad, queue):
+            first_row = 16 * a + 4 * quad
+            queue.dma_start(
+                v_planes[a][32 * quad : 32 * quad + 4, :].bitcast(I32),
+                picked_scale_rows[first_row : first_row + 4, :].bitcast(I32),
+            )
+
+        for quad in range(1, 4):
+            move_scale_rows(0, quad, nc.sync)
+        w4_high = load_w4("w4_raw1", 1)
+        for quad in range(4):
+            move_scale_rows(1, quad, nc.sync if quad < 3 else nc.gpsimd)
         pos1_sb = load_list("pos1_sb", pos1)
         pos2_sb = load_list("pos2_sb", pos2)
         gain_runs = kept("gain_runs", [P, 2, 16], F32)
@@ -139,68 +142,75 @@ def tile_list_prerequisite_mastery_kernel(
 
         v_words = {}
 
-        def gather_words(a, half):
+        def gather_words(a, half, cuts=1):
             picked = kept("v_words%d%d" % (a, half), [P, BANK], U32)
-            entries = offs_sb[:, BANK // PER_COLUMN * half : BANK // PER_COLUMN * (half + 1)]
-            nc.vector.tensor_copy(picked[:], table[a][:].indirect(entries))
+            width = BANK // cuts
+            for i in range(cuts):
+                first = BANK * half + width * i
+                entries = offs_sb[:, first // PER_COLUMN : (first + width) // PER_COLUMN]
+                nc.vector.tensor_copy(picked[:, width * i : width * (i + 1)], table[a][:].indirect(entries))
             v_words[a, half] = picked
 
-        w4_codes, w4_planes = {}, {}
+        w4_planes = kept("w4_planes", [P, 4, 4, P], U8)
+        nc.scalar.copy(
+            w4_planes[:].bitcast(U32).rearrange("p g t q -> p g q t"),
+            w4_scale_rows[:].bitcast(U32).rearrange("p a (b q t) -> p (a b) q t", b=2, t=4),
+        )
+        w4_codes = {}
 
-        def order_w4_planes(b, slots, tile):
-            rows = w4_scale_rows[:, :, BANK * b : BANK * (b + 1)].bitcast(I32).rearrange("p a (q t) -> p a t q", t=4)
-            nc.vector.tensor_copy(tile[:].bitcast(I32), rows[:, :, slots, :])
-            for t in range(slots.start, slots.stop):
-                w4_planes[b, t] = tile[:, :, t - slots.start, :]
+        def order_w4_low():
+            tile = kept("w4_codes0", [P, 2, 4, 2 * P], U8)
+            words = w4_low[:].bitcast(U32).rearrange("p a (q t w) -> p a t q w", t=4, w=2)
+            nc.scalar.copy(tile[:].bitcast(U32).rearrange("p a t (q w) -> p a t q w", w=2), words)
+            for a in range(2):
+                w4_codes[0, a] = tile[:, a, :, :]
 
-        def order_w4_codes(b, slots, tile):
-            words = w4_raw[b][:].bitcast(I32).rearrange("p a (q t w) -> p a t q w", t=4, w=2)
-            nc.vector.tensor_copy(
-                tile[:].bitcast(I32).rearrange("p a t (q w) -> p a t q w", w=2), words[:, :, slots, :, :]
-            )
-            for t in range(slots.start, slots.stop):
-                w4_codes[b, t] = tile[:, :, t - slots.start, :]
+        def order_w4_high():
+            tile = placed("w4_codes1", [P, 2, 4, 2 * P], U8, W4_CODES1_AT)
+            words = w4_high[:].bitcast(I32).rearrange("p a (q t w) -> p a t q w", t=4, w=2)
+            nc.vector.tensor_copy(tile[:].bitcast(I32).rearrange("p a t (q w) -> p a t q w", w=2), words)
+            for a in range(2):
+                w4_codes[1, a] = tile[:, a, :, :]
 
         idle = bank(PSUM_BANKS - 1)
         for i in range(WARM_PASSES):
             nc.tensor.matmul_mx(
                 out=idle[:],
-                lhsT=w4_raw[0][:, 0, 2 * P * i : 2 * P * (i + 1)].bitcast(FP4X4),
+                lhsT=w4_low[:, 0, 2 * P * i : 2 * P * (i + 1)].bitcast(FP4X4),
                 lhsT_scale=w4_scale_rows[:, 0, P * i : P * (i + 1)],
                 rhs=table[0][:, 0:BANK].bitcast(FP8X4),
                 rhs_scale=w4_scale_rows[:, 1, 0:BANK],
                 start=True,
                 stop=True,
             )
+        order_w4_low()
         gather_words(0, 0)
-        order_w4_planes(0, slice(0, 2), kept("w4_planes_first", [P, 2, 2, P], U8))
-        order_w4_codes(0, slice(0, 2), kept("w4_codes_first", [P, 2, 2, 2 * P], U8))
         gather_words(0, 1)
+        nc.vector.tensor_copy(v_planes[0][0:32, :].bitcast(I32), picked_scale_rows[0:32, :].bitcast(I32))
         gather_words(1, 0)
-        gather_words(1, 1)
-        order_w4_codes(0, slice(2, 4), placed("w4_codes_next", [P, 2, 2, 2 * P], U8, W4_CODES0_AT))
-        order_w4_planes(0, slice(2, 4), placed("w4_planes_next", [P, 2, 2, P], U8, W4_PLANES0_AT))
-        order_w4_planes(1, slice(0, 4), placed("w4_planes1", [P, 2, 4, P], U8, W4_PLANES1_AT))
-        order_w4_codes(1, slice(0, 4), placed("w4_codes1", [P, 2, 4, 2 * P], U8, W4_CODES1_AT))
+        gather_words(1, 1, cuts=2)
+        order_w4_high()
 
         h = [kept("h%d" % j, [P, S], F32) for j in range(ROW_TILES)]
+        banks_used = []
 
-        def first_product(j, half):
+        def first_product(j, half, part=slice(0, BANK)):
             b, t = divmod(j, 4)
-            cols = slice(BANK * half, BANK * (half + 1))
-            acc = bank(2 * j + half)
+            cols = slice(BANK * half + part.start, BANK * half + part.stop)
+            acc = bank(len(banks_used))
+            banks_used.append(acc)
             order = (0, 1) if 2 * j + half < PASS0_FIRST else (1, 0)
             for a in order:
                 nc.tensor.matmul_mx(
-                    out=acc[:],
-                    lhsT=w4_codes[b, t][:, a, :].bitcast(FP4X4),
-                    lhsT_scale=w4_planes[b, t][:, a, :],
-                    rhs=v_words[a, half][:].bitcast(FP8X4),
+                    out=acc[:, part],
+                    lhsT=w4_codes[b, a][:, t, :].bitcast(FP4X4),
+                    lhsT_scale=w4_planes[:, 2 * a + b, t, :],
+                    rhs=v_words[a, half][:, part].bitcast(FP8X4),
                     rhs_scale=v_planes[a][:, cols],
                     start=(a == order[0]),
                     stop=(a == order[1]),
                 )
-            nc.scalar.copy(h[j][:, cols], acc[:])
+            nc.scalar.copy(h[j][:, cols], acc[:, part])
 
         def quantise(name, woven, codes):
             plane = kept(name + "_plane", [P, codes.shape[1]], U8)
@@ -252,9 +262,11 @@ def tile_list_prerequisite_mastery_kernel(
         def quantise_z(name, woven):
             return quantise(name, woven, kept(name + "_codes", [P, woven.shape[1]], U32)[:])
 
-        for half in range(2):
-            for j in range(2):
-                first_product(j, half)
+        first_product(0, 0)
+        first_product(0, 1, slice(0, BANK // 2))
+        first_product(0, 1, slice(BANK // 2, BANK))
+        first_product(1, 0)
+        first_product(1, 1)
         pick_left(0)
         pick_left(1)
         for j in range(2, LEAD):

@@ -140,16 +140,11 @@ def tile_list_prerequisite_mastery_kernel(
         with nc.allow_non_contiguous_dma(reason="one value a partition"):
             nc.sync.dma_start(bias_sb[:], bias.rearrange("(j p) -> p j", p=P))
 
-        v_words = {}
+        v_words = [kept("v_words%d" % a, [P, S], U32) for a in range(2)]
 
-        def gather_words(a, half, cuts=1):
-            picked = kept("v_words%d%d" % (a, half), [P, BANK], U32)
-            width = BANK // cuts
-            for i in range(cuts):
-                first = BANK * half + width * i
-                entries = offs_sb[:, first // PER_COLUMN : (first + width) // PER_COLUMN]
-                nc.vector.tensor_copy(picked[:, width * i : width * (i + 1)], table[a][:].indirect(entries))
-            v_words[a, half] = picked
+        def gather_words(a, cols):
+            entries = offs_sb[:, cols.start // PER_COLUMN : cols.stop // PER_COLUMN]
+            nc.vector.tensor_copy(v_words[a][:, cols], table[a][:].indirect(entries))
 
         w4_planes = kept("w4_planes", [P, 4, 4, P], U8)
         nc.scalar.copy(
@@ -184,11 +179,10 @@ def tile_list_prerequisite_mastery_kernel(
                 stop=True,
             )
         order_w4_low()
-        gather_words(0, 0)
-        gather_words(0, 1)
+        gather_words(0, slice(0, S))
         nc.vector.tensor_copy(v_planes[0][0:32, :].bitcast(I32), picked_scale_rows[0:32, :].bitcast(I32))
-        gather_words(1, 0)
-        gather_words(1, 1, cuts=2)
+        for cols in (slice(0, 512), slice(512, 768), slice(768, S)):
+            gather_words(1, cols)
         order_w4_high()
 
         h = [kept("h%d" % j, [P, S], F32) for j in range(ROW_TILES)]
@@ -205,7 +199,7 @@ def tile_list_prerequisite_mastery_kernel(
                     out=acc[:, part],
                     lhsT=w4_codes[b, a][:, t, :].bitcast(FP4X4),
                     lhsT_scale=w4_planes[:, 2 * a + b, t, :],
-                    rhs=v_words[a, half][:, part].bitcast(FP8X4),
+                    rhs=v_words[a][:, cols].bitcast(FP8X4),
                     rhs_scale=v_planes[a][:, cols],
                     start=(a == order[0]),
                     stop=(a == order[1]),
@@ -287,22 +281,20 @@ def tile_list_prerequisite_mastery_kernel(
             first_product(j + LEAD, 1)
             pick_left(j + LEAD)
 
-        rows_a = kept("z_rows10", [P, 4, 2 * P], F32)
+        rows_ab = kept("z_rows10", [P, 4, 3 * P], F32)
         for pair in ((4, 5), (6, 7)):
             for j in pair:
                 squash(j)
             for j in pair:
                 gate(j)
-                pick_right(j, rows_a[:, j - 4, :], PIECES[0])
-        rows_b = kept("z_rows11", [P, 4, P], F32, "left5")
-        for t in range(4):
-            pick_right(4 + t, rows_b[:, t, :], PIECES[1])
+                for part in PIECES[0:2] if j == ROW_TILES - 1 else [slice(0, 3 * P)]:
+                    pick_right(j, rows_ab[:, j - 4, part], part)
         woven0 = [
             weave_z(kept("z_woven0%d" % i, [P, 2 * P, 4], BF16)[:], z_rows0[:, :, 2 * P * i : 2 * P * (i + 1)])
             for i in range(2)
         ]
-        woven_a = weave_z(kept("z_woven_a", [P, 2 * P, 4], BF16)[:], rows_a[:])
-        woven_b = weave_z(kept("z_woven_b", [P, P, 4], BF16)[:], rows_b[:])
+        woven_a = weave_z(kept("z_woven_a", [P, 2 * P, 4], BF16)[:], rows_ab[:, :, PIECES[0]])
+        woven_b = weave_z(kept("z_woven_b", [P, P, 4], BF16)[:], rows_ab[:, :, PIECES[1]])
         codes0 = kept("w2_codes0", [P, 2 * P], U32, "left6")
         codes, plane = quantise("w2_0", w2_early[:, 0 : 2 * P, :], codes0[:])
         for j in range(2):
@@ -351,9 +343,10 @@ def tile_list_prerequisite_mastery_kernel(
 
         result = placed("result", [P, OUT_TILES, UNITS], F32, RESULT_AT)
         one_couple = [kept("one_couple%d" % j, [P, UNITS], F32) for j in range(OUT_TILES)]
-        both = [kept("both%d" % j, [P, UNITS], F32) for j in range(OUT_TILES)]
+        both_first = kept("both_first", [P, UNITS], F32)
+        both_rest = kept("both_rest", [P, OUT_TILES - 1, UNITS], F32, "both_first")
+        both = [both_first[:]] + [both_rest[:, j, :] for j in range(OUT_TILES - 1)]
         all_units = slice(0, UNITS)
-        halves = [slice(0, UNITS // 2), slice(UNITS // 2, UNITS)]
 
         def pick_first(j, part):
             entries = pos3_sb[:, part.start // PER_COLUMN : part.stop // PER_COLUMN]
@@ -368,10 +361,17 @@ def tile_list_prerequisite_mastery_kernel(
             last = j == OUT_TILES - 1 and part.stop == UNITS
             (nc.scalar if last else nc.sync).dma_start(out[P * j : P * (j + 1), part], result[:, j, part])
 
-        for j in range(OUT_TILES):
-            for part in halves:
-                pick_first(j, part)
-            for part in halves:
-                add_second(j, part)
-            for part in halves if j == OUT_TILES - 1 else [all_units]:
-                finish(j, part)
+        halves = [slice(0, UNITS // 2), slice(UNITS // 2, UNITS)]
+        for part in halves:
+            pick_first(0, part)
+        for part in halves:
+            add_second(0, part)
+        finish(0, all_units)
+        for j in range(1, OUT_TILES):
+            pick_first(j, all_units)
+        for j in (1, 2):
+            add_second(j, all_units)
+            finish(j, all_units)
+        for part in halves:
+            add_second(OUT_TILES - 1, part)
+            finish(OUT_TILES - 1, part)

@@ -38,6 +38,7 @@ W4_PLANES1_AT = 38912
 W4_CODES0_AT = 39936
 W4_PLANES0_AT = 40960
 W2_ROWS1_AT = 44992
+W4_THIRD_AT = 28544
 LAST_LEFT_AT = 5120
 LAST_ROWS_AT = 5120
 W2_LATE_CODES_AT = 5120
@@ -92,10 +93,8 @@ def tile_list_prerequisite_mastery_kernel(
             nc.sync.dma_start(words[:].bitcast(I32), tab_words[a].rearrange("p t i -> p (t i)").bitcast(I32))
             return words
 
-        def load_w4(name, b):
-            tile = kept(name, [P, 2, H], U8)
-            columns = w4_words[:, :, H * b : H * (b + 1)]
-            nc.sync.dma_start(tile[:].bitcast(I32), columns.rearrange("a p c -> p a c").bitcast(I32))
+        def load_w4(tile, a, first, last, queue):
+            queue.dma_start(tile[:].bitcast(I32), w4_words[a][:, H * first : H * last].bitcast(I32))
             return tile
 
         table = [load_table(0)]
@@ -104,11 +103,14 @@ def tile_list_prerequisite_mastery_kernel(
                 w4_scale_rows[32 * quad : 32 * quad + 4, :, :].bitcast(I32),
                 w4_scales[:, 4 * quad : 4 * quad + 4, :].rearrange("a s c -> s a c").bitcast(I32),
             )
-        w4_low = load_w4("w4_raw0", 0)
+        w4_first = load_w4(kept("w4_raw00", [P, H], U8), 0, 0, 1, nc.sync)
         table.append(load_table(1))
 
         picked_scale_rows = kept("picked_scale_rows", [P, S], U8)
-        nc.vector.tensor_copy(picked_scale_rows[:], scale_window[:].indirect(offs_sb[:]))
+        list_parts = [slice(0, 768), slice(768, S)]
+        for part in list_parts:
+            entries = offs_sb[:, part.start // PER_COLUMN : part.stop // PER_COLUMN]
+            nc.vector.tensor_copy(picked_scale_rows[:, part], scale_window[:].indirect(entries))
         def move_scale_rows(a, quad, queue):
             first_row = 16 * a + 4 * quad
             queue.dma_start(
@@ -118,9 +120,10 @@ def tile_list_prerequisite_mastery_kernel(
 
         for quad in range(1, 4):
             move_scale_rows(0, quad, nc.sync)
-        w4_high = load_w4("w4_raw1", 1)
+        w4_second = load_w4(kept("w4_raw1", [P, 2 * H], U8), 1, 0, 2, nc.sync)
         for quad in range(4):
             move_scale_rows(1, quad, nc.sync if quad < 3 else nc.gpsimd)
+        w4_third = load_w4(placed("w4_raw01", [P, H], U8, W4_THIRD_AT), 0, 1, 2, nc.gpsimd)
         pos1_sb = load_list("pos1_sb", pos1)
         pos2_sb = load_list("pos2_sb", pos2)
         gain_runs = kept("gain_runs", [P, 2, 16], F32)
@@ -153,37 +156,32 @@ def tile_list_prerequisite_mastery_kernel(
         )
         w4_codes = {}
 
-        def order_w4_low():
-            tile = kept("w4_codes0", [P, 2, 4, 2 * P], U8)
-            words = w4_low[:].bitcast(U32).rearrange("p a (q t w) -> p a t q w", t=4, w=2)
-            nc.scalar.copy(tile[:].bitcast(U32).rearrange("p a t (q w) -> p a t q w", w=2), words)
-            for a in range(2):
-                w4_codes[0, a] = tile[:, a, :, :]
-
-        def order_w4_high():
-            tile = placed("w4_codes1", [P, 2, 4, 2 * P], U8, W4_CODES1_AT)
-            words = w4_high[:].bitcast(I32).rearrange("p a (q t w) -> p a t q w", t=4, w=2)
-            nc.vector.tensor_copy(tile[:].bitcast(I32).rearrange("p a t (q w) -> p a t q w", w=2), words)
-            for a in range(2):
-                w4_codes[1, a] = tile[:, a, :, :]
+        def order_w4_codes(b, a, copy, raw, tile):
+            words = raw.bitcast(U32).rearrange("p (q t w) -> p t q w", t=4, w=2)
+            copy(tile[:].bitcast(U32).rearrange("p t (q w) -> p t q w", w=2), words)
+            w4_codes[b, a] = tile[:]
 
         idle = bank(PSUM_BANKS - 1)
         for i in range(WARM_PASSES):
             nc.tensor.matmul_mx(
                 out=idle[:],
-                lhsT=w4_low[:, 0, 2 * P * i : 2 * P * (i + 1)].bitcast(FP4X4),
+                lhsT=w4_first[:, 2 * P * i : 2 * P * (i + 1)].bitcast(FP4X4),
                 lhsT_scale=w4_scale_rows[:, 0, P * i : P * (i + 1)],
                 rhs=table[0][:, 0:BANK].bitcast(FP8X4),
                 rhs_scale=w4_scale_rows[:, 1, 0:BANK],
                 start=True,
                 stop=True,
             )
-        order_w4_low()
+        shape = [P, 4, 2 * P]
+        order_w4_codes(0, 0, nc.scalar.copy, w4_first[:], kept("w4_codes00", shape, U8))
+        order_w4_codes(0, 1, nc.scalar.copy, w4_second[:, 0:H], kept("w4_codes01", shape, U8))
         gather_words(0, slice(0, S))
-        nc.vector.tensor_copy(v_planes[0][0:32, :].bitcast(I32), picked_scale_rows[0:32, :].bitcast(I32))
+        for part in list_parts:
+            nc.vector.tensor_copy(v_planes[0][0:32, part].bitcast(I32), picked_scale_rows[0:32, part].bitcast(I32))
         for cols in (slice(0, 512), slice(512, 768), slice(768, S)):
             gather_words(1, cols)
-        order_w4_high()
+        order_w4_codes(1, 1, nc.vector.tensor_copy, w4_second[:, H : 2 * H], placed("w4_codes11", shape, U8, W4_CODES1_AT))
+        order_w4_codes(1, 0, nc.vector.tensor_copy, w4_third[:], placed("w4_codes10", shape, U8, W4_PLANES1_AT))
 
         h = [kept("h%d" % j, [P, S], F32) for j in range(ROW_TILES)]
         banks_used = []
@@ -215,10 +213,9 @@ def tile_list_prerequisite_mastery_kernel(
 
         w2_woven, w2_mx = {}, {}
 
-        def round_w2(b, j, woven):
-            rows = w2_rows[b][:, :, P * j : P * (j + 1)].rearrange("p t n -> p n t")
+        def round_w2(b, cols, woven):
+            rows = w2_rows[b][:, :, cols].rearrange("p t n -> p n t")
             nc.gpsimd.tensor_scalar(woven, rows, 1.0, 0.0, ALU.mult, ALU.add)
-            w2_woven[b, j] = woven
 
         def quantise_w2(b, j, codes):
             w2_mx[b, j] = quantise("w2_%d%d" % (b, j), w2_woven[b, j], codes)
@@ -267,9 +264,10 @@ def tile_list_prerequisite_mastery_kernel(
             first_product(j, 0)
             first_product(j, 1)
             pick_left(j)
-        w2_early = kept("w2_early", [P, N, 4], BF16, "w4_raw1")
-        for j in range(OUT_TILES):
-            round_w2(0, j, w2_early[:, P * j : P * (j + 1), :])
+        w2_early = placed("w2_early", [P, N, 4], BF16, W4_THIRD_AT)
+        round_w2(0, slice(0, N), w2_early[:])
+        for j in (2, 3):
+            w2_woven[0, j] = w2_early[:, P * j : P * (j + 1), :]
 
         z_rows0 = kept("z_rows0", [P, 4, COUPLES], F32)
         for j in range(4):
@@ -277,7 +275,8 @@ def tile_list_prerequisite_mastery_kernel(
             first_product(j + LEAD, 0)
             gate(j)
             pick_right(j, z_rows0[:, j, :], whole)
-            round_w2(1, j, kept("w2_tied%d" % j, [P, P, 4], BF16, "mastery%d" % j)[:])
+            w2_woven[1, j] = kept("w2_tied%d" % j, [P, P, 4], BF16, "mastery%d" % j)[:]
+            round_w2(1, slice(P * j, P * (j + 1)), w2_woven[1, j])
             first_product(j + LEAD, 1)
             pick_left(j + LEAD)
 

@@ -24,25 +24,13 @@ PSUM_BANKS = 8
 PER_COLUMN = 16
 ROW_TILES = H // P
 OUT_TILES = N // P
+HALF = H // 2
 
-LEAD = 4
 PIECES = (slice(0, 256), slice(256, 384), slice(384, 512))
-PASS0_FIRST = 2
 WARM_PASSES = 4
-
-W2_ROWS0_AT = 18432
-SCALE_WINDOW_AT = 26560
-TABLE1_AT = 36864
-W4_CODES1_AT = 36864
-W4_PLANES1_AT = 38912
-W4_CODES0_AT = 39936
-W4_PLANES0_AT = 40960
-W2_ROWS1_AT = 44992
-W4_THIRD_AT = 28544
-LAST_LEFT_AT = 5120
-LAST_ROWS_AT = 5120
-W2_LATE_CODES_AT = 5120
-RESULT_AT = 5120
+QUADRANTS = (0, 2, 1, 3)
+LOWER, UPPER = slice(0, 512), slice(512, 1024)
+THIRD, FOURTH = slice(512, 768), slice(768, 1024)
 
 
 def tile_list_prerequisite_mastery_kernel(
@@ -52,7 +40,6 @@ def tile_list_prerequisite_mastery_kernel(
     with ExitStack() as ctx:
         lists = ctx.enter_context(tc.tile_pool(name="lists", bufs=1))
         keep = ctx.enter_context(tc.tile_pool(name="keep", bufs=1))
-        shared = ctx.enter_context(tc.tile_pool(name="shared", bufs=1))
         psum = ctx.enter_context(tc.psum_pool(name="psum", bufs=1))
 
         def load_list(name, dram):
@@ -66,17 +53,18 @@ def tile_list_prerequisite_mastery_kernel(
         def bank(i):
             return psum.tile([P, BANK], F32, name="bank%d" % (i % PSUM_BANKS))
 
-        def placed(name, shape, dtype, offset):
-            return shared.tile(shape, dtype, name=name, offset=offset, align_bytes=64)
+        def entries(tile, part):
+            return tile[:, part.start // PER_COLUMN : part.stop // PER_COLUMN]
 
-        scale_window = placed("scale_window", [P, T], U8, SCALE_WINDOW_AT)
+        scale_window = kept("scale_window", [P, T], U8)
         nc.scalar.dma_start(
             scale_window[0:32, :].bitcast(I32), tab_scales.rearrange("a q t -> (a q) t").bitcast(I32)
         )
         offs_sb = load_list("offs_sb", offs)
 
-        w4_scale_rows = kept("w4_scale_rows", [P, 2, H], U8)
-        nc.gpsimd.memset(w4_scale_rows[:].bitcast(I32), 0)
+        w4_scale_rows = [kept("w4_scale_rows%d" % b, [P, 2, HALF], U8) for b in range(2)]
+        for rows in w4_scale_rows:
+            nc.gpsimd.memset(rows[:].bitcast(I32), 0)
 
         warm_input = kept("warm_input", [P, 1], F32)
         nc.vector.memset(warm_input[:], 0.0)
@@ -89,28 +77,37 @@ def tile_list_prerequisite_mastery_kernel(
             nc.vector.memset(plane[:].bitcast(I32), 0)
 
         def load_table(a):
-            words = placed("table1", [P, T], U32, TABLE1_AT) if a else kept("table0", [P, T], U32)
+            words = kept("table%d" % a, [P, T], U32)
             nc.sync.dma_start(words[:].bitcast(I32), tab_words[a].rearrange("p t i -> p (t i)").bitcast(I32))
             return words
 
-        def load_w4(tile, a, first, last, queue):
-            queue.dma_start(tile[:].bitcast(I32), w4_words[a][:, H * first : H * last].bitcast(I32))
-            return tile
+        def load_w4_scales(b):
+            for quad in QUADRANTS:
+                nc.sync.dma_start(
+                    w4_scale_rows[b][32 * quad : 32 * quad + 4, :, :].bitcast(I32),
+                    w4_scales[:, 4 * quad : 4 * quad + 4, HALF * b : HALF * (b + 1)]
+                    .rearrange("a s c -> s a c")
+                    .bitcast(I32),
+                )
+
+        def load_w4_lower(a):
+            raw = kept("w4_raw%d" % a, [P, H], U8)
+            nc.sync.dma_start(raw[:].bitcast(I32), w4_words[a][:, 0:H].bitcast(I32))
+            return raw
 
         table = [load_table(0)]
-        for quad in range(4):
-            nc.sync.dma_start(
-                w4_scale_rows[32 * quad : 32 * quad + 4, :, :].bitcast(I32),
-                w4_scales[:, 4 * quad : 4 * quad + 4, :].rearrange("a s c -> s a c").bitcast(I32),
-            )
-        w4_first = load_w4(kept("w4_raw00", [P, H], U8), 0, 0, 1, nc.sync)
+        load_w4_scales(0)
+        w4_lower = [load_w4_lower(0)]
+        pos1_sb = load_list("pos1_sb", pos1)
         table.append(load_table(1))
 
         picked_scale_rows = kept("picked_scale_rows", [P, S], U8)
         list_parts = [slice(0, 768), slice(768, S)]
         for part in list_parts:
-            entries = offs_sb[:, part.start // PER_COLUMN : part.stop // PER_COLUMN]
-            nc.vector.tensor_copy(picked_scale_rows[:, part], scale_window[:].indirect(entries))
+            nc.vector.tensor_copy(picked_scale_rows[:, part], scale_window[:].indirect(entries(offs_sb, part)))
+        for part in list_parts:
+            nc.vector.tensor_copy(v_planes[0][0:32, part].bitcast(I32), picked_scale_rows[0:32, part].bitcast(I32))
+
         def move_scale_rows(a, quad, queue):
             first_row = 16 * a + 4 * quad
             queue.dma_start(
@@ -118,91 +115,104 @@ def tile_list_prerequisite_mastery_kernel(
                 picked_scale_rows[first_row : first_row + 4, :].bitcast(I32),
             )
 
-        for quad in range(1, 4):
+        for quad in QUADRANTS[1:]:
             move_scale_rows(0, quad, nc.sync)
-        w4_second = load_w4(kept("w4_raw1", [P, 2 * H], U8), 1, 0, 2, nc.sync)
-        for quad in range(4):
+        w4_lower.append(load_w4_lower(1))
+        for quad in QUADRANTS:
             move_scale_rows(1, quad, nc.sync if quad < 3 else nc.gpsimd)
-        w4_third = load_w4(placed("w4_raw01", [P, H], U8, W4_THIRD_AT), 0, 1, 2, nc.gpsimd)
-        pos1_sb = load_list("pos1_sb", pos1)
-        pos2_sb = load_list("pos2_sb", pos2)
+        w4_upper = kept("w4_upper", [P, 2, H], U8, "scale_window")
+        nc.gpsimd.dma_start(w4_upper[:].bitcast(I32), w4_words[:, :, H : 2 * H].rearrange("a p c -> p a c").bitcast(I32))
         gain_runs = kept("gain_runs", [P, 2, 16], F32)
         gain_view = gain.rearrange("(b q c) -> q b c", b=2, c=16)
         for e in range(4):
             nc.sync.dma_start(gain_runs[e:P:4, :, 0:13], gain_view[:, :, e : e + 13])
+        load_w4_scales(1)
 
-        w2_rows = [placed("w2_rows0", [P, 4, N], F32, W2_ROWS0_AT), placed("w2_rows1", [P, 4, N], F32, W2_ROWS1_AT)]
-        w2_view = w2.rearrange("(b q t e) n -> b e q t n", b=2, t=4, e=4)
-        for e in range(4):
-            nc.gpsimd.dma_start(w2_rows[0][e:P:4, :, :], w2_view[0][e])
-        for e in range(4):
-            nc.sync.dma_start(w2_rows[1][e:P:4, :, :], w2_view[1][e])
+        w2_view = w2.rearrange("(b q t e) n -> b t q e n", b=2, t=4, e=4)
+
+        w2_rows = [kept("w2_rows%d" % b, [P, 4, N], F32) for b in range(2)]
+
+        def load_w2(b):
+            for t in range(4):
+                nc.sync.dma_start(w2_rows[b][:, t, :], w2_view[b][t])
+
+        load_w2(0)
+        pos2_sb = load_list("pos2_sb", pos2)
+        load_w2(1)
         pos3_sb = load_list("pos3_sb", pos3)
         pos4_sb = load_list("pos4_sb", pos4)
         bias_sb = kept("bias_sb", [P, OUT_TILES], F32)
         with nc.allow_non_contiguous_dma(reason="one value a partition"):
             nc.sync.dma_start(bias_sb[:], bias.rearrange("(j p) -> p j", p=P))
 
-        v_words = [kept("v_words%d" % a, [P, S], U32) for a in range(2)]
+        w4_planes = [kept("w4_planes%d" % b, [P, 2, 4, P], U8) for b in range(2)]
 
-        def gather_words(a, cols):
-            entries = offs_sb[:, cols.start // PER_COLUMN : cols.stop // PER_COLUMN]
-            nc.vector.tensor_copy(v_words[a][:, cols], table[a][:].indirect(entries))
+        def order_w4_scales(b, copy):
+            copy(
+                w4_planes[b][:].bitcast(U32).rearrange("p a t q -> p a q t"),
+                w4_scale_rows[b][:].bitcast(U32).rearrange("p a (q t) -> p a q t", t=4),
+            )
 
-        w4_planes = kept("w4_planes", [P, 4, 4, P], U8)
-        nc.scalar.copy(
-            w4_planes[:].bitcast(U32).rearrange("p g t q -> p g q t"),
-            w4_scale_rows[:].bitcast(U32).rearrange("p a (b q t) -> p (a b) q t", b=2, t=4),
-        )
-        w4_codes = {}
-
-        def order_w4_codes(b, a, copy, raw, tile):
-            words = raw.bitcast(U32).rearrange("p (q t w) -> p t q w", t=4, w=2)
-            copy(tile[:].bitcast(U32).rearrange("p t (q w) -> p t q w", w=2), words)
-            w4_codes[b, a] = tile[:]
+        order_w4_scales(0, nc.scalar.copy)
 
         idle = bank(PSUM_BANKS - 1)
         for i in range(WARM_PASSES):
             nc.tensor.matmul_mx(
                 out=idle[:],
-                lhsT=w4_first[:, 2 * P * i : 2 * P * (i + 1)].bitcast(FP4X4),
-                lhsT_scale=w4_scale_rows[:, 0, P * i : P * (i + 1)],
+                lhsT=w4_lower[0][:, 2 * P * i : 2 * P * (i + 1)].bitcast(FP4X4),
+                lhsT_scale=w4_scale_rows[0][:, 0, P * i : P * (i + 1)],
                 rhs=table[0][:, 0:BANK].bitcast(FP8X4),
-                rhs_scale=w4_scale_rows[:, 1, 0:BANK],
+                rhs_scale=w4_scale_rows[0][:, 1, :],
                 start=True,
                 stop=True,
             )
-        shape = [P, 4, 2 * P]
-        order_w4_codes(0, 0, nc.scalar.copy, w4_first[:], kept("w4_codes00", shape, U8))
-        order_w4_codes(0, 1, nc.scalar.copy, w4_second[:, 0:H], kept("w4_codes01", shape, U8))
-        gather_words(0, slice(0, S))
-        for part in list_parts:
-            nc.vector.tensor_copy(v_planes[0][0:32, part].bitcast(I32), picked_scale_rows[0:32, part].bitcast(I32))
-        for cols in (slice(0, 512), slice(512, 768), slice(768, S)):
-            gather_words(1, cols)
-        order_w4_codes(1, 1, nc.vector.tensor_copy, w4_second[:, H : 2 * H], placed("w4_codes11", shape, U8, W4_CODES1_AT))
-        order_w4_codes(1, 0, nc.vector.tensor_copy, w4_third[:], placed("w4_codes10", shape, U8, W4_PLANES1_AT))
+        w4_codes = {}
+        for a in range(2):
+            codes = kept("w4_codes0%d" % a, [P, 4, 2 * P], U8)
+            nc.scalar.copy(
+                codes[:].bitcast(U32).rearrange("p t (q w) -> p t q w", w=2),
+                w4_lower[a][:].bitcast(U32).rearrange("p (q t w) -> p t q w", t=4, w=2),
+            )
+            w4_codes[0, a] = codes[:]
+
+        v_words = [kept("v_words%d" % a, [P, S], U32) for a in range(2)]
+        nc.vector.tensor_copy(v_words[0][:], table[0][:].indirect(offs_sb[:]))
+        for cols in (LOWER, THIRD, FOURTH):
+            nc.vector.tensor_copy(v_words[1][:, cols], table[1][:].indirect(entries(offs_sb, cols)))
+        upper_codes = kept("w4_codes1", [P, 2, 4, 2 * P], U8, "table1")
+        nc.vector.tensor_copy(
+            upper_codes[:].bitcast(U32).rearrange("p a t (q w) -> p a t q w", w=2),
+            w4_upper[:].bitcast(U32).rearrange("p a (q t w) -> p a t q w", t=4, w=2),
+        )
+        for a in range(2):
+            w4_codes[1, a] = upper_codes[:, a, :, :]
+        order_w4_scales(1, nc.gpsimd.tensor_copy)
 
         h = [kept("h%d" % j, [P, S], F32) for j in range(ROW_TILES)]
-        banks_used = []
+        sums = {}
 
-        def first_product(j, half, part=slice(0, BANK)):
+        def multiply(j, cols, a):
             b, t = divmod(j, 4)
-            cols = slice(BANK * half + part.start, BANK * half + part.stop)
-            acc = bank(len(banks_used))
-            banks_used.append(acc)
-            order = (0, 1) if 2 * j + half < PASS0_FIRST else (1, 0)
-            for a in order:
-                nc.tensor.matmul_mx(
-                    out=acc[:, part],
-                    lhsT=w4_codes[b, a][:, t, :].bitcast(FP4X4),
-                    lhsT_scale=w4_planes[:, 2 * a + b, t, :],
-                    rhs=v_words[a][:, cols].bitcast(FP8X4),
-                    rhs_scale=v_planes[a][:, cols],
-                    start=(a == order[0]),
-                    stop=(a == order[1]),
-                )
-            nc.scalar.copy(h[j][:, cols], acc[:, part])
+            opens = (j, cols.start) not in sums
+            if opens:
+                sums[j, cols.start] = bank(len(sums))[:, 0 : cols.stop - cols.start]
+            nc.tensor.matmul_mx(
+                out=sums[j, cols.start],
+                lhsT=w4_codes[b, a][:, t, :].bitcast(FP4X4),
+                lhsT_scale=w4_planes[b][:, a, t, :],
+                rhs=v_words[a][:, cols].bitcast(FP8X4),
+                rhs_scale=v_planes[a][:, cols],
+                start=opens,
+                stop=not opens,
+            )
+
+        def empty(j, cols, copy=nc.scalar.copy):
+            copy(h[j][:, cols], sums[j, cols.start])
+
+        def first_product(j, cols):
+            multiply(j, cols, 1)
+            multiply(j, cols, 0)
+            empty(j, cols)
 
         def quantise(name, woven, codes):
             plane = kept(name + "_plane", [P, codes.shape[1]], U8)
@@ -213,9 +223,8 @@ def tile_list_prerequisite_mastery_kernel(
 
         w2_woven, w2_mx = {}, {}
 
-        def round_w2(b, cols, woven):
-            rows = w2_rows[b][:, :, cols].rearrange("p t n -> p n t")
-            nc.gpsimd.tensor_scalar(woven, rows, 1.0, 0.0, ALU.mult, ALU.add)
+        def round_w2(rows, woven):
+            nc.gpsimd.tensor_scalar(woven, rows.rearrange("p t n -> p n t"), 1.0, 0.0, ALU.mult, ALU.add)
 
         def quantise_w2(b, j, codes):
             w2_mx[b, j] = quantise("w2_%d%d" % (b, j), w2_woven[b, j], codes)
@@ -224,22 +233,20 @@ def tile_list_prerequisite_mastery_kernel(
         whole = slice(0, COUPLES)
 
         def pick_left(j):
-            name, shape = "left%d" % j, [P, COUPLES]
-            left[j] = placed(name, shape, F32, LAST_LEFT_AT) if j == ROW_TILES - 1 else kept(name, shape, F32)
+            left[j] = kept("left%d" % j, [P, COUPLES], F32, "scale_window" if j == 0 else None)
             nc.vector.tensor_copy(left[j][:], h[j][:].indirect(pos1_sb[:]))
 
         def squash(j):
-            nc.scalar.activation(left[j][:], left[j][:], ACT.Tanh, scale=0.5)
+            nc.scalar.activation(squashed[:, j, :], left[j][:], ACT.Tanh, scale=0.5)
 
         def gate(j):
             b, t = divmod(j, 4)
             factor = gain_runs[:, b, 4 * t : 4 * t + 1]
             mastery[j] = kept("mastery%d" % j, [P, COUPLES], F32)
-            nc.scalar.activation(mastery[j][:], left[j][:], ACT.Identity, bias=factor, scale=factor)
+            nc.scalar.activation(mastery[j][:], squashed[:, j, :], ACT.Identity, bias=factor, scale=factor)
 
         def pick_right(j, z_slot, couples):
-            entries = pos2_sb[:, couples.start // PER_COLUMN : couples.stop // PER_COLUMN]
-            nc.vector.tensor_tensor(z_slot, h[j][:].indirect(entries), mastery[j][:, couples], ALU.mult)
+            nc.vector.tensor_tensor(z_slot, h[j][:].indirect(entries(pos2_sb, couples)), mastery[j][:, couples], ALU.mult)
 
         def weave_z(woven, rows):
             nc.scalar.activation(
@@ -253,39 +260,47 @@ def tile_list_prerequisite_mastery_kernel(
         def quantise_z(name, woven):
             return quantise(name, woven, kept(name + "_codes", [P, woven.shape[1]], U32)[:])
 
-        first_product(0, 0)
-        first_product(0, 1, slice(0, BANK // 2))
-        first_product(0, 1, slice(BANK // 2, BANK))
-        first_product(1, 0)
-        first_product(1, 1)
+        early = [(0, LOWER), (0, THIRD), (0, FOURTH), (1, LOWER), (1, UPPER)]
+        for j, cols in early:
+            multiply(j, cols, 0)
+        multiply(0, LOWER, 1)
+        empty(0, LOWER)
+        multiply(1, LOWER, 1)
+        multiply(0, THIRD, 1)
+        empty(0, THIRD)
+        empty(1, LOWER)
+        multiply(2, LOWER, 1)
+        multiply(0, FOURTH, 1)
+        empty(0, FOURTH, nc.vector.tensor_copy)
         pick_left(0)
+        multiply(1, UPPER, 1)
+        empty(1, UPPER)
         pick_left(1)
-        for j in range(2, LEAD):
-            first_product(j, 0)
-            first_product(j, 1)
+        multiply(2, LOWER, 0)
+        empty(2, LOWER)
+        first_product(2, UPPER)
+        pick_left(2)
+        for j in range(3, ROW_TILES):
+            first_product(j, LOWER)
+            first_product(j, UPPER)
             pick_left(j)
-        w2_early = placed("w2_early", [P, N, 4], BF16, W4_THIRD_AT)
-        round_w2(0, slice(0, N), w2_early[:])
-        for j in (2, 3):
-            w2_woven[0, j] = w2_early[:, P * j : P * (j + 1), :]
+        w2_rounded = [kept("w2_rounded%d" % b, [P, N, 4], BF16) for b in range(2)]
+        for b in range(2):
+            round_w2(w2_rows[b][:], w2_rounded[b][:])
+            for j in range(OUT_TILES):
+                w2_woven[b, j] = w2_rounded[b][:, P * j : P * (j + 1), :]
 
         z_rows0 = kept("z_rows0", [P, 4, COUPLES], F32)
-        for j in range(4):
-            squash(j)
-            first_product(j + LEAD, 0)
-            gate(j)
-            pick_right(j, z_rows0[:, j, :], whole)
-            w2_woven[1, j] = kept("w2_tied%d" % j, [P, P, 4], BF16, "mastery%d" % j)[:]
-            round_w2(1, slice(P * j, P * (j + 1)), w2_woven[1, j])
-            first_product(j + LEAD, 1)
-            pick_left(j + LEAD)
-
         rows_ab = kept("z_rows10", [P, 4, 3 * P], F32)
-        for pair in ((4, 5), (6, 7)):
-            for j in pair:
-                squash(j)
-            for j in pair:
-                gate(j)
+        squashed = kept("squashed", [P, ROW_TILES, COUPLES], F32, "table1")
+        squash(0)
+        for j in range(ROW_TILES):
+            if j + 1 < ROW_TILES:
+                squash(j + 1)
+            gate(j)
+            if j < 4:
+                pick_right(j, z_rows0[:, j, :], whole)
+            else:
                 for part in PIECES[0:2] if j == ROW_TILES - 1 else [slice(0, 3 * P)]:
                     pick_right(j, rows_ab[:, j - 4, part], part)
         woven0 = [
@@ -294,12 +309,12 @@ def tile_list_prerequisite_mastery_kernel(
         ]
         woven_a = weave_z(kept("z_woven_a", [P, 2 * P, 4], BF16)[:], rows_ab[:, :, PIECES[0]])
         woven_b = weave_z(kept("z_woven_b", [P, P, 4], BF16)[:], rows_ab[:, :, PIECES[1]])
-        codes0 = kept("w2_codes0", [P, 2 * P], U32, "left6")
-        codes, plane = quantise("w2_0", w2_early[:, 0 : 2 * P, :], codes0[:])
+        codes0 = kept("w2_codes0", [P, 2 * P], U32, "left7")
+        codes, plane = quantise("w2_0", w2_rounded[0][:, 0 : 2 * P, :], codes0[:])
         for j in range(2):
             w2_mx[0, j] = (codes[:, P * j : P * (j + 1)], plane[:, P * j : P * (j + 1)])
         z0 = [quantise_z("z0_low", woven0[0])]
-        rows_c = placed("z_rows12", [P, 4, P], F32, LAST_ROWS_AT)
+        rows_c = kept("z_rows12", [P, 4, P], F32, "table1")
         for t in range(4):
             pick_right(4 + t, rows_c[:, t, :], PIECES[2])
         woven_c = weave_z(kept("z_woven_c", [P, P, 4], BF16)[:], rows_c[:])
@@ -308,7 +323,7 @@ def tile_list_prerequisite_mastery_kernel(
         z0.append(quantise("z0_high", woven0[1], kept("z0_high_codes", [P, 2 * P], U32, "h6")[:]))
         z1 += [quantise_z("z_b", woven_b), quantise_z("z_c", woven_c)]
         late_pieces = [(1, 1), (0, 2), (1, 2), (0, 3), (1, 3)]
-        late_codes = placed("w2_late_codes", [P, len(late_pieces), P], U32, W2_LATE_CODES_AT)
+        late_codes = kept("w2_late_codes", [P, len(late_pieces), P], U32, "table1")
         for i, (b, j) in enumerate(late_pieces):
             quantise_w2(b, j, late_codes[:, i, :])
 
@@ -335,12 +350,12 @@ def tile_list_prerequisite_mastery_kernel(
                 )
             nc.scalar.copy(y[j][:, span], acc[:, span])
 
-        second_product(0, (0,), bank(0))
-        second_product(0, (1, 2), bank(1))
+        second_product(0, (0,), bank(1))
+        second_product(0, (1, 2), bank(2))
         for j in range(1, OUT_TILES):
-            second_product(j, (0, 1, 2), bank(j + 1))
+            second_product(j, (0, 1, 2), bank(j + 2))
 
-        result = placed("result", [P, OUT_TILES, UNITS], F32, RESULT_AT)
+        result = kept("result", [P, OUT_TILES, UNITS], F32, "table1")
         one_couple = [kept("one_couple%d" % j, [P, UNITS], F32) for j in range(OUT_TILES)]
         both_first = kept("both_first", [P, UNITS], F32)
         both_rest = kept("both_rest", [P, OUT_TILES - 1, UNITS], F32, "both_first")
@@ -348,12 +363,12 @@ def tile_list_prerequisite_mastery_kernel(
         all_units = slice(0, UNITS)
 
         def pick_first(j, part):
-            entries = pos3_sb[:, part.start // PER_COLUMN : part.stop // PER_COLUMN]
-            nc.vector.tensor_copy(one_couple[j][:, part], y[j][:].indirect(entries))
+            nc.vector.tensor_copy(one_couple[j][:, part], y[j][:].indirect(entries(pos3_sb, part)))
 
         def add_second(j, part):
-            entries = pos4_sb[:, part.start // PER_COLUMN : part.stop // PER_COLUMN]
-            nc.vector.tensor_tensor(both[j][:, part], y[j][:].indirect(entries), one_couple[j][:, part], ALU.add)
+            nc.vector.tensor_tensor(
+                both[j][:, part], y[j][:].indirect(entries(pos4_sb, part)), one_couple[j][:, part], ALU.add
+            )
 
         def finish(j, part):
             nc.scalar.activation(result[:, j, part], both[j][:, part], ACT.Silu, bias=bias_sb[:, j : j + 1])

@@ -82,12 +82,10 @@ def tile_list_prerequisite_mastery_kernel(
             return words
 
         def load_w4_scales(b):
-            for quad in QUADRANTS:
+            for s in range(4):
                 nc.sync.dma_start(
-                    w4_scale_rows[b][32 * quad : 32 * quad + 4, :, :].bitcast(I32),
-                    w4_scales[:, 4 * quad : 4 * quad + 4, HALF * b : HALF * (b + 1)]
-                    .rearrange("a s c -> s a c")
-                    .bitcast(I32),
+                    w4_scale_rows[b][s:P:32, :, :].bitcast(I32),
+                    w4_scales[:, s:16:4, HALF * b : HALF * (b + 1)].rearrange("a q c -> q a c").bitcast(I32),
                 )
 
         def load_w4_lower(a):
@@ -118,8 +116,10 @@ def tile_list_prerequisite_mastery_kernel(
         for quad in QUADRANTS[1:]:
             move_scale_rows(0, quad, nc.sync)
         w4_lower.append(load_w4_lower(1))
-        for quad in QUADRANTS:
-            move_scale_rows(1, quad, nc.sync if quad < 3 else nc.gpsimd)
+        for s in range(4):
+            (nc.sync if s < 3 else nc.gpsimd).dma_start(
+                v_planes[1][s:P:32, :].bitcast(I32), picked_scale_rows[16 + s : 32 : 4, :].bitcast(I32)
+            )
         w4_upper = kept("w4_upper", [P, 2, H], U8, "scale_window")
         nc.gpsimd.dma_start(w4_upper[:].bitcast(I32), w4_words[:, :, H : 2 * H].rearrange("a p c -> p a c").bitcast(I32))
         gain_runs = kept("gain_runs", [P, 2, 16], F32)
@@ -173,20 +173,28 @@ def tile_list_prerequisite_mastery_kernel(
                 codes[:].bitcast(U32).rearrange("p t (q w) -> p t q w", w=2),
                 w4_lower[a][:].bitcast(U32).rearrange("p (q t w) -> p t q w", t=4, w=2),
             )
-            w4_codes[0, a] = codes[:]
+            for t in range(4):
+                w4_codes[0, a, t] = codes[:, t, :]
 
         v_words = [kept("v_words%d" % a, [P, S], U32) for a in range(2)]
         nc.vector.tensor_copy(v_words[0][:], table[0][:].indirect(offs_sb[:]))
         for cols in (LOWER, THIRD, FOURTH):
             nc.vector.tensor_copy(v_words[1][:, cols], table[1][:].indirect(entries(offs_sb, cols)))
-        upper_codes = kept("w4_codes1", [P, 2, 4, 2 * P], U8, "table1")
-        nc.vector.tensor_copy(
-            upper_codes[:].bitcast(U32).rearrange("p a t (q w) -> p a t q w", w=2),
-            w4_upper[:].bitcast(U32).rearrange("p a (q t w) -> p a t q w", t=4, w=2),
-        )
-        for a in range(2):
-            w4_codes[1, a] = upper_codes[:, a, :, :]
+        upper_words = w4_upper[:].bitcast(U32).rearrange("p a (q t w) -> p a t q w", t=4, w=2)
+        upper_codes = [kept("w4_codes1%d" % i, [P, 2, 2, 2 * P], U8) for i in range(2)]
+
+        def order_upper_codes(i):
+            nc.gpsimd.tensor_copy(
+                upper_codes[i][:].bitcast(U32).rearrange("p a t (q w) -> p a t q w", w=2),
+                upper_words[:, :, 2 * i : 2 * i + 2, :, :],
+            )
+            for a in range(2):
+                for t in range(2):
+                    w4_codes[1, a, 2 * i + t] = upper_codes[i][:, a, t, :]
+
+        order_upper_codes(0)
         order_w4_scales(1, nc.gpsimd.tensor_copy)
+        order_upper_codes(1)
 
         h = [kept("h%d" % j, [P, S], F32) for j in range(ROW_TILES)]
         sums = {}
@@ -198,7 +206,7 @@ def tile_list_prerequisite_mastery_kernel(
                 sums[j, cols.start] = bank(len(sums))[:, 0 : cols.stop - cols.start]
             nc.tensor.matmul_mx(
                 out=sums[j, cols.start],
-                lhsT=w4_codes[b, a][:, t, :].bitcast(FP4X4),
+                lhsT=w4_codes[b, a, t].bitcast(FP4X4),
                 lhsT_scale=w4_planes[b][:, a, t, :],
                 rhs=v_words[a][:, cols].bitcast(FP8X4),
                 rhs_scale=v_planes[a][:, cols],
@@ -233,17 +241,17 @@ def tile_list_prerequisite_mastery_kernel(
         whole = slice(0, COUPLES)
 
         def pick_left(j):
-            left[j] = kept("left%d" % j, [P, COUPLES], F32, "scale_window" if j == 0 else None)
+            left[j] = kept("left%d" % j, [P, COUPLES], F32)
             nc.vector.tensor_copy(left[j][:], h[j][:].indirect(pos1_sb[:]))
 
         def squash(j):
-            nc.scalar.activation(squashed[:, j, :], left[j][:], ACT.Tanh, scale=0.5)
+            nc.scalar.activation(squashed[j], left[j][:], ACT.Tanh, scale=0.5)
 
         def gate(j):
             b, t = divmod(j, 4)
             factor = gain_runs[:, b, 4 * t : 4 * t + 1]
             mastery[j] = kept("mastery%d" % j, [P, COUPLES], F32)
-            nc.scalar.activation(mastery[j][:], squashed[:, j, :], ACT.Identity, bias=factor, scale=factor)
+            nc.scalar.activation(mastery[j][:], squashed[j], ACT.Identity, bias=factor, scale=factor)
 
         def pick_right(j, z_slot, couples):
             nc.vector.tensor_tensor(z_slot, h[j][:].indirect(entries(pos2_sb, couples)), mastery[j][:, couples], ALU.mult)
@@ -260,15 +268,14 @@ def tile_list_prerequisite_mastery_kernel(
         def quantise_z(name, woven):
             return quantise(name, woven, kept(name + "_codes", [P, woven.shape[1]], U32)[:])
 
-        early = [(0, LOWER), (0, THIRD), (0, FOURTH), (1, LOWER), (1, UPPER)]
-        for j, cols in early:
+        for j, cols in [(0, LOWER), (0, THIRD), (0, FOURTH), (1, LOWER)]:
             multiply(j, cols, 0)
-        multiply(0, LOWER, 1)
-        empty(0, LOWER)
-        multiply(1, LOWER, 1)
+        for j in range(2):
+            multiply(j, LOWER, 1)
+            empty(j, LOWER)
         multiply(0, THIRD, 1)
-        empty(0, THIRD)
-        empty(1, LOWER)
+        empty(0, THIRD, nc.vector.tensor_copy)
+        multiply(1, UPPER, 0)
         multiply(2, LOWER, 1)
         multiply(0, FOURTH, 1)
         empty(0, FOURTH, nc.vector.tensor_copy)
@@ -280,10 +287,14 @@ def tile_list_prerequisite_mastery_kernel(
         empty(2, LOWER)
         first_product(2, UPPER)
         pick_left(2)
+        squashed = {}
         for j in range(3, ROW_TILES):
             first_product(j, LOWER)
             first_product(j, UPPER)
             pick_left(j)
+            if j == 5:
+                squashed[0] = kept("squashed0", [P, COUPLES], F32, "w4_codes10")[:]
+                squash(0)
         w2_rounded = [kept("w2_rounded%d" % b, [P, N, 4], BF16) for b in range(2)]
         for b in range(2):
             round_w2(w2_rows[b][:], w2_rounded[b][:])
@@ -292,11 +303,13 @@ def tile_list_prerequisite_mastery_kernel(
 
         z_rows0 = kept("z_rows0", [P, 4, COUPLES], F32)
         rows_ab = kept("z_rows10", [P, 4, 3 * P], F32)
-        squashed = kept("squashed", [P, ROW_TILES, COUPLES], F32, "table1")
-        squash(0)
+        squashed_rest = kept("squashed", [P, ROW_TILES - 1, COUPLES], F32, "w4_codes11")
+        for j in range(1, ROW_TILES):
+            squashed[j] = squashed_rest[:, j - 1, :]
+        squash(1)
         for j in range(ROW_TILES):
-            if j + 1 < ROW_TILES:
-                squash(j + 1)
+            if j + 2 < ROW_TILES:
+                squash(j + 2)
             gate(j)
             if j < 4:
                 pick_right(j, z_rows0[:, j, :], whole)
@@ -309,12 +322,12 @@ def tile_list_prerequisite_mastery_kernel(
         ]
         woven_a = weave_z(kept("z_woven_a", [P, 2 * P, 4], BF16)[:], rows_ab[:, :, PIECES[0]])
         woven_b = weave_z(kept("z_woven_b", [P, P, 4], BF16)[:], rows_ab[:, :, PIECES[1]])
-        codes0 = kept("w2_codes0", [P, 2 * P], U32, "left7")
+        codes0 = kept("w2_codes0", [P, 2 * P], U32, "mastery3")
         codes, plane = quantise("w2_0", w2_rounded[0][:, 0 : 2 * P, :], codes0[:])
         for j in range(2):
             w2_mx[0, j] = (codes[:, P * j : P * (j + 1)], plane[:, P * j : P * (j + 1)])
         z0 = [quantise_z("z0_low", woven0[0])]
-        rows_c = kept("z_rows12", [P, 4, P], F32, "table1")
+        rows_c = kept("z_rows12", [P, 4, P], F32, "w4_codes11")
         for t in range(4):
             pick_right(4 + t, rows_c[:, t, :], PIECES[2])
         woven_c = weave_z(kept("z_woven_c", [P, P, 4], BF16)[:], rows_c[:])
@@ -323,7 +336,7 @@ def tile_list_prerequisite_mastery_kernel(
         z0.append(quantise("z0_high", woven0[1], kept("z0_high_codes", [P, 2 * P], U32, "h6")[:]))
         z1 += [quantise_z("z_b", woven_b), quantise_z("z_c", woven_c)]
         late_pieces = [(1, 1), (0, 2), (1, 2), (0, 3), (1, 3)]
-        late_codes = kept("w2_late_codes", [P, len(late_pieces), P], U32, "table1")
+        late_codes = kept("w2_late_codes", [P, len(late_pieces), P], U32, "w4_codes11")
         for i, (b, j) in enumerate(late_pieces):
             quantise_w2(b, j, late_codes[:, i, :])
 
@@ -355,7 +368,7 @@ def tile_list_prerequisite_mastery_kernel(
         for j in range(1, OUT_TILES):
             second_product(j, (0, 1, 2), bank(j + 2))
 
-        result = kept("result", [P, OUT_TILES, UNITS], F32, "table1")
+        result = kept("result", [P, OUT_TILES, UNITS], F32, "w4_codes11")
         one_couple = [kept("one_couple%d" % j, [P, UNITS], F32) for j in range(OUT_TILES)]
         both_first = kept("both_first", [P, UNITS], F32)
         both_rest = kept("both_rest", [P, OUT_TILES - 1, UNITS], F32, "both_first")

@@ -30,7 +30,7 @@ PIECES = (slice(0, 256), slice(256, 384), slice(384, 512))
 WARM_PASSES = 4
 QUADRANTS = (0, 2, 1, 3)
 LOWER, UPPER = slice(0, 512), slice(512, 1024)
-THIRD, FOURTH = slice(512, 768), slice(768, 1024)
+THIRD, FOURTH = slice(512, 896), slice(896, 1024)
 
 
 def tile_list_prerequisite_mastery_kernel(
@@ -96,7 +96,6 @@ def tile_list_prerequisite_mastery_kernel(
         table = [load_table(0)]
         load_w4_scales(0)
         w4_lower = [load_w4_lower(0)]
-        pos1_sb = load_list("pos1_sb", pos1)
         table.append(load_table(1))
 
         picked_scale_rows = kept("picked_scale_rows", [P, S], U8)
@@ -122,6 +121,7 @@ def tile_list_prerequisite_mastery_kernel(
             )
         w4_upper = kept("w4_upper", [P, 2, H], U8, "scale_window")
         nc.gpsimd.dma_start(w4_upper[:].bitcast(I32), w4_words[:, :, H : 2 * H].rearrange("a p c -> p a c").bitcast(I32))
+        pos1_sb = load_list("pos1_sb", pos1)
         gain_runs = kept("gain_runs", [P, 2, 16], F32)
         gain_view = gain.rearrange("(b q c) -> q b c", b=2, c=16)
         for e in range(4):
@@ -202,17 +202,21 @@ def tile_list_prerequisite_mastery_kernel(
         def multiply(j, cols, a):
             b, t = divmod(j, 4)
             opens = (j, cols.start) not in sums
+            width = cols.stop - cols.start
             if opens:
-                sums[j, cols.start] = bank(len(sums))[:, 0 : cols.stop - cols.start]
-            nc.tensor.matmul_mx(
-                out=sums[j, cols.start],
-                lhsT=w4_codes[b, a, t].bitcast(FP4X4),
-                lhsT_scale=w4_planes[b][:, a, t, :],
-                rhs=v_words[a][:, cols].bitcast(FP8X4),
-                rhs_scale=v_planes[a][:, cols],
-                start=opens,
-                stop=not opens,
-            )
+                sums[j, cols.start] = bank(len(sums))[:, 0:width]
+            parts = [slice(0, 2 * P), slice(2 * P, width)] if width == 3 * P else [slice(0, width)]
+            for i, part in enumerate(parts):
+                picked = slice(cols.start + part.start, cols.start + part.stop)
+                nc.tensor.matmul_mx(
+                    out=sums[j, cols.start][:, part],
+                    lhsT=w4_codes[b, a, t].bitcast(FP4X4),
+                    lhsT_scale=w4_planes[b][:, a, t, :],
+                    rhs=v_words[a][:, picked].bitcast(FP8X4),
+                    rhs_scale=v_planes[a][:, picked],
+                    start=opens and i == 0,
+                    stop=not opens and i == len(parts) - 1,
+                )
 
         def empty(j, cols, copy=nc.scalar.copy):
             copy(h[j][:, cols], sums[j, cols.start])
@@ -273,18 +277,15 @@ def tile_list_prerequisite_mastery_kernel(
         for j in range(2):
             multiply(j, LOWER, 1)
             empty(j, LOWER)
-        multiply(0, THIRD, 1)
-        empty(0, THIRD, nc.vector.tensor_copy)
         multiply(1, UPPER, 0)
-        multiply(2, LOWER, 1)
-        multiply(0, FOURTH, 1)
-        empty(0, FOURTH, nc.vector.tensor_copy)
+        for cols in (THIRD, FOURTH):
+            multiply(0, cols, 1)
+            empty(0, cols, nc.vector.tensor_copy)
         pick_left(0)
         multiply(1, UPPER, 1)
         empty(1, UPPER)
         pick_left(1)
-        multiply(2, LOWER, 0)
-        empty(2, LOWER)
+        first_product(2, LOWER)
         first_product(2, UPPER)
         pick_left(2)
         squashed = {}
@@ -306,10 +307,9 @@ def tile_list_prerequisite_mastery_kernel(
         squashed_rest = kept("squashed", [P, ROW_TILES - 1, COUPLES], F32, "w4_codes11")
         for j in range(1, ROW_TILES):
             squashed[j] = squashed_rest[:, j - 1, :]
-        squash(1)
         for j in range(ROW_TILES):
-            if j + 2 < ROW_TILES:
-                squash(j + 2)
+            if j + 1 < ROW_TILES:
+                squash(j + 1)
             gate(j)
             if j < 4:
                 pick_right(j, z_rows0[:, j, :], whole)
@@ -322,20 +322,16 @@ def tile_list_prerequisite_mastery_kernel(
         ]
         woven_a = weave_z(kept("z_woven_a", [P, 2 * P, 4], BF16)[:], rows_ab[:, :, PIECES[0]])
         woven_b = weave_z(kept("z_woven_b", [P, P, 4], BF16)[:], rows_ab[:, :, PIECES[1]])
-        codes0 = kept("w2_codes0", [P, 2 * P], U32, "mastery3")
-        codes, plane = quantise("w2_0", w2_rounded[0][:, 0 : 2 * P, :], codes0[:])
-        for j in range(2):
-            w2_mx[0, j] = (codes[:, P * j : P * (j + 1)], plane[:, P * j : P * (j + 1)])
-        z0 = [quantise_z("z0_low", woven0[0])]
         rows_c = kept("z_rows12", [P, 4, P], F32, "w4_codes11")
         for t in range(4):
             pick_right(4 + t, rows_c[:, t, :], PIECES[2])
         woven_c = weave_z(kept("z_woven_c", [P, P, 4], BF16)[:], rows_c[:])
-        quantise_w2(1, 0, kept("w2_codes10", [P, P], U32, "h4")[:])
-        z1 = [quantise("z_a", woven_a, kept("z_a_codes", [P, 2 * P], U32, "h5")[:])]
-        z0.append(quantise("z0_high", woven0[1], kept("z0_high_codes", [P, 2 * P], U32, "h6")[:]))
-        z1 += [quantise_z("z_b", woven_b), quantise_z("z_c", woven_c)]
-        late_pieces = [(1, 1), (0, 2), (1, 2), (0, 3), (1, 3)]
+        quantise_w2(0, 0, kept("w2_codes00", [P, P], U32, "h4")[:])
+        z0 = [quantise("z0_low", woven0[0], kept("z0_low_codes", [P, 2 * P], U32, "h5")[:])]
+        quantise_w2(1, 0, kept("w2_codes10", [P, P], U32, "h6")[:])
+        z0.append(quantise("z0_high", woven0[1], kept("z0_high_codes", [P, 2 * P], U32, "h7")[:]))
+        z1 = [quantise_z("z_a", woven_a), quantise_z("z_b", woven_b), quantise_z("z_c", woven_c)]
+        late_pieces = [(b, j) for j in range(1, OUT_TILES) for b in range(2)]
         late_codes = kept("w2_late_codes", [P, len(late_pieces), P], U32, "w4_codes11")
         for i, (b, j) in enumerate(late_pieces):
             quantise_w2(b, j, late_codes[:, i, :])

@@ -60,11 +60,14 @@ def tile_list_prerequisite_mastery_kernel(
         nc.scalar.dma_start(
             scale_window[0:32, :].bitcast(I32), tab_scales.rearrange("a q t -> (a q) t").bitcast(I32)
         )
+        lower_scale_rows = kept("lower_scale_rows", [32, HALF], U8)
+        nc.scalar.dma_start(
+            lower_scale_rows[:].bitcast(I32), w4_scales[:, :, 0:HALF].rearrange("a q c -> (a q) c").bitcast(I32)
+        )
         offs_sb = load_list("offs_sb", offs)
 
-        w4_scale_rows = [kept("w4_scale_rows%d" % b, [P, 2, HALF], U8) for b in range(2)]
-        for rows in w4_scale_rows:
-            nc.gpsimd.memset(rows[:].bitcast(I32), 0)
+        upper_scale_rows = kept("upper_scale_rows", [P, 2, HALF], U8)
+        nc.gpsimd.memset(upper_scale_rows[:].bitcast(I32), 0)
 
         warm_input = kept("warm_input", [P, 1], F32)
         nc.vector.memset(warm_input[:], 0.0)
@@ -72,7 +75,7 @@ def tile_list_prerequisite_mastery_kernel(
         nc.scalar.activation(warm[:], warm_input[:], ACT.Silu)
         nc.vector.memset(scale_window[64:128, :].bitcast(I32), 0)
         nc.vector.memset(scale_window[32:64, :].bitcast(I32), 0)
-        v_planes = [kept("v_plane%d" % a, [P, S], U8) for a in range(2)]
+        v_planes = [kept("v_plane%d" % a, [P, S + HALF], U8) for a in range(2)]
         for plane in v_planes:
             nc.vector.memset(plane[:].bitcast(I32), 0)
 
@@ -81,20 +84,15 @@ def tile_list_prerequisite_mastery_kernel(
             nc.sync.dma_start(words[:].bitcast(I32), tab_words[a].rearrange("p t i -> p (t i)").bitcast(I32))
             return words
 
-        def load_w4_scales(b):
-            for s in range(4):
-                nc.sync.dma_start(
-                    w4_scale_rows[b][s:P:32, :, :].bitcast(I32),
-                    w4_scales[:, s:16:4, HALF * b : HALF * (b + 1)].rearrange("a q c -> q a c").bitcast(I32),
-                )
-
         def load_w4_lower(a):
             raw = kept("w4_raw%d" % a, [P, H], U8)
             nc.sync.dma_start(raw[:].bitcast(I32), w4_words[a][:, 0:H].bitcast(I32))
             return raw
 
         table = [load_table(0)]
-        load_w4_scales(0)
+        pos1_sb = load_list("pos1_sb", pos1)
+        pos2_sb = load_list("pos2_sb", pos2)
+        pos3_sb = load_list("pos3_sb", pos3)
         w4_lower = [load_w4_lower(0)]
         table.append(load_table(1))
 
@@ -104,12 +102,16 @@ def tile_list_prerequisite_mastery_kernel(
             nc.vector.tensor_copy(picked_scale_rows[:, part], scale_window[:].indirect(entries(offs_sb, part)))
         for part in list_parts:
             nc.vector.tensor_copy(v_planes[0][0:32, part].bitcast(I32), picked_scale_rows[0:32, part].bitcast(I32))
+        nc.scalar.copy(
+            v_planes[0][0:32, S:].bitcast(U32).rearrange("p (t q) -> p q t", t=4),
+            lower_scale_rows[:].bitcast(U32).rearrange("p (q t) -> p q t", t=4),
+        )
 
         def move_scale_rows(a, quad, queue):
             first_row = 16 * a + 4 * quad
             queue.dma_start(
                 v_planes[a][32 * quad : 32 * quad + 4, :].bitcast(I32),
-                picked_scale_rows[first_row : first_row + 4, :].bitcast(I32),
+                v_planes[0][first_row : first_row + 4, :].bitcast(I32),
             )
 
         for quad in QUADRANTS[1:]:
@@ -117,16 +119,19 @@ def tile_list_prerequisite_mastery_kernel(
         w4_lower.append(load_w4_lower(1))
         for s in range(4):
             (nc.sync if s < 3 else nc.gpsimd).dma_start(
-                v_planes[1][s:P:32, :].bitcast(I32), picked_scale_rows[16 + s : 32 : 4, :].bitcast(I32)
+                v_planes[1][s:P:32, :].bitcast(I32), v_planes[0][16 + s : 32 : 4, :].bitcast(I32)
             )
-        w4_upper = kept("w4_upper", [P, 2, H], U8, "scale_window")
+        w4_upper = kept("w4_upper", [P, 2, H], U8, "picked_scale_rows")
         nc.gpsimd.dma_start(w4_upper[:].bitcast(I32), w4_words[:, :, H : 2 * H].rearrange("a p c -> p a c").bitcast(I32))
-        pos1_sb = load_list("pos1_sb", pos1)
         gain_runs = kept("gain_runs", [P, 2, 16], F32)
         gain_view = gain.rearrange("(b q c) -> q b c", b=2, c=16)
         for e in range(4):
             nc.sync.dma_start(gain_runs[e:P:4, :, 0:13], gain_view[:, :, e : e + 13])
-        load_w4_scales(1)
+        for s in range(4):
+            nc.sync.dma_start(
+                upper_scale_rows[s:P:32, :, :].bitcast(I32),
+                w4_scales[:, s:16:4, HALF:H].rearrange("a q c -> q a c").bitcast(I32),
+            )
 
         w2_view = w2.rearrange("(b q t e) n -> b t q e n", b=2, t=4, e=4)
 
@@ -137,32 +142,20 @@ def tile_list_prerequisite_mastery_kernel(
                 nc.sync.dma_start(w2_rows[b][:, t, :], w2_view[b][t])
 
         load_w2(0)
-        pos2_sb = load_list("pos2_sb", pos2)
         load_w2(1)
-        pos3_sb = load_list("pos3_sb", pos3)
         pos4_sb = load_list("pos4_sb", pos4)
         bias_sb = kept("bias_sb", [P, OUT_TILES], F32)
         with nc.allow_non_contiguous_dma(reason="one value a partition"):
             nc.sync.dma_start(bias_sb[:], bias.rearrange("(j p) -> p j", p=P))
-
-        w4_planes = [kept("w4_planes%d" % b, [P, 2, 4, P], U8) for b in range(2)]
-
-        def order_w4_scales(b, copy):
-            copy(
-                w4_planes[b][:].bitcast(U32).rearrange("p a t q -> p a q t"),
-                w4_scale_rows[b][:].bitcast(U32).rearrange("p a (q t) -> p a q t", t=4),
-            )
-
-        order_w4_scales(0, nc.scalar.copy)
 
         idle = bank(PSUM_BANKS - 1)
         for i in range(WARM_PASSES):
             nc.tensor.matmul_mx(
                 out=idle[:],
                 lhsT=w4_lower[0][:, 2 * P * i : 2 * P * (i + 1)].bitcast(FP4X4),
-                lhsT_scale=w4_scale_rows[0][:, 0, P * i : P * (i + 1)],
+                lhsT_scale=scale_window[:, P * i : P * (i + 1)],
                 rhs=table[0][:, 0:BANK].bitcast(FP8X4),
-                rhs_scale=w4_scale_rows[0][:, 1, :],
+                rhs_scale=scale_window[:, 0:BANK],
                 start=True,
                 stop=True,
             )
@@ -193,7 +186,11 @@ def tile_list_prerequisite_mastery_kernel(
                     w4_codes[1, a, 2 * i + t] = upper_codes[i][:, a, t, :]
 
         order_upper_codes(0)
-        order_w4_scales(1, nc.gpsimd.tensor_copy)
+        upper_planes = kept("upper_planes", [P, 2, 4, P], U8)
+        nc.gpsimd.tensor_copy(
+            upper_planes[:].bitcast(U32).rearrange("p a t q -> p a q t"),
+            upper_scale_rows[:].bitcast(U32).rearrange("p a (q t) -> p a q t", t=4),
+        )
         order_upper_codes(1)
 
         h = [kept("h%d" % j, [P, S], F32) for j in range(ROW_TILES)]
@@ -211,7 +208,7 @@ def tile_list_prerequisite_mastery_kernel(
                 nc.tensor.matmul_mx(
                     out=sums[j, cols.start][:, part],
                     lhsT=w4_codes[b, a, t].bitcast(FP4X4),
-                    lhsT_scale=w4_planes[b][:, a, t, :],
+                    lhsT_scale=upper_planes[:, a, t, :] if b else v_planes[a][:, S + P * t : S + P * (t + 1)],
                     rhs=v_words[a][:, picked].bitcast(FP8X4),
                     rhs_scale=v_planes[a][:, picked],
                     start=opens and i == 0,

@@ -90,9 +90,6 @@ def tile_list_prerequisite_mastery_kernel(
             return raw
 
         table = [load_table(0)]
-        pos1_sb = load_list("pos1_sb", pos1)
-        pos2_sb = load_list("pos2_sb", pos2)
-        pos3_sb = load_list("pos3_sb", pos3)
         w4_lower = [load_w4_lower(0)]
         table.append(load_table(1))
 
@@ -123,6 +120,7 @@ def tile_list_prerequisite_mastery_kernel(
             )
         w4_upper = kept("w4_upper", [P, 2, H], U8, "picked_scale_rows")
         nc.gpsimd.dma_start(w4_upper[:].bitcast(I32), w4_words[:, :, H : 2 * H].rearrange("a p c -> p a c").bitcast(I32))
+        pos1_sb = load_list("pos1_sb", pos1)
         gain_runs = kept("gain_runs", [P, 2, 16], F32)
         gain_view = gain.rearrange("(b q c) -> q b c", b=2, c=16)
         for e in range(4):
@@ -142,7 +140,9 @@ def tile_list_prerequisite_mastery_kernel(
                 nc.sync.dma_start(w2_rows[b][:, t, :], w2_view[b][t])
 
         load_w2(0)
+        pos2_sb = load_list("pos2_sb", pos2)
         load_w2(1)
+        pos3_sb = load_list("pos3_sb", pos3)
         pos4_sb = load_list("pos4_sb", pos4)
         bias_sb = kept("bias_sb", [P, OUT_TILES], F32)
         with nc.allow_non_contiguous_dma(reason="one value a partition"):

@@ -326,8 +326,9 @@ def tile_list_prerequisite_mastery_kernel(
         quantise_w2(0, 0, kept("w2_codes00", [P, P], U32, "h4")[:])
         z0 = [quantise("z0_low", woven0[0], kept("z0_low_codes", [P, 2 * P], U32, "h5")[:])]
         quantise_w2(1, 0, kept("w2_codes10", [P, P], U32, "h6")[:])
+        z1 = [quantise_z("z_a", woven_a)]
         z0.append(quantise("z0_high", woven0[1], kept("z0_high_codes", [P, 2 * P], U32, "h7")[:]))
-        z1 = [quantise_z("z_a", woven_a), quantise_z("z_b", woven_b), quantise_z("z_c", woven_c)]
+        z1 += [quantise_z("z_b", woven_b), quantise_z("z_c", woven_c)]
         late_pieces = [(b, j) for j in range(1, OUT_TILES) for b in range(2)]
         late_codes = kept("w2_late_codes", [P, len(late_pieces), P], U32, "w4_codes11")
         for i, (b, j) in enumerate(late_pieces):
@@ -354,12 +355,13 @@ def tile_list_prerequisite_mastery_kernel(
                     start=(i == 0),
                     stop=(i == len(passes) - 1),
                 )
-            nc.scalar.copy(y[j][:, span], acc[:, span])
+            return lambda: nc.scalar.copy(y[j][:, span], acc[:, span])
 
-        second_product(0, (0,), bank(1))
-        second_product(0, (1, 2), bank(2))
-        for j in range(1, OUT_TILES):
-            second_product(j, (0, 1, 2), bank(j + 2))
+        for piece in range(len(PIECES)):
+            second_product(0, (piece,), bank(1 + piece))()
+        for j in (1, 2):
+            second_product(j, (0, 1, 2), bank(j + 3))()
+        empty_last = second_product(OUT_TILES - 1, (0, 1, 2), bank(OUT_TILES + 2))
 
         result = kept("result", [P, OUT_TILES, UNITS], F32, "w4_codes11")
         one_couple = [kept("one_couple%d" % j, [P, UNITS], F32) for j in range(OUT_TILES)]
@@ -387,11 +389,14 @@ def tile_list_prerequisite_mastery_kernel(
         for part in halves:
             add_second(0, part)
         finish(0, all_units)
-        for j in range(1, OUT_TILES):
+        empty_last()
+        for j in (1, 2):
             pick_first(j, all_units)
         for j in (1, 2):
             add_second(j, all_units)
             finish(j, all_units)
+        for part in halves:
+            pick_first(OUT_TILES - 1, part)
         for part in halves:
             add_second(OUT_TILES - 1, part)
             finish(OUT_TILES - 1, part)

from contextlib import ExitStack

import concourse.mybir as mybir

K, H, N = 1024, 1024, 512
T, S = 2048, 1024
COUPLES, UNITS = 512, 256
FLOPS = 2 * K * H * S + 2 * H * N * COUPLES

F32 = mybir.dt.float32
BF16 = mybir.dt.bfloat16
I32 = mybir.dt.int32
U32 = mybir.dt.uint32
U16 = mybir.dt.uint16
U8 = mybir.dt.uint8
FP8X4 = mybir.dt.float8_e4m3fn_x4
FP4X4 = mybir.dt.float4_e2m1fn_x4
ACT = mybir.ActivationFunctionType
ALU = mybir.AluOpType

P = 128
BANK = 512
PSUM_BANKS = 8
PER_COLUMN = 16
ROW_TILES = H // P
OUT_TILES = N // P
HALF = H // 2

PIECES = (slice(0, 256), slice(256, 384), slice(384, 512))
WARM_PASSES = 4
QUADRANTS = (0, 2, 1, 3)
LOWER, UPPER = slice(0, 512), slice(512, 1024)
THIRD, FOURTH = slice(512, 896), slice(896, 1024)


def tile_list_prerequisite_mastery_kernel(
    tc, tab_words, tab_scales, offs, w4_words, w4_scales, pos1, pos2, gain, w2, pos3, pos4, bias, out
):
    nc = tc.nc
    with ExitStack() as ctx:
        lists = ctx.enter_context(tc.tile_pool(name="lists", bufs=1))
        keep = ctx.enter_context(tc.tile_pool(name="keep", bufs=1))
        psum = ctx.enter_context(tc.psum_pool(name="psum", bufs=1))

        def load_list(name, dram):
            tile = lists.tile([P, dram.shape[1]], U16, name=name)
            nc.sync.dma_start(tile[:], dram)
            return tile

        def kept(name, shape, dtype, over=None):
            return keep.tile(shape, dtype, name=name, tag=over or name, align_bytes=64)

        def bank(i):
            return psum.tile([P, BANK], F32, name="bank%d" % (i % PSUM_BANKS))

        def entries(tile, part):
            return tile[:, part.start // PER_COLUMN : part.stop // PER_COLUMN]

        scale_window = kept("scale_window", [P, T], U8)
        nc.scalar.dma_start(
            scale_window[0:32, :].bitcast(I32), tab_scales.rearrange("a q t -> (a q) t").bitcast(I32)
        )
        lower_scale_rows = kept("lower_scale_rows", [32, HALF], U8)
        nc.scalar.dma_start(
            lower_scale_rows[:].bitcast(I32), w4_scales[:, :, 0:HALF].rearrange("a q c -> (a q) c").bitcast(I32)
        )
        offs_sb = load_list("offs_sb", offs)

        upper_scale_rows = kept("upper_scale_rows", [P, 2, HALF], U8)
        nc.gpsimd.memset(upper_scale_rows[:].bitcast(I32), 0)

        warm_input = kept("warm_input", [P, 1], F32)
        nc.vector.memset(warm_input[:], 0.0)
        warm = kept("warm", [P, 1], F32)
        nc.scalar.activation(warm[:], warm_input[:], ACT.Silu)
        nc.vector.memset(scale_window[64:128, :].bitcast(I32), 0)
        nc.vector.memset(scale_window[32:64, :].bitcast(I32), 0)
        v_planes = [kept("v_plane%d" % a, [P, S + HALF], U8) for a in range(2)]
        for plane in v_planes:
            nc.vector.memset(plane[:].bitcast(I32), 0)

        def load_table(a):
            words = kept("table%d" % a, [P, T], U32)
            nc.sync.dma_start(words[:].bitcast(I32), tab_words[a].rearrange("p t i -> p (t i)").bitcast(I32))
            return words

        def load_w4_lower(a):
            raw = kept("w4_raw%d" % a, [P, H], U8)
            nc.sync.dma_start(raw[:].bitcast(I32), w4_words[a][:, 0:H].bitcast(I32))
            return raw

        table = [load_table(0)]
        w4_lower = [load_w4_lower(0)]
        table.append(load_table(1))

        picked_scale_rows = kept("picked_scale_rows", [P, S], U8)
        list_parts = [slice(0, 768), slice(768, S)]
        for part in list_parts:
            nc.vector.tensor_copy(picked_scale_rows[:, part], scale_window[:].indirect(entries(offs_sb, part)))
        for part in list_parts:
            nc.vector.tensor_copy(v_planes[0][0:32, part].bitcast(I32), picked_scale_rows[0:32, part].bitcast(I32))
        nc.scalar.copy(
            v_planes[0][0:32, S:].bitcast(U32).rearrange("p (t q) -> p q t", t=4),
            lower_scale_rows[:].bitcast(U32).rearrange("p (q t) -> p q t", t=4),
        )

        def move_scale_rows(a, quad, queue):
            first_row = 16 * a + 4 * quad
            queue.dma_start(
                v_planes[a][32 * quad : 32 * quad + 4, :].bitcast(I32),
                v_planes[0][first_row : first_row + 4, :].bitcast(I32),
            )

        for quad in QUADRANTS[1:]:
            move_scale_rows(0, quad, nc.sync)
        w4_lower.append(load_w4_lower(1))
        for s in range(4):
            (nc.sync if s < 3 else nc.gpsimd).dma_start(
                v_planes[1][s:P:32, :].bitcast(I32), v_planes[0][16 + s : 32 : 4, :].bitcast(I32)
            )
        w4_upper = kept("w4_upper", [P, 2, H], U8, "picked_scale_rows")
        nc.gpsimd.dma_start(w4_upper[:].bitcast(I32), w4_words[:, :, H : 2 * H].rearrange("a p c -> p a c").bitcast(I32))
        pos1_sb = load_list("pos1_sb", pos1)
        gain_runs = kept("gain_runs", [P, 2, 16], F32)
        gain_view = gain.rearrange("(b q c) -> q b c", b=2, c=16)
        for e in range(4):
            nc.sync.dma_start(gain_runs[e:P:4, :, 0:13], gain_view[:, :, e : e + 13])
        for s in range(4):
            nc.sync.dma_start(
                upper_scale_rows[s:P:32, :, :].bitcast(I32),
                w4_scales[:, s:16:4, HALF:H].rearrange("a q c -> q a c").bitcast(I32),
            )

        w2_view = w2.rearrange("(b q t e) n -> b t q e n", b=2, t=4, e=4)

        w2_rows = [kept("w2_rows%d" % b, [P, 4, N], F32) for b in range(2)]

        def load_w2(b):
            for t in range(4):
                nc.sync.dma_start(w2_rows[b][:, t, :], w2_view[b][t])

        load_w2(0)
        pos2_sb = load_list("pos2_sb", pos2)
        load_w2(1)
        pos3_sb = load_list("pos3_sb", pos3)
        pos4_sb = load_list("pos4_sb", pos4)
        bias_sb = kept("bias_sb", [P, OUT_TILES], F32)
        with nc.allow_non_contiguous_dma(reason="one value a partition"):
            nc.sync.dma_start(bias_sb[:], bias.rearrange("(j p) -> p j", p=P))

        idle = bank(PSUM_BANKS - 1)
        for i in range(WARM_PASSES):
            nc.tensor.matmul_mx(
                out=idle[:],
                lhsT=w4_lower[0][:, 2 * P * i : 2 * P * (i + 1)].bitcast(FP4X4),
                lhsT_scale=scale_window[:, P * i : P * (i + 1)],
                rhs=table[0][:, 0:BANK].bitcast(FP8X4),
                rhs_scale=scale_window[:, 0:BANK],
                start=True,
                stop=True,
            )
        w4_codes = {}
        for a in range(2):
            codes = kept("w4_codes0%d" % a, [P, 4, 2 * P], U8)
            nc.scalar.copy(
                codes[:].bitcast(U32).rearrange("p t (q w) -> p t q w", w=2),
                w4_lower[a][:].bitcast(U32).rearrange("p (q t w) -> p t q w", t=4, w=2),
            )
            for t in range(4):
                w4_codes[0, a, t] = codes[:, t, :]

        v_words = [kept("v_words%d" % a, [P, S], U32) for a in range(2)]
        nc.vector.tensor_copy(v_words[0][:], table[0][:].indirect(offs_sb[:]))
        for cols in (LOWER, THIRD, FOURTH):
            nc.vector.tensor_copy(v_words[1][:, cols], table[1][:].indirect(entries(offs_sb, cols)))
        upper_words = w4_upper[:].bitcast(U32).rearrange("p a (q t w) -> p a t q w", t=4, w=2)
        upper_codes = [kept("w4_codes1%d" % i, [P, 2, 2, 2 * P], U8) for i in range(2)]

        def order_upper_codes(i):
            nc.gpsimd.tensor_copy(
                upper_codes[i][:].bitcast(U32).rearrange("p a t (q w) -> p a t q w", w=2),
                upper_words[:, :, 2 * i : 2 * i + 2, :, :],
            )
            for a in range(2):
                for t in range(2):
                    w4_codes[1, a, 2 * i + t] = upper_codes[i][:, a, t, :]

        order_upper_codes(0)
        upper_planes = kept("upper_planes", [P, 2, 4, P], U8)
        nc.gpsimd.tensor_copy(
            upper_planes[:].bitcast(U32).rearrange("p a t q -> p a q t"),
            upper_scale_rows[:].bitcast(U32).rearrange("p a (q t) -> p a q t", t=4),
        )
        order_upper_codes(1)

        h = [kept("h%d" % j, [P, S], F32) for j in range(ROW_TILES)]
        sums = {}

        def multiply(j, cols, a):
            b, t = divmod(j, 4)
            opens = (j, cols.start) not in sums
            width = cols.stop - cols.start
            if opens:
                sums[j, cols.start] = bank(len(sums))[:, 0:width]
            parts = [slice(0, 2 * P), slice(2 * P, width)] if width == 3 * P else [slice(0, width)]
            for i, part in enumerate(parts):
                picked = slice(cols.start + part.start, cols.start + part.stop)
                nc.tensor.matmul_mx(
                    out=sums[j, cols.start][:, part],
                    lhsT=w4_codes[b, a, t].bitcast(FP4X4),
                    lhsT_scale=upper_planes[:, a, t, :] if b else v_planes[a][:, S + P * t : S + P * (t + 1)],
                    rhs=v_words[a][:, picked].bitcast(FP8X4),
                    rhs_scale=v_planes[a][:, picked],
                    start=opens and i == 0,
                    stop=not opens and i == len(parts) - 1,
                )

        def empty(j, cols, copy=nc.scalar.copy):
            copy(h[j][:, cols], sums[j, cols.start])

        def first_product(j, cols):
            multiply(j, cols, 1)
            multiply(j, cols, 0)
            empty(j, cols)

        def quantise(name, woven, codes):
            plane = kept(name + "_plane", [P, codes.shape[1]], U8)
            nc.vector.quantize_mx(
                out=codes.bitcast(FP8X4), scales=plane[:], in_=woven.rearrange("p m t -> p (m t)")
            )
            return codes, plane[:]

        w2_woven, w2_mx = {}, {}

        def round_w2(rows, woven):
            nc.gpsimd.tensor_scalar(woven, rows.rearrange("p t n -> p n t"), 1.0, 0.0, ALU.mult, ALU.add)

        def quantise_w2(b, j, codes):
            w2_mx[b, j] = quantise("w2_%d%d" % (b, j), w2_woven[b, j], codes)

        left, mastery = {}, {}
        whole = slice(0, COUPLES)

        def pick_left(j):
            left[j] = kept("left%d" % j, [P, COUPLES], F32)
            nc.vector.tensor_copy(left[j][:], h[j][:].indirect(pos1_sb[:]))

        def squash(j):
            nc.scalar.activation(squashed[j], left[j][:], ACT.Tanh, scale=0.5)

        def gate(j):
            b, t = divmod(j, 4)
            factor = gain_runs[:, b, 4 * t : 4 * t + 1]
            mastery[j] = kept("mastery%d" % j, [P, COUPLES], F32)
            nc.scalar.activation(mastery[j][:], squashed[j], ACT.Identity, bias=factor, scale=factor)

        def pick_right(j, z_slot, couples):
            nc.vector.tensor_tensor(z_slot, h[j][:].indirect(entries(pos2_sb, couples)), mastery[j][:, couples], ALU.mult)

        def weave_z(woven, rows):
            nc.scalar.activation(
                woven.rearrange("p (c i) t -> p c t i", i=4),
                rows.rearrange("p t (c i) -> p c t i", i=4),
                ACT.Copy,
                scale=0.5,
            )
            return woven

        def quantise_z(name, woven):
            return quantise(name, woven, kept(name + "_codes", [P, woven.shape[1]], U32)[:])

        for j, cols in [(0, LOWER), (0, THIRD), (0, FOURTH), (1, LOWER)]:
            multiply(j, cols, 0)
        for j in range(2):
            multiply(j, LOWER, 1)
            empty(j, LOWER)
        multiply(1, UPPER, 0)
        for cols in (THIRD, FOURTH):
            multiply(0, cols, 1)
            empty(0, cols, nc.vector.tensor_copy)
        pick_left(0)
        multiply(1, UPPER, 1)
        empty(1, UPPER)
        pick_left(1)
        first_product(2, LOWER)
        first_product(2, UPPER)
        pick_left(2)
        squashed = {}
        for j in range(3, ROW_TILES):
            first_product(j, LOWER)
            first_product(j, UPPER)
            pick_left(j)
            if j == 5:
                squashed[0] = kept("squashed0", [P, COUPLES], F32, "w4_codes10")[:]
                squash(0)
        w2_rounded = [kept("w2_rounded%d" % b, [P, N, 4], BF16) for b in range(2)]
        for b in range(2):
            round_w2(w2_rows[b][:], w2_rounded[b][:])
            for j in range(OUT_TILES):
                w2_woven[b, j] = w2_rounded[b][:, P * j : P * (j + 1), :]

        z_rows0 = kept("z_rows0", [P, 4, COUPLES], F32)
        rows_ab = kept("z_rows10", [P, 4, 3 * P], F32)
        squashed_rest = kept("squashed", [P, ROW_TILES - 1, COUPLES], F32, "w4_codes11")
        for j in range(1, ROW_TILES):
            squashed[j] = squashed_rest[:, j - 1, :]
        for j in range(ROW_TILES):
            if j + 1 < ROW_TILES:
                squash(j + 1)
            gate(j)
            if j < 4:
                pick_right(j, z_rows0[:, j, :], whole)
            else:
                for part in PIECES[0:2] if j == ROW_TILES - 1 else [slice(0, 3 * P)]:
                    pick_right(j, rows_ab[:, j - 4, part], part)
        woven0 = [
            weave_z(kept("z_woven0%d" % i, [P, 2 * P, 4], BF16)[:], z_rows0[:, :, 2 * P * i : 2 * P * (i + 1)])
            for i in range(2)
        ]
        woven_a = weave_z(kept("z_woven_a", [P, 2 * P, 4], BF16)[:], rows_ab[:, :, PIECES[0]])
        woven_b = weave_z(kept("z_woven_b", [P, P, 4], BF16)[:], rows_ab[:, :, PIECES[1]])
        rows_c = kept("z_rows12", [P, 4, P], F32, "w4_codes11")
        for t in range(4):
            pick_right(4 + t, rows_c[:, t, :], PIECES[2])
        woven_c = weave_z(kept("z_woven_c", [P, P, 4], BF16)[:], rows_c[:])
        quantise_w2(0, 0, kept("w2_codes00", [P, P], U32, "h4")[:])
        z0 = [quantise("z0_low", woven0[0], kept("z0_low_codes", [P, 2 * P], U32, "h5")[:])]
        quantise_w2(1, 0, kept("w2_codes10", [P, P], U32, "h6")[:])
        z1 = [quantise_z("z_a", woven_a)]
        z0.append(quantise("z0_high", woven0[1], kept("z0_high_codes", [P, 2 * P], U32, "h7")[:]))
        z1 += [quantise_z("z_b", woven_b), quantise_z("z_c", woven_c)]
        late_pieces = [(b, j) for j in range(1, OUT_TILES) for b in range(2)]
        late_codes = kept("w2_late_codes", [P, len(late_pieces), P], U32, "w4_codes11")
        for i, (b, j) in enumerate(late_pieces):
            quantise_w2(b, j, late_codes[:, i, :])

        y = [kept("y%d" % j, [P, COUPLES], F32) for j in range(OUT_TILES)]

        def second_product(j, pieces, acc):
            span = slice(PIECES[pieces[0]].start, PIECES[pieces[-1]].stop)
            passes = []
            for i, (codes, plane) in enumerate(z0):
                part = slice(max(span.start, 2 * P * i), min(span.stop, 2 * P * (i + 1)))
                if part.start < part.stop:
                    within = slice(part.start - 2 * P * i, part.stop - 2 * P * i)
                    passes.append((0, part, codes[:, within], plane[:, within]))
            passes += [(1, PIECES[i], z1[i][0], z1[i][1]) for i in pieces]
            for i, (b, part, codes, plane) in enumerate(passes):
                nc.tensor.matmul_mx(
                    out=acc[:, part],
                    lhsT=w2_mx[b, j][0].bitcast(FP8X4),
                    lhsT_scale=w2_mx[b, j][1],
                    rhs=codes.bitcast(FP8X4),
                    rhs_scale=plane,
                    start=(i == 0),
                    stop=(i == len(passes) - 1),
                )
            return lambda: nc.scalar.copy(y[j][:, span], acc[:, span])

        for piece in range(len(PIECES)):
            second_product(0, (piece,), bank(1 + piece))()
        for j in (1, 2):
            second_product(j, (0, 1, 2), bank(j + 3))()
        empty_last = second_product(OUT_TILES - 1, (0, 1, 2), bank(OUT_TILES + 2))

        result = kept("result", [P, OUT_TILES, UNITS], F32, "w4_codes11")
        one_couple = [kept("one_couple%d" % j, [P, UNITS], F32) for j in range(OUT_TILES)]
        both_first = kept("both_first", [P, UNITS], F32)
        both_rest = kept("both_rest", [P, OUT_TILES - 1, UNITS], F32, "both_first")
        both = [both_first[:]] + [both_rest[:, j, :] for j in range(OUT_TILES - 1)]
        all_units = slice(0, UNITS)

        def pick_first(j, part):
            nc.vector.tensor_copy(one_couple[j][:, part], y[j][:].indirect(entries(pos3_sb, part)))

        def add_second(j, part):
            nc.vector.tensor_tensor(
                both[j][:, part], y[j][:].indirect(entries(pos4_sb, part)), one_couple[j][:, part], ALU.add
            )

        def finish(j, part):
            nc.scalar.activation(result[:, j, part], both[j][:, part], ACT.Silu, bias=bias_sb[:, j : j + 1])
            last = j == OUT_TILES - 1 and part.stop == UNITS
            (nc.scalar if last else nc.sync).dma_start(out[P * j : P * (j + 1), part], result[:, j, part])

        halves = [slice(0, UNITS // 2), slice(UNITS // 2, UNITS)]
        for part in halves:
            pick_first(0, part)
        for part in halves:
            add_second(0, part)
        finish(0, all_units)
        empty_last()
        for j in (1, 2):
            pick_first(j, all_units)
        for j in (1, 2):
            add_second(j, all_units)
            finish(j, all_units)
        for part in halves:
            pick_first(OUT_TILES - 1, part)
        for part in halves:
            add_second(OUT_TILES - 1, part)
            finish(OUT_TILES - 1, part)
